import numpy as np
import ml_dtypes


def mxq(x, axis, fmt="e4m3"):
    dtype, down = {"e4m3": (ml_dtypes.float8_e4m3fn, 7), "e5m2": (ml_dtypes.float8_e5m2, 14)}[fmt]
    v = np.moveaxis(np.asarray(x, np.float32).astype(ml_dtypes.bfloat16).astype(np.float64), axis, -1)
    blocks = v.reshape(v.shape[:-1] + (-1, 32))
    amax = np.abs(blocks).max(-1, keepdims=True)
    byte = np.maximum(np.where(amax > 0, np.frexp(amax)[1] - 1 + 127, 0) - down, 1)
    scale = np.exp2(byte - 127.0)
    codes = (blocks / scale).astype(np.float32).astype(dtype).astype(np.float64)
    return np.moveaxis((codes * scale).reshape(v.shape), -1, axis)


WIDE = False


def mx_kscale(k):
    if not WIDE:
        return np.ones(k)
    levels = np.array([10, -10, 5, -5, 0])
    if k % 512:
        return np.exp2(np.random.permutation(np.resize(levels, k // 32))).repeat(32)
    a = np.empty((k // 512, 16))
    for p in range(k // 512):
        a[p, :8] = np.random.permutation(np.resize(levels, 8))
        for g in range(8):
            far = levels[np.abs(levels - a[p, g]) >= 10]
            a[p, g + 8] = far[np.random.randint(len(far))]
    return np.exp2(a.ravel()).repeat(32)


def f64(x):
    return np.asarray(x).astype(np.float64)


def striped(idx):
    return np.tile(idx.reshape(-1, 16).T, (8, 1)).astype(np.uint16)


def unstriped(offs):
    return offs[:16].T.reshape(-1).astype(np.int64)


E2M1 = np.array([0.0, 0.5, 1.0, 1.5, 2.0, 3.0, 4.0, 6.0, -0.0, -0.5, -1.0, -1.5, -2.0, -3.0, -4.0, -6.0])


def pack_fp4(w):
    k, n = w.shape
    w = f64(np.asarray(w, np.float32).astype(ml_dtypes.bfloat16)).reshape(k // 32, 32, n)
    amax = np.abs(w).max(1)
    mant, ex = np.frexp(amax / 6.0)
    byte = np.clip(np.where(amax > 0, np.where(mant > 0.5, ex, ex - 1) + 127, 1), 1, 254)
    scaled = (w * np.exp2(127.0 - byte)[:, None, :]).reshape(k, n).astype(np.float32)
    c = np.ascontiguousarray(scaled.reshape(k // 512, 128, 4, n).transpose(0, 1, 3, 2)).astype(ml_dtypes.float4_e2m1fn).view(np.uint8) & 0xF
    words = (c[..., 0::2] | (c[..., 1::2] << 4)).reshape(k // 512, 128, 2 * n)
    return np.ascontiguousarray(words), np.ascontiguousarray(byte.astype(np.uint8).reshape(k // 512, 16, n))


def unpack_fp4(words, scales):
    g, _, n = scales.shape
    words = np.ascontiguousarray(words).reshape(g, 128, n, 2)
    nib = np.empty((g, 128, n, 4), np.uint8)
    nib[..., 0::2] = words & 0xF
    nib[..., 1::2] = words >> 4
    vals = E2M1[nib] * np.repeat(np.exp2(scales.astype(np.float64) - 127.0), 8, axis=1)[..., None]
    return vals.transpose(0, 1, 3, 2).reshape(g * 512, n)


def relu(v):
    return np.maximum(v, 0.0)


K, T, S, V, H, N = 512, 4096, 1024, 512, 512, 128


def setup_inputs():
    n = np.random.standard_normal
    s = mx_kscale(K)[:, None]
    u = mx_kscale(H)
    packed_xT = pack_fp4(n((K, T)) * s)
    return {
        "x_words": packed_xT[0],
        "x_scales": packed_xT[1],
        "w1": (n((K, H)) / np.sqrt(K) / s * u).astype(np.float32),
        "w2": (n((H, N)) / np.sqrt(2 * H) / u[:, None]).astype(np.float32),
        "w3": (n((H, N)) / np.sqrt(2 * H) / u[:, None]).astype(np.float32),
        "offs": striped(np.random.permutation(T)[:S]),
        "cen": striped(np.random.permutation(S)[:V]),
        "pos1": striped(np.random.permutation(S)[:V]),
        "pos2": striped(np.random.permutation(S)[:V]),
        "pos3": striped(np.random.permutation(S)[:V]),
        "pos4": striped(np.random.permutation(S)[:V]),
    }


def reference(x_words, x_scales, w1, w2, w3, offs, cen, pos1, pos2, pos3, pos4):
    xq = unpack_fp4(x_words, x_scales)[:, unstriped(offs)]
    h = relu(mxq(f64(w1), 0, "e4m3").T @ xq)
    g = h[:, unstriped(cen)]
    z = np.maximum(np.maximum(np.maximum(h[:, unstriped(pos1)], h[:, unstriped(pos2)]), h[:, unstriped(pos3)]), h[:, unstriped(pos4)])
    return relu(mxq(f64(w2), 0, "e4m3").T @ mxq(g, 0, "e4m3") + mxq(f64(w3), 0, "e4m3").T @ mxq(z, 0, "e4m3"))

@@ -1,0 +1,163 @@
+from contextlib import ExitStack
+
+import concourse.mybir as mybir
+
+K, T, S, V, H, N = 512, 4096, 1024, 512, 512, 128
+FLOPS = 2 * K * H * S + 2 * 2 * H * N * V
+
+F32 = mybir.dt.float32
+BF16 = mybir.dt.bfloat16
+I32 = mybir.dt.int32
+U32 = mybir.dt.uint32
+U16 = mybir.dt.uint16
+U8 = mybir.dt.uint8
+FP8X4 = mybir.dt.float8_e4m3fn_x4
+FP4X4 = mybir.dt.float4_e2m1fn_x4
+RELU = mybir.ActivationFunctionType.Relu
+MAX = mybir.AluOpType.max
+
+P = 128
+PACK = 4
+BANK = 512
+LAST = 128
+FIRST = V - LAST
+
+
+def tile_picked_sagecat_maxrelu_p_kernel(tc, x_words, x_scales, w1, w2, w3, offs, cen, pos1, pos2, pos3, pos4, out):
+    nc = tc.nc
+    with ExitStack() as ctx:
+        lists = ctx.enter_context(tc.tile_pool(name="lists", bufs=1))
+        keep = ctx.enter_context(tc.tile_pool(name="keep", bufs=1))
+        early = ctx.enter_context(tc.tile_pool(name="early", bufs=1))
+        psum = ctx.enter_context(tc.psum_pool(name="psum", bufs=1))
+
+        offs_t = lists.tile([P, S // 16], U16, name="offs_t")
+        nc.sync.dma_start(offs_t[:], offs)
+
+        w1_raw = keep.tile([P, PACK, H], F32, name="w1_raw")
+        nc.sync.dma_start(w1_raw[:], w1.rearrange("(p j) c -> p j c", j=PACK))
+
+        x_tab = early.tile([P, T], U16, name="x_tab", align_bytes=64, offset=T)
+        nc.sync.dma_start(x_tab[:].bitcast(I32), x_words[0].bitcast(I32))
+
+        s_tab = early.tile([P, T], U8, name="s_tab", align_bytes=64, offset=0)
+        nc.vector.memset(s_tab[:].bitcast(I32), 0)
+        for q in range(4):
+            nc.scalar.dma_start(s_tab[32 * q : 32 * q + 4, :].bitcast(I32), x_scales[0, 4 * q : 4 * q + 4, :].bitcast(I32))
+
+        w23_raw = keep.tile([P, 2, PACK, N], F32, name="w23_raw")
+        for i, w in enumerate((w2, w3)):
+            nc.sync.dma_start(w23_raw[:, i, :, :], w.rearrange("(p j) c -> p j c", j=PACK))
+
+        pos_t = []
+        for d, pos in enumerate((pos1, pos2, pos3, pos4)):
+            lt = lists.tile([P, V // 16], U16, name="pos_t%d" % d)
+            nc.sync.dma_start(lt[:], pos)
+            pos_t.append(lt)
+        cen_t = lists.tile([P, V // 16], U16, name="cen_t")
+        nc.sync.dma_start(cen_t[:], cen)
+
+        x_scale = keep.tile([P, S], U8, name="x_scale", align_bytes=64)
+        nc.vector.tensor_copy(x_scale[:], s_tab[:].indirect(offs_t[:]))
+        x_code = early.tile([P, S], U16, name="x_code", align_bytes=64, offset=0)
+
+        w1_bf = keep.tile([P, PACK, P, PACK], BF16, name="w1_bf", align_bytes=64)
+        w1_code = early.tile([P, H], U32, name="w1_code", align_bytes=64, offset=2 * S)
+        w1_scale = keep.tile([P, H], U8, name="w1_scale", align_bytes=64)
+        for u in range(2):
+            nc.scalar.copy(
+                out=w1_bf[:, 2 * u : 2 * u + 2, :, :].rearrange("p t m j -> p m t j"),
+                in_=w1_raw[:].rearrange("p j (m t) -> p m t j", t=PACK)[:, :, 2 * u : 2 * u + 2, :],
+            )
+            cols = slice(2 * u * P, (2 * u + 2) * P)
+            nc.vector.quantize_mx(
+                out=w1_code[:, cols].bitcast(FP8X4), scales=w1_scale[:, cols],
+                in_=w1_bf[:, 2 * u : 2 * u + 2, :, :].rearrange("p t m j -> p (t m j)"),
+            )
+            nc.vector.tensor_copy(x_code[:, u * BANK : (u + 1) * BANK], x_tab[:].indirect(offs_t[:, u * BANK // 16 : (u + 1) * BANK // 16]))
+
+        w23_bf = keep.tile([P, 2, N, PACK], BF16, name="w23_bf", align_bytes=64)
+        nc.scalar.copy(out=w23_bf[:], in_=w23_raw[:].rearrange("p i j c -> p i c j"))
+        w23_code = early.tile([P, 2 * N], U32, name="w23_code", align_bytes=64, offset=T)
+        w23_scale = keep.tile([P, 2 * N], U8, name="w23_scale", align_bytes=64)
+        nc.vector.quantize_mx(out=w23_code[:].bitcast(FP8X4), scales=w23_scale[:], in_=w23_bf[:].rearrange("p i c j -> p (i c j)"))
+
+        h = []
+        bank = 0
+        for t in range(PACK):
+            ht = keep.tile([P, S], F32, name="h%d" % t, align_bytes=64)
+            pieces = ((0, 512), (512, 768), (768, S)) if t == 0 else ((0, 512), (512, S))
+            for a, b in pieces:
+                acc = psum.tile([P, b - a], F32, name="h_acc%d_%d" % (t, a), tag="bank%d" % (bank % 8))
+                bank = bank + 1
+                nc.tensor.matmul_mx(
+                    out=acc[:], lhsT=w1_code[:, t * P : (t + 1) * P].bitcast(FP8X4), lhsT_scale=w1_scale[:, t * P : (t + 1) * P],
+                    rhs=x_code[:, a:b].bitcast(FP4X4), rhs_scale=x_scale[:, a:b], start=True, stop=True,
+                )
+                if t == 0 and b == S:
+                    nc.vector.tensor_scalar_max(ht[:, a:b], acc[:], 0.0)
+                else:
+                    nc.scalar.activation(ht[:, a:b], acc[:], RELU)
+            h.append(ht)
+
+        z_planes = keep.tile([P, PACK, V], BF16, name="z_planes", align_bytes=64)
+        for t in range(PACK - 1):
+            nb = keep.tile([P, 4, V], BF16, name="nb%d" % t, align_bytes=64)
+            for d in range(4):
+                nc.vector.tensor_copy(nb[:, d, :], h[t][:].indirect(pos_t[d][:]))
+            pair = keep.tile([P, 2, V], BF16, name="pair%d" % t, align_bytes=64)
+            nc.vector.tensor_tensor(pair[:], nb[:, 0:2, :], nb[:, 2:4, :], MAX)
+            nc.vector.tensor_tensor(z_planes[:, t, :], pair[:, 0, :], pair[:, 1, :], MAX)
+
+        t = PACK - 1
+        nb = keep.tile([P, 4, V], BF16, name="nb3", align_bytes=64)
+        pair = keep.tile([P, 2, V], BF16, name="pair3", align_bytes=64)
+        first_cen = cen_t[:, 0 : FIRST // 16]
+        last_cen = cen_t[:, FIRST // 16 : V // 16]
+        for d in range(3):
+            nc.vector.tensor_copy(nb[:, d, :], h[t][:].indirect(pos_t[d][:]))
+        nc.vector.tensor_tensor(pair[:, 0, :], nb[:, 0, :], nb[:, 1, :], MAX)
+        nc.vector.tensor_copy(nb[:, 3, :], h[t][:].indirect(pos_t[3][:]))
+        nc.vector.tensor_tensor(pair[:, 1, :], pair[:, 0, :], nb[:, 2, :], MAX)
+        nc.vector.tensor_copy(nb[:, 0, 0:FIRST], h[0][:].indirect(first_cen))
+        nc.vector.tensor_tensor(z_planes[:, t, :], pair[:, 1, :], nb[:, 3, :], MAX)
+        for u in range(1, PACK):
+            nc.vector.tensor_copy(nb[:, u, 0:FIRST], h[u][:].indirect(first_cen))
+
+        z_bf = keep.tile([P, V, PACK], BF16, name="z_bf", align_bytes=64)
+        nc.scalar.copy(out=z_bf[:], in_=z_planes[:].rearrange("p t v -> p v t"))
+        z_code = keep.tile([P, V], U32, name="z_code", align_bytes=64)
+        z_scale = keep.tile([P, V], U8, name="z_scale", align_bytes=64)
+        nc.vector.quantize_mx(out=z_code[:].bitcast(FP8X4), scales=z_scale[:], in_=z_bf[:].rearrange("p v t -> p (v t)"))
+
+        groups = ((0, 256), (256, FIRST), (FIRST, V))
+        g_bf = []
+        for a, b in groups[:2]:
+            gt = keep.tile([P, b - a, PACK], BF16, name="g_bf%d" % a, tag="g_bf%d" % a, align_bytes=64)
+            nc.scalar.copy(out=gt[:], in_=nb[:, :, a:b].rearrange("p t v -> p v t"))
+            g_bf.append(gt[:].rearrange("p v t -> p (v t)"))
+        g_last = z_bf[:, 0:LAST, :].rearrange("p v t -> p (v t)")
+        for t in range(PACK):
+            nc.vector.tensor_copy(g_last[:, t : LAST * PACK : PACK], h[t][:].indirect(last_cen))
+        g_bf.append(g_last)
+
+
+        for i, (a, b) in enumerate(groups):
+            gc = keep.tile([P, b - a], U32, name="g_code%d" % a, tag="g_bf0" if b == V else "g_code%d" % a, align_bytes=64)
+            gs = keep.tile([P, b - a], U8, name="g_scale%d" % a, align_bytes=64)
+            nc.vector.quantize_mx(out=gc[:].bitcast(FP8X4), scales=gs[:], in_=g_bf[i])
+            acc = psum.tile([P, b - a], F32, name="o_acc%d" % i, tag="bank%d" % (i + 1))
+            nc.tensor.matmul_mx(
+                out=acc[:], lhsT=w23_code[:, N : 2 * N].bitcast(FP8X4), lhsT_scale=w23_scale[:, N : 2 * N],
+                rhs=z_code[:, a:b].bitcast(FP8X4), rhs_scale=z_scale[:, a:b], start=True, stop=False,
+            )
+            nc.tensor.matmul_mx(
+                out=acc[:], lhsT=w23_code[:, 0:N].bitcast(FP8X4), lhsT_scale=w23_scale[:, 0:N],
+                rhs=gc[:].bitcast(FP8X4), rhs_scale=gs[:], start=False, stop=True,
+            )
+            res = keep.tile([P, b - a], F32, name="res%d" % i)
+            if b == V:
+                nc.vector.tensor_scalar_max(res[:], acc[:], 0.0)
+            else:
+                nc.scalar.activation(res[:], acc[:], RELU)
+            nc.sync.dma_start(out[:, a:b], res[:])

@@ -28,30 +28,34 @@ def tile_picked_sagecat_maxrelu_p_kernel(tc, x_words, x_scales, w1, w2, w3, offs
     with ExitStack() as ctx:
         lists = ctx.enter_context(tc.tile_pool(name="lists", bufs=1))
         keep = ctx.enter_context(tc.tile_pool(name="keep", bufs=1))
-        early = ctx.enter_context(tc.tile_pool(name="early", bufs=1))
         psum = ctx.enter_context(tc.psum_pool(name="psum", bufs=1))
 
         offs_t = lists.tile([P, S // 16], U16, name="offs_t")
         nc.sync.dma_start(offs_t[:], offs)
 
-        w1_raw = keep.tile([P, PACK, H], F32, name="w1_raw")
-        nc.sync.dma_start(w1_raw[:], w1.rearrange("(p j) c -> p j c", j=PACK))
+        pos_t = []
+        for d, pos in enumerate((pos1, pos2)):
+            lt = lists.tile([P, V // 16], U16, name="pos_t%d" % d)
+            nc.sync.dma_start(lt[:], pos)
+            pos_t.append(lt)
 
-        x_tab = early.tile([P, T], U16, name="x_tab", align_bytes=64, offset=T)
-        nc.sync.dma_start(x_tab[:].bitcast(I32), x_words[0].bitcast(I32))
-
-        s_tab = early.tile([P, T], U8, name="s_tab", align_bytes=64, offset=0)
+        s_tab = keep.tile([P, T], U8, name="s_tab", align_bytes=64)
         nc.vector.memset(s_tab[:].bitcast(I32), 0)
         for q in range(4):
-            nc.scalar.dma_start(s_tab[32 * q : 32 * q + 4, :].bitcast(I32), x_scales[0, 4 * q : 4 * q + 4, :].bitcast(I32))
+            nc.sync.dma_start(s_tab[32 * q : 32 * q + 4, :].bitcast(I32), x_scales[0, 4 * q : 4 * q + 4, :].bitcast(I32))
 
-        w23_raw = keep.tile([P, 2, PACK, N], F32, name="w23_raw")
-        for i, w in enumerate((w2, w3)):
-            nc.sync.dma_start(w23_raw[:, i, :, :], w.rearrange("(p j) c -> p j c", j=PACK))
+        x_tab = keep.tile([P, T], U16, name="x_tab", align_bytes=64)
+        nc.sync.dma_start(x_tab[:].bitcast(I32), x_words[0].bitcast(I32))
 
-        pos_t = []
-        for d, pos in enumerate((pos1, pos2, pos3, pos4)):
-            lt = lists.tile([P, V // 16], U16, name="pos_t%d" % d)
+        w1_rows = w1.rearrange("(p j) c -> p j c", j=PACK)
+        w1_raw = []
+        for half in range(2):
+            raw = keep.tile([P, PACK, H // 2], F32, name="w1_raw%d" % half, tag="raw%d" % half)
+            nc.sync.dma_start(raw[:], w1_rows[:, :, half * (H // 2) : (half + 1) * (H // 2)])
+            w1_raw.append(raw)
+
+        for d, pos in enumerate((pos3, pos4)):
+            lt = lists.tile([P, V // 16], U16, name="pos_t%d" % (d + 2))
             nc.sync.dma_start(lt[:], pos)
             pos_t.append(lt)
         cen_t = lists.tile([P, V // 16], U16, name="cen_t")
@@ -59,28 +63,22 @@ def tile_picked_sagecat_maxrelu_p_kernel(tc, x_words, x_scales, w1, w2, w3, offs
 
         x_scale = keep.tile([P, S], U8, name="x_scale", align_bytes=64)
         nc.vector.tensor_copy(x_scale[:], s_tab[:].indirect(offs_t[:]))
-        x_code = early.tile([P, S], U16, name="x_code", align_bytes=64, offset=0)
+        x_code = keep.tile([P, S], U16, name="x_code", align_bytes=64)
+        nc.vector.tensor_copy(x_code[:], x_tab[:].indirect(offs_t[:]))
 
         w1_bf = keep.tile([P, PACK, P, PACK], BF16, name="w1_bf", align_bytes=64)
-        w1_code = early.tile([P, H], U32, name="w1_code", align_bytes=64, offset=2 * S)
+        w1_code = keep.tile([P, H], U32, name="w1_code", align_bytes=64)
         w1_scale = keep.tile([P, H], U8, name="w1_scale", align_bytes=64)
-        for u in range(2):
-            nc.scalar.copy(
-                out=w1_bf[:, 2 * u : 2 * u + 2, :, :].rearrange("p t m j -> p m t j"),
-                in_=w1_raw[:].rearrange("p j (m t) -> p m t j", t=PACK)[:, :, 2 * u : 2 * u + 2, :],
-            )
-            cols = slice(2 * u * P, (2 * u + 2) * P)
+        by_plane = [raw[:].rearrange("p j (m t) -> p m t j", t=PACK) for raw in w1_raw]
+        dst = w1_bf[:].rearrange("p t m j -> p m t j")
+        nc.scalar.copy(out=dst[:, 0 : P // 2, :, :], in_=by_plane[0])
+        for t0, t1 in ((0, 1), (1, 2), (2, PACK)):
+            nc.scalar.copy(out=dst[:, P // 2 : P, t0:t1, :], in_=by_plane[1][:, :, t0:t1, :])
+            cols = slice(t0 * P, t1 * P)
             nc.vector.quantize_mx(
                 out=w1_code[:, cols].bitcast(FP8X4), scales=w1_scale[:, cols],
-                in_=w1_bf[:, 2 * u : 2 * u + 2, :, :].rearrange("p t m j -> p (t m j)"),
+                in_=w1_bf[:, t0:t1, :, :].rearrange("p t m j -> p (t m j)"),
             )
-            nc.vector.tensor_copy(x_code[:, u * BANK : (u + 1) * BANK], x_tab[:].indirect(offs_t[:, u * BANK // 16 : (u + 1) * BANK // 16]))
-
-        w23_bf = keep.tile([P, 2, N, PACK], BF16, name="w23_bf", align_bytes=64)
-        nc.scalar.copy(out=w23_bf[:], in_=w23_raw[:].rearrange("p i j c -> p i c j"))
-        w23_code = early.tile([P, 2 * N], U32, name="w23_code", align_bytes=64, offset=T)
-        w23_scale = keep.tile([P, 2 * N], U8, name="w23_scale", align_bytes=64)
-        nc.vector.quantize_mx(out=w23_code[:].bitcast(FP8X4), scales=w23_scale[:], in_=w23_bf[:].rearrange("p i c j -> p (i c j)"))
 
         h = []
         bank = 0
@@ -100,29 +98,36 @@ def tile_picked_sagecat_maxrelu_p_kernel(tc, x_words, x_scales, w1, w2, w3, offs
                     nc.scalar.activation(ht[:, a:b], acc[:], RELU)
             h.append(ht)
 
-        z_planes = keep.tile([P, PACK, V], BF16, name="z_planes", align_bytes=64)
-        for t in range(PACK - 1):
-            nb = keep.tile([P, 4, V], BF16, name="nb%d" % t, align_bytes=64)
-            for d in range(4):
-                nc.vector.tensor_copy(nb[:, d, :], h[t][:].indirect(pos_t[d][:]))
-            pair = keep.tile([P, 2, V], BF16, name="pair%d" % t, align_bytes=64)
-            nc.vector.tensor_tensor(pair[:], nb[:, 0:2, :], nb[:, 2:4, :], MAX)
-            nc.vector.tensor_tensor(z_planes[:, t, :], pair[:, 0, :], pair[:, 1, :], MAX)
+        w23_raw = keep.tile([P, 2, PACK, N], F32, name="w23_raw", tag="raw1")
+        for i, w in enumerate((w2, w3)):
+            nc.sync.dma_start(w23_raw[:, i, :, :], w.rearrange("(p j) c -> p j c", j=PACK))
+        w23_bf = keep.tile([P, 2, N, PACK], BF16, name="w23_bf", align_bytes=64)
+        nc.scalar.copy(out=w23_bf[:], in_=w23_raw[:].rearrange("p i j c -> p i c j"))
+        w23_code = keep.tile([P, 2 * N], U32, name="w23_code", align_bytes=64)
+        w23_scale = keep.tile([P, 2 * N], U8, name="w23_scale", align_bytes=64)
 
-        t = PACK - 1
-        nb = keep.tile([P, 4, V], BF16, name="nb3", align_bytes=64)
-        pair = keep.tile([P, 2, V], BF16, name="pair3", align_bytes=64)
+        nc.vector.quantize_mx(out=w23_code[:].bitcast(FP8X4), scales=w23_scale[:], in_=w23_bf[:].rearrange("p i c j -> p (i c j)"))
+
+        nb = keep.tile([P, 4, PACK, V], BF16, name="nb", align_bytes=64)
+        top2 = keep.tile([P, PACK, V], BF16, name="top2", align_bytes=64)
+        top3 = keep.tile([P, PACK, V], BF16, name="top3", align_bytes=64)
+        z_planes = keep.tile([P, PACK, V], BF16, name="z_planes", align_bytes=64)
+        g_planes = nb[:, 0, :, :]
         first_cen = cen_t[:, 0 : FIRST // 16]
         last_cen = cen_t[:, FIRST // 16 : V // 16]
-        for d in range(3):
-            nc.vector.tensor_copy(nb[:, d, :], h[t][:].indirect(pos_t[d][:]))
-        nc.vector.tensor_tensor(pair[:, 0, :], nb[:, 0, :], nb[:, 1, :], MAX)
-        nc.vector.tensor_copy(nb[:, 3, :], h[t][:].indirect(pos_t[3][:]))
-        nc.vector.tensor_tensor(pair[:, 1, :], pair[:, 0, :], nb[:, 2, :], MAX)
-        nc.vector.tensor_copy(nb[:, 0, 0:FIRST], h[0][:].indirect(first_cen))
-        nc.vector.tensor_tensor(z_planes[:, t, :], pair[:, 1, :], nb[:, 3, :], MAX)
-        for u in range(1, PACK):
-            nc.vector.tensor_copy(nb[:, u, 0:FIRST], h[u][:].indirect(first_cen))
+        for t in range(PACK):
+            for d in range(3):
+                nc.vector.tensor_copy(nb[:, d, t, :], h[t][:].indirect(pos_t[d][:]))
+            if t == PACK - 1:
+                nc.vector.tensor_tensor(top2[:], nb[:, 0, :, :], nb[:, 1, :, :], MAX)
+            nc.vector.tensor_copy(nb[:, 3, t, :], h[t][:].indirect(pos_t[3][:]))
+        nc.vector.tensor_tensor(top3[:], top2[:], nb[:, 2, :, :], MAX)
+        nc.vector.tensor_copy(g_planes[:, 0, 0:FIRST], h[0][:].indirect(first_cen))
+        nc.vector.tensor_tensor(z_planes[:], top3[:], nb[:, 3, :, :], MAX)
+        for t in range(1, PACK):
+            nc.vector.tensor_copy(g_planes[:, t, 0:FIRST], h[t][:].indirect(first_cen))
+        for t in range(PACK):
+            nc.vector.tensor_copy(g_planes[:, t, FIRST:V], h[t][:].indirect(last_cen))
 
         z_bf = keep.tile([P, V, PACK], BF16, name="z_bf", align_bytes=64)
         nc.scalar.copy(out=z_bf[:], in_=z_planes[:].rearrange("p t v -> p v t"))
@@ -131,21 +136,12 @@ def tile_picked_sagecat_maxrelu_p_kernel(tc, x_words, x_scales, w1, w2, w3, offs
         nc.vector.quantize_mx(out=z_code[:].bitcast(FP8X4), scales=z_scale[:], in_=z_bf[:].rearrange("p v t -> p (v t)"))
 
         groups = ((0, 256), (256, FIRST), (FIRST, V))
-        g_bf = []
-        for a, b in groups[:2]:
-            gt = keep.tile([P, b - a, PACK], BF16, name="g_bf%d" % a, tag="g_bf%d" % a, align_bytes=64)
-            nc.scalar.copy(out=gt[:], in_=nb[:, :, a:b].rearrange("p t v -> p v t"))
-            g_bf.append(gt[:].rearrange("p v t -> p (v t)"))
-        g_last = z_bf[:, 0:LAST, :].rearrange("p v t -> p (v t)")
-        for t in range(PACK):
-            nc.vector.tensor_copy(g_last[:, t : LAST * PACK : PACK], h[t][:].indirect(last_cen))
-        g_bf.append(g_last)
-
-
         for i, (a, b) in enumerate(groups):
-            gc = keep.tile([P, b - a], U32, name="g_code%d" % a, tag="g_bf0" if b == V else "g_code%d" % a, align_bytes=64)
+            gt = keep.tile([P, b - a, PACK], BF16, name="g_bf%d" % a, align_bytes=64)
+            nc.scalar.copy(out=gt[:], in_=g_planes[:, :, a:b].rearrange("p t v -> p v t"))
+            gc = keep.tile([P, b - a], U32, name="g_code%d" % a, align_bytes=64)
             gs = keep.tile([P, b - a], U8, name="g_scale%d" % a, align_bytes=64)
-            nc.vector.quantize_mx(out=gc[:].bitcast(FP8X4), scales=gs[:], in_=g_bf[i])
+            nc.vector.quantize_mx(out=gc[:].bitcast(FP8X4), scales=gs[:], in_=gt[:].rearrange("p v t -> p (v t)"))
             acc = psum.tile([P, b - a], F32, name="o_acc%d" % i, tag="bank%d" % (i + 1))
             nc.tensor.matmul_mx(
                 out=acc[:], lhsT=w23_code[:, N : 2 * N].bitcast(FP8X4), lhsT_scale=w23_scale[:, N : 2 * N],

@@ -108,22 +108,21 @@ def tile_picked_sagecat_maxrelu_p_kernel(tc, x_words, x_scales, w1, w2, w3, offs
 
         nc.vector.quantize_mx(out=w23_code[:].bitcast(FP8X4), scales=w23_scale[:], in_=w23_bf[:].rearrange("p i c j -> p (i c j)"))
 
-        nb = keep.tile([P, 4, PACK, V], BF16, name="nb", align_bytes=64)
-        top2 = keep.tile([P, PACK, V], BF16, name="top2", align_bytes=64)
-        top3 = keep.tile([P, PACK, V], BF16, name="top3", align_bytes=64)
+        picked = keep.tile([P, PACK, 4, V], F32, name="picked")
+        nb = [keep.tile([P, 2, PACK, V], BF16, name="nb%d" % u, tag="nb%d" % u, align_bytes=64) for u in range(2)]
+        top = keep.tile([P, 2, PACK, V], BF16, name="top", align_bytes=64)
         z_planes = keep.tile([P, PACK, V], BF16, name="z_planes", align_bytes=64)
-        g_planes = nb[:, 0, :, :]
         first_cen = cen_t[:, 0 : FIRST // 16]
         last_cen = cen_t[:, FIRST // 16 : V // 16]
         for t in range(PACK):
-            for d in range(3):
-                nc.vector.tensor_copy(nb[:, d, t, :], h[t][:].indirect(pos_t[d][:]))
-            if t == PACK - 1:
-                nc.vector.tensor_tensor(top2[:], nb[:, 0, :, :], nb[:, 1, :, :], MAX)
-            nc.vector.tensor_copy(nb[:, 3, t, :], h[t][:].indirect(pos_t[3][:]))
-        nc.vector.tensor_tensor(top3[:], top2[:], nb[:, 2, :, :], MAX)
+            for d in range(4):
+                nc.vector.tensor_copy(picked[:, t, d, :], h[t][:].indirect(pos_t[d][:]))
+                nc.scalar.copy(out=nb[d // 2][:, d % 2, t, :], in_=picked[:, t, d, :])
+        for u in range(2):
+            nc.vector.tensor_tensor(top[:, u, :, :], nb[u][:, 0, :, :], nb[u][:, 1, :, :], MAX)
+        g_planes = keep.tile([P, PACK, V], F32, name="g_planes", tag="nb0", align_bytes=64)
         nc.vector.tensor_copy(g_planes[:, 0, 0:FIRST], h[0][:].indirect(first_cen))
-        nc.vector.tensor_tensor(z_planes[:], top3[:], nb[:, 3, :, :], MAX)
+        nc.vector.tensor_tensor(z_planes[:], top[:, 0, :, :], top[:, 1, :, :], MAX)
         for t in range(1, PACK):
             nc.vector.tensor_copy(g_planes[:, t, 0:FIRST], h[t][:].indirect(first_cen))
         for t in range(PACK):

@@ -30,22 +30,21 @@ def tile_picked_sagecat_maxrelu_p_kernel(tc, x_words, x_scales, w1, w2, w3, offs
         keep = ctx.enter_context(tc.tile_pool(name="keep", bufs=1))
         psum = ctx.enter_context(tc.psum_pool(name="psum", bufs=1))
 
+        s_tab = keep.tile([P, T], U8, name="s_tab", align_bytes=64)
+        nc.sync.dma_start(s_tab[P - 16 : P, :].bitcast(I32), x_scales[0].bitcast(I32))
+        nc.vector.memset(s_tab[0 : P - 16, :].bitcast(I32), 0)
+
         offs_t = lists.tile([P, S // 16], U16, name="offs_t")
         nc.sync.dma_start(offs_t[:], offs)
 
+        x_tab = keep.tile([P, T], U16, name="x_tab", align_bytes=64)
+        nc.sync.dma_start(x_tab[:].bitcast(I32), x_words[0].bitcast(I32))
+
         pos_t = []
-        for d, pos in enumerate((pos1, pos2)):
+        for d, pos in enumerate((pos1, pos2, pos3)):
             lt = lists.tile([P, V // 16], U16, name="pos_t%d" % d)
             nc.sync.dma_start(lt[:], pos)
             pos_t.append(lt)
-
-        s_tab = keep.tile([P, T], U8, name="s_tab", align_bytes=64)
-        nc.vector.memset(s_tab[:].bitcast(I32), 0)
-        for q in range(4):
-            nc.sync.dma_start(s_tab[32 * q : 32 * q + 4, :].bitcast(I32), x_scales[0, 4 * q : 4 * q + 4, :].bitcast(I32))
-
-        x_tab = keep.tile([P, T], U16, name="x_tab", align_bytes=64)
-        nc.sync.dma_start(x_tab[:].bitcast(I32), x_words[0].bitcast(I32))
 
         w1_rows = w1.rearrange("(p j) c -> p j c", j=PACK)
         w1_raw = []
@@ -54,15 +53,18 @@ def tile_picked_sagecat_maxrelu_p_kernel(tc, x_words, x_scales, w1, w2, w3, offs
             nc.sync.dma_start(raw[:], w1_rows[:, :, half * (H // 2) : (half + 1) * (H // 2)])
             w1_raw.append(raw)
 
-        for d, pos in enumerate((pos3, pos4)):
-            lt = lists.tile([P, V // 16], U16, name="pos_t%d" % (d + 2))
-            nc.sync.dma_start(lt[:], pos)
-            pos_t.append(lt)
+        lt = lists.tile([P, V // 16], U16, name="pos_t3")
+        nc.sync.dma_start(lt[:], pos4)
+        pos_t.append(lt)
         cen_t = lists.tile([P, V // 16], U16, name="cen_t")
         nc.sync.dma_start(cen_t[:], cen)
 
+        s_picked = keep.tile([P, S], U8, name="s_picked", align_bytes=64)
+        nc.vector.tensor_copy(s_picked[:], s_tab[:].indirect(offs_t[:]))
         x_scale = keep.tile([P, S], U8, name="x_scale", align_bytes=64)
-        nc.vector.tensor_copy(x_scale[:], s_tab[:].indirect(offs_t[:]))
+        nc.vector.memset(x_scale[:].bitcast(I32), 0)
+        for q in range(4):
+            nc.sync.dma_start(x_scale[32 * q : 32 * q + 4, :].bitcast(I32), s_picked[P - 16 + 4 * q : P - 12 + 4 * q, :].bitcast(I32))
         x_code = keep.tile([P, S], U16, name="x_code", align_bytes=64)
         nc.vector.tensor_copy(x_code[:], x_tab[:].indirect(offs_t[:]))
 

@@ -15,6 +15,8 @@ FP8X4 = mybir.dt.float8_e4m3fn_x4
 FP4X4 = mybir.dt.float4_e2m1fn_x4
 RELU = mybir.ActivationFunctionType.Relu
 MAX = mybir.AluOpType.max
+ADD = mybir.AluOpType.add
+SUB = mybir.AluOpType.subtract
 
 P = 128
 PACK = 4
@@ -28,6 +30,7 @@ def tile_picked_sagecat_maxrelu_p_kernel(tc, x_words, x_scales, w1, w2, w3, offs
     with ExitStack() as ctx:
         lists = ctx.enter_context(tc.tile_pool(name="lists", bufs=1))
         keep = ctx.enter_context(tc.tile_pool(name="keep", bufs=1))
+        after = ctx.enter_context(tc.tile_pool(name="after", bufs=1))
         psum = ctx.enter_context(tc.psum_pool(name="psum", bufs=1))
 
         s_tab = keep.tile([P, T], U8, name="s_tab", align_bytes=64)
@@ -105,27 +108,50 @@ def tile_picked_sagecat_maxrelu_p_kernel(tc, x_words, x_scales, w1, w2, w3, offs
             nc.sync.dma_start(w23_raw[:, i, :, :], w.rearrange("(p j) c -> p j c", j=PACK))
         w23_bf = keep.tile([P, 2, N, PACK], BF16, name="w23_bf", align_bytes=64)
         nc.scalar.copy(out=w23_bf[:], in_=w23_raw[:].rearrange("p i j c -> p i c j"))
-        w23_code = keep.tile([P, 2 * N], U32, name="w23_code", align_bytes=64)
-        w23_scale = keep.tile([P, 2 * N], U8, name="w23_scale", align_bytes=64)
 
-        nc.vector.quantize_mx(out=w23_code[:].bitcast(FP8X4), scales=w23_scale[:], in_=w23_bf[:].rearrange("p i c j -> p (i c j)"))
-
-        picked = keep.tile([P, PACK, 4, V], F32, name="picked")
-        nb = [keep.tile([P, 2, PACK, V], BF16, name="nb%d" % u, tag="nb%d" % u, align_bytes=64) for u in range(2)]
-        top = keep.tile([P, 2, PACK, V], BF16, name="top", align_bytes=64)
-        z_planes = keep.tile([P, PACK, V], BF16, name="z_planes", align_bytes=64)
-        first_cen = cen_t[:, 0 : FIRST // 16]
-        last_cen = cen_t[:, FIRST // 16 : V // 16]
+        early = keep.tile([P, 2, 2, 2, V], BF16, name="early", align_bytes=64)
+        late = keep.tile([P, 2, 2, 2, V], BF16, name="late", tag="late", align_bytes=64)
         for t in range(PACK):
             for d in range(4):
-                nc.vector.tensor_copy(picked[:, t, d, :], h[t][:].indirect(pos_t[d][:]))
-                nc.scalar.copy(out=nb[d // 2][:, d % 2, t, :], in_=picked[:, t, d, :])
-        for u in range(2):
-            nc.vector.tensor_tensor(top[:, u, :, :], nb[u][:, 0, :, :], nb[u][:, 1, :, :], MAX)
-        g_planes = keep.tile([P, PACK, V], F32, name="g_planes", tag="nb0", align_bytes=64)
-        nc.vector.tensor_copy(g_planes[:, 0, 0:FIRST], h[0][:].indirect(first_cen))
-        nc.vector.tensor_tensor(z_planes[:], top[:, 0, :, :], top[:, 1, :, :], MAX)
-        for t in range(1, PACK):
+                dst_nb = early[:, t, d // 2, d % 2, :] if t < 2 else late[:, d % 2, d // 2, t - 2, :]
+                nc.vector.tensor_copy(dst_nb, h[t][:].indirect(pos_t[d][:]))
+
+        top = keep.tile([P, 2, 2, V], BF16, name="top", align_bytes=64)
+        gain = {}
+
+        def rise(t, u):
+            diff = keep.tile([P, V], F32, name="diff%d%d" % (t, u))
+            nc.gpsimd.tensor_tensor(diff[:], early[:, t, u, 1, :], early[:, t, u, 0, :], SUB)
+            if (t, u) == (1, 1):
+                gain[t, u] = after.tile([P, V], F32, name="gain_last", offset=0, align_bytes=64)
+            else:
+                gain[t, u] = keep.tile([P, V], F32, name="gain%d%d" % (t, u), align_bytes=64)
+            nc.scalar.activation(gain[t, u][:], diff[:], RELU)
+
+        def settle(t, u):
+            nc.gpsimd.tensor_tensor(top[:, u, t, :], early[:, t, u, 0, :], gain[t, u][:], ADD)
+
+        rise(0, 0)
+        rise(0, 1)
+        settle(0, 0)
+        rise(1, 0)
+        settle(0, 1)
+        rise(1, 1)
+        settle(1, 0)
+        settle(1, 1)
+
+        z_planes = after.tile([P, PACK, V], BF16, name="z_planes", offset=6144, align_bytes=64)
+        nc.vector.tensor_tensor(z_planes[:, 0:2, :], top[:, 0, :, :], top[:, 1, :, :], MAX)
+        top_late = after.tile([P, 2, 2, V], BF16, name="top_late", offset=1024, align_bytes=64)
+        nc.vector.tensor_tensor(top_late[:], late[:, 0, :, :, :], late[:, 1, :, :, :], MAX)
+        w23_code = after.tile([P, 2 * N], U32, name="w23_code", offset=0, align_bytes=64)
+        w23_scale = keep.tile([P, 2 * N], U8, name="w23_scale", align_bytes=64)
+        nc.vector.quantize_mx(out=w23_code[:].bitcast(FP8X4), scales=w23_scale[:], in_=w23_bf[:].rearrange("p i c j -> p (i c j)"))
+        nc.vector.tensor_tensor(z_planes[:, 2:4, :], top_late[:, 0, :, :], top_late[:, 1, :, :], MAX)
+        first_cen = cen_t[:, 0 : FIRST // 16]
+        last_cen = cen_t[:, FIRST // 16 : V // 16]
+        g_planes = keep.tile([P, PACK, V], F32, name="g_planes", tag="late", align_bytes=64)
+        for t in range(PACK):
             nc.vector.tensor_copy(g_planes[:, t, 0:FIRST], h[t][:].indirect(first_cen))
         for t in range(PACK):
             nc.vector.tensor_copy(g_planes[:, t, FIRST:V], h[t][:].indirect(last_cen))
@@ -138,7 +164,7 @@ def tile_picked_sagecat_maxrelu_p_kernel(tc, x_words, x_scales, w1, w2, w3, offs
 
         groups = ((0, 256), (256, FIRST), (FIRST, V))
         for i, (a, b) in enumerate(groups):
-            gt = keep.tile([P, b - a, PACK], BF16, name="g_bf%d" % a, align_bytes=64)
+            gt = after.tile([P, b - a, PACK], BF16, name="g_bf%d" % a, offset=6144 + 8 * a, align_bytes=64)
             nc.scalar.copy(out=gt[:], in_=g_planes[:, :, a:b].rearrange("p t v -> p v t"))
             gc = keep.tile([P, b - a], U32, name="g_code%d" % a, align_bytes=64)
             gs = keep.tile([P, b - a], U8, name="g_scale%d" % a, align_bytes=64)

@@ -49,12 +49,10 @@ def tile_picked_sagecat_maxrelu_p_kernel(tc, x_words, x_scales, w1, w2, w3, offs
             nc.sync.dma_start(lt[:], pos)
             pos_t.append(lt)
 
-        w1_rows = w1.rearrange("(p j) c -> p j c", j=PACK)
-        w1_raw = []
-        for half in range(2):
-            raw = keep.tile([P, PACK, H // 2], F32, name="w1_raw%d" % half, tag="raw%d" % half)
-            nc.sync.dma_start(raw[:], w1_rows[:, :, half * (H // 2) : (half + 1) * (H // 2)])
-            w1_raw.append(raw)
+        w1_rows = w1.rearrange("(p j) c -> p (j c)", j=PACK)
+        w1_raw = keep.tile([P, PACK * H], F32, name="w1_raw", tag="raw1")
+        for j in (0, 2):
+            nc.sync.dma_start(w1_raw[:, j * H : (j + 2) * H], w1_rows[:, j * H : (j + 2) * H])
 
         lt = lists.tile([P, V // 16], U16, name="pos_t3")
         nc.sync.dma_start(lt[:], pos4)
@@ -71,18 +69,21 @@ def tile_picked_sagecat_maxrelu_p_kernel(tc, x_words, x_scales, w1, w2, w3, offs
         x_code = keep.tile([P, S], U16, name="x_code", align_bytes=64)
         nc.vector.tensor_copy(x_code[:], x_tab[:].indirect(offs_t[:]))
 
-        w1_bf = keep.tile([P, PACK, P, PACK], BF16, name="w1_bf", align_bytes=64)
         w1_code = keep.tile([P, H], U32, name="w1_code", align_bytes=64)
         w1_scale = keep.tile([P, H], U8, name="w1_scale", align_bytes=64)
-        by_plane = [raw[:].rearrange("p j (m t) -> p m t j", t=PACK) for raw in w1_raw]
-        dst = w1_bf[:].rearrange("p t m j -> p m t j")
-        nc.scalar.copy(out=dst[:, 0 : P // 2, :, :], in_=by_plane[0])
-        for t0, t1 in ((0, 1), (1, 2), (2, PACK)):
-            nc.scalar.copy(out=dst[:, P // 2 : P, t0:t1, :], in_=by_plane[1][:, :, t0:t1, :])
+        src = w1_raw[:].rearrange("p (j m t) -> p t m j", j=PACK, t=PACK)
+        first_bf = keep.tile([P, P, PACK], BF16, name="first_bf", tag="w1_bf", align_bytes=64)
+        nc.scalar.copy(out=first_bf[:, :, 0:2], in_=src[:, 0, :, 0:2])
+        nc.scalar.copy(out=first_bf[:, 0:64, 2:4], in_=src[:, 0, 0:64, 2:4])
+        nc.vector.tensor_copy(out=first_bf[:, 64:P, 2:4], in_=src[:, 0, 64:P, 2:4])
+        nc.vector.quantize_mx(out=w1_code[:, 0:P].bitcast(FP8X4), scales=w1_scale[:, 0:P], in_=first_bf[:].rearrange("p m j -> p (m j)"))
+        rest_bf = keep.tile([P, 3, P, PACK], BF16, name="rest_bf", tag="w1_bf", align_bytes=64)
+        nc.vector.tensor_copy(out=rest_bf[:].rearrange("p t m j -> p m t j"), in_=src[:, 1:4, :, :].rearrange("p t m j -> p m t j"))
+        for t0, t1 in ((1, 2), (2, PACK)):
             cols = slice(t0 * P, t1 * P)
             nc.vector.quantize_mx(
                 out=w1_code[:, cols].bitcast(FP8X4), scales=w1_scale[:, cols],
-                in_=w1_bf[:, t0:t1, :, :].rearrange("p t m j -> p (t m j)"),
+                in_=rest_bf[:, t0 - 1 : t1 - 1, :, :].rearrange("p t m j -> p (t m j)"),
             )
 
         h = []
@@ -110,48 +111,49 @@ def tile_picked_sagecat_maxrelu_p_kernel(tc, x_words, x_scales, w1, w2, w3, offs
         nc.scalar.copy(out=w23_bf[:], in_=w23_raw[:].rearrange("p i j c -> p i c j"))
 
         early = keep.tile([P, 2, 2, 2, V], BF16, name="early", align_bytes=64)
-        late = keep.tile([P, 2, 2, 2, V], BF16, name="late", tag="late", align_bytes=64)
+        shared = keep.tile([P, 5 * V], F32, name="shared", align_bytes=64)
+        g_planes = shared[:, 0 : PACK * V].rearrange("p (t v) -> p t v", t=PACK)
+        late = shared[:, FIRST : FIRST + PACK * V].bitcast(BF16).rearrange("p (e u t v) -> p e u t v", e=2, u=2, t=2)
         for t in range(PACK):
             for d in range(4):
                 dst_nb = early[:, t, d // 2, d % 2, :] if t < 2 else late[:, d % 2, d // 2, t - 2, :]
                 nc.vector.tensor_copy(dst_nb, h[t][:].indirect(pos_t[d][:]))
 
+        first_cen = cen_t[:, 0 : FIRST // 16]
+        last_cen = cen_t[:, FIRST // 16 : V // 16]
+        nc.vector.tensor_copy(g_planes[:, 0, 0:FIRST], h[0][:].indirect(first_cen))
+
         top = keep.tile([P, 2, 2, V], BF16, name="top", align_bytes=64)
-        gain = {}
-
-        def rise(t, u):
-            diff = keep.tile([P, V], F32, name="diff%d%d" % (t, u))
-            nc.gpsimd.tensor_tensor(diff[:], early[:, t, u, 1, :], early[:, t, u, 0, :], SUB)
-            if (t, u) == (1, 1):
-                gain[t, u] = after.tile([P, V], F32, name="gain_last", offset=0, align_bytes=64)
-            else:
-                gain[t, u] = keep.tile([P, V], F32, name="gain%d%d" % (t, u), align_bytes=64)
-            nc.scalar.activation(gain[t, u][:], diff[:], RELU)
-
-        def settle(t, u):
-            nc.gpsimd.tensor_tensor(top[:, u, t, :], early[:, t, u, 0, :], gain[t, u][:], ADD)
-
-        rise(0, 0)
-        rise(0, 1)
-        settle(0, 0)
-        rise(1, 0)
-        settle(0, 1)
-        rise(1, 1)
-        settle(1, 0)
-        settle(1, 1)
-
+        gain = keep.tile([P, 2, 2, V], F32, name="gain", align_bytes=64)
+        gain_top = after.tile([P, V], F32, name="gain_top", offset=0, align_bytes=64)
         z_planes = after.tile([P, PACK, V], BF16, name="z_planes", offset=6144, align_bytes=64)
-        nc.vector.tensor_tensor(z_planes[:, 0:2, :], top[:, 0, :, :], top[:, 1, :, :], MAX)
+
+        def rise(name, a, b, out_gain):
+            diff = keep.tile([P, V], F32, name=name)
+            nc.gpsimd.tensor_tensor(diff[:], b, a, SUB)
+            nc.scalar.activation(out_gain, diff[:], RELU)
+
+        def rise_pair(t, u):
+            rise("diff%d%d" % (t, u), early[:, t, u, 0, :], early[:, t, u, 1, :], gain[:, t, u, :])
+
+        rise_pair(0, 0)
+        rise_pair(0, 1)
+        nc.gpsimd.tensor_tensor(top[:, 0, 0, :], early[:, 0, 0, 0, :], gain[:, 0, 0, :], ADD)
+        rise_pair(1, 0)
+        nc.gpsimd.tensor_tensor(top[:, 0, 1, :], early[:, 0, 1, 0, :], gain[:, 0, 1, :], ADD)
+        rise_pair(1, 1)
+        rise("diff02", top[:, 0, 0, :], top[:, 0, 1, :], gain_top[:])
+        nc.gpsimd.tensor_tensor(top[:, 1, :, :], early[:, 1, :, 0, :], gain[:, 1, :, :], ADD)
+        nc.gpsimd.tensor_tensor(z_planes[:, 0, :], top[:, 0, 0, :], gain_top[:], ADD)
+
+        nc.vector.tensor_tensor(z_planes[:, 1, :], top[:, 1, 0, :], top[:, 1, 1, :], MAX)
         top_late = after.tile([P, 2, 2, V], BF16, name="top_late", offset=1024, align_bytes=64)
         nc.vector.tensor_tensor(top_late[:], late[:, 0, :, :, :], late[:, 1, :, :, :], MAX)
         w23_code = after.tile([P, 2 * N], U32, name="w23_code", offset=0, align_bytes=64)
         w23_scale = keep.tile([P, 2 * N], U8, name="w23_scale", align_bytes=64)
         nc.vector.quantize_mx(out=w23_code[:].bitcast(FP8X4), scales=w23_scale[:], in_=w23_bf[:].rearrange("p i c j -> p (i c j)"))
         nc.vector.tensor_tensor(z_planes[:, 2:4, :], top_late[:, 0, :, :], top_late[:, 1, :, :], MAX)
-        first_cen = cen_t[:, 0 : FIRST // 16]
-        last_cen = cen_t[:, FIRST // 16 : V // 16]
-        g_planes = keep.tile([P, PACK, V], F32, name="g_planes", tag="late", align_bytes=64)
-        for t in range(PACK):
+        for t in range(1, PACK):
             nc.vector.tensor_copy(g_planes[:, t, 0:FIRST], h[t][:].indirect(first_cen))
         for t in range(PACK):
             nc.vector.tensor_copy(g_planes[:, t, FIRST:V], h[t][:].indirect(last_cen))

@@ -44,7 +44,7 @@ def tile_picked_sagecat_maxrelu_p_kernel(tc, x_words, x_scales, w1, w2, w3, offs
         nc.sync.dma_start(x_tab[:].bitcast(I32), x_words[0].bitcast(I32))
 
         pos_t = []
-        for d, pos in enumerate((pos1, pos2, pos3)):
+        for d, pos in enumerate((pos1, pos2)):
             lt = lists.tile([P, V // 16], U16, name="pos_t%d" % d)
             nc.sync.dma_start(lt[:], pos)
             pos_t.append(lt)
@@ -54,9 +54,10 @@ def tile_picked_sagecat_maxrelu_p_kernel(tc, x_words, x_scales, w1, w2, w3, offs
         for j in (0, 2):
             nc.sync.dma_start(w1_raw[:, j * H : (j + 2) * H], w1_rows[:, j * H : (j + 2) * H])
 
-        lt = lists.tile([P, V // 16], U16, name="pos_t3")
-        nc.sync.dma_start(lt[:], pos4)
-        pos_t.append(lt)
+        for d, pos in enumerate((pos3, pos4)):
+            lt = lists.tile([P, V // 16], U16, name="pos_t%d" % (d + 2))
+            nc.sync.dma_start(lt[:], pos)
+            pos_t.append(lt)
         cen_t = lists.tile([P, V // 16], U16, name="cen_t")
         nc.sync.dma_start(cen_t[:], cen)
 
@@ -77,14 +78,12 @@ def tile_picked_sagecat_maxrelu_p_kernel(tc, x_words, x_scales, w1, w2, w3, offs
         nc.scalar.copy(out=first_bf[:, 0:64, 2:4], in_=src[:, 0, 0:64, 2:4])
         nc.vector.tensor_copy(out=first_bf[:, 64:P, 2:4], in_=src[:, 0, 64:P, 2:4])
         nc.vector.quantize_mx(out=w1_code[:, 0:P].bitcast(FP8X4), scales=w1_scale[:, 0:P], in_=first_bf[:].rearrange("p m j -> p (m j)"))
-        rest_bf = keep.tile([P, 3, P, PACK], BF16, name="rest_bf", tag="w1_bf", align_bytes=64)
-        nc.vector.tensor_copy(out=rest_bf[:].rearrange("p t m j -> p m t j"), in_=src[:, 1:4, :, :].rearrange("p t m j -> p m t j"))
-        for t0, t1 in ((1, 2), (2, PACK)):
-            cols = slice(t0 * P, t1 * P)
-            nc.vector.quantize_mx(
-                out=w1_code[:, cols].bitcast(FP8X4), scales=w1_scale[:, cols],
-                in_=rest_bf[:, t0 - 1 : t1 - 1, :, :].rearrange("p t m j -> p (t m j)"),
-            )
+        second_bf = keep.tile([P, P, PACK], BF16, name="second_bf", align_bytes=64)
+        nc.scalar.copy(out=second_bf[:], in_=src[:, 1, :, :])
+        rest_bf = keep.tile([P, 2, P, PACK], BF16, name="rest_bf", tag="w1_bf", align_bytes=64)
+        nc.vector.tensor_copy(out=rest_bf[:].rearrange("p t m j -> p m t j"), in_=src[:, 2:4, :, :].rearrange("p t m j -> p m t j"))
+        nc.vector.quantize_mx(out=w1_code[:, P : 2 * P].bitcast(FP8X4), scales=w1_scale[:, P : 2 * P], in_=second_bf[:].rearrange("p m j -> p (m j)"))
+        nc.vector.quantize_mx(out=w1_code[:, 2 * P : H].bitcast(FP8X4), scales=w1_scale[:, 2 * P : H], in_=rest_bf[:].rearrange("p t m j -> p (t m j)"))
 
         h = []
         bank = 0
@@ -159,7 +158,7 @@ def tile_picked_sagecat_maxrelu_p_kernel(tc, x_words, x_scales, w1, w2, w3, offs
             nc.vector.tensor_copy(g_planes[:, t, FIRST:V], h[t][:].indirect(last_cen))
 
         z_bf = keep.tile([P, V, PACK], BF16, name="z_bf", align_bytes=64)
-        nc.scalar.copy(out=z_bf[:], in_=z_planes[:].rearrange("p t v -> p v t"))
+        nc.scalar.copy(out=z_bf[:].rearrange("p (c i) t -> p c t i", i=4), in_=z_planes[:].rearrange("p t (c i) -> p c t i", i=4))
         z_code = keep.tile([P, V], U32, name="z_code", align_bytes=64)
         z_scale = keep.tile([P, V], U8, name="z_scale", align_bytes=64)
         nc.vector.quantize_mx(out=z_code[:].bitcast(FP8X4), scales=z_scale[:], in_=z_bf[:].rearrange("p v t -> p (v t)"))
@@ -167,7 +166,7 @@ def tile_picked_sagecat_maxrelu_p_kernel(tc, x_words, x_scales, w1, w2, w3, offs
         groups = ((0, 256), (256, FIRST), (FIRST, V))
         for i, (a, b) in enumerate(groups):
             gt = after.tile([P, b - a, PACK], BF16, name="g_bf%d" % a, offset=6144 + 8 * a, align_bytes=64)
-            nc.scalar.copy(out=gt[:], in_=g_planes[:, :, a:b].rearrange("p t v -> p v t"))
+            nc.scalar.copy(out=gt[:].rearrange("p (c i) t -> p c t i", i=4), in_=g_planes[:, :, a:b].rearrange("p t (c i) -> p c t i", i=4))
             gc = keep.tile([P, b - a], U32, name="g_code%d" % a, align_bytes=64)
             gs = keep.tile([P, b - a], U8, name="g_scale%d" % a, align_bytes=64)
             nc.vector.quantize_mx(out=gc[:].bitcast(FP8X4), scales=gs[:], in_=gt[:].rearrange("p v t -> p (v t)"))

@@ -20,9 +20,18 @@ SUB = mybir.AluOpType.subtract
 
 P = 128
 PACK = 4
+STRIPE = 16
+BLOCKS = K // 32
 BANK = 512
+BANKS = 8
 LAST = 128
 FIRST = V - LAST
+RUN = 4
+
+AT_FINAL_GAIN = 0
+AT_W23_CODE = 0
+AT_LATE_TOPS = 1024
+AT_Z_PLANES = 6144
 
 
 def tile_picked_sagecat_maxrelu_p_kernel(tc, x_words, x_scales, w1, w2, w3, offs, cen, pos1, pos2, pos3, pos4, out):
@@ -30,156 +39,162 @@ def tile_picked_sagecat_maxrelu_p_kernel(tc, x_words, x_scales, w1, w2, w3, offs
     with ExitStack() as ctx:
         lists = ctx.enter_context(tc.tile_pool(name="lists", bufs=1))
         keep = ctx.enter_context(tc.tile_pool(name="keep", bufs=1))
-        after = ctx.enter_context(tc.tile_pool(name="after", bufs=1))
+        reuse = ctx.enter_context(tc.tile_pool(name="reuse", bufs=1))
         psum = ctx.enter_context(tc.psum_pool(name="psum", bufs=1))
 
-        s_tab = keep.tile([P, T], U8, name="s_tab", align_bytes=64)
-        nc.sync.dma_start(s_tab[P - 16 : P, :].bitcast(I32), x_scales[0].bitcast(I32))
-        nc.vector.memset(s_tab[0 : P - 16, :].bitcast(I32), 0)
+        def load_list(name, source, entries):
+            tile = lists.tile([P, entries // STRIPE], U16, name=name)
+            nc.sync.dma_start(tile[:], source)
+            return tile
 
-        offs_t = lists.tile([P, S // 16], U16, name="offs_t")
-        nc.sync.dma_start(offs_t[:], offs)
+        def quantise(codes, scales, values):
+            nc.vector.quantize_mx(out=codes.bitcast(FP8X4), scales=scales, in_=values)
+
+        def interleave(grouped, planes):
+            nc.scalar.copy(out=grouped.rearrange("p (c i) t -> p c t i", i=RUN), in_=planes.rearrange("p t (c i) -> p c t i", i=RUN))
+
+        scale_rows = slice(P - BLOCKS, P)
+        s_tab = keep.tile([P, T], U8, name="s_tab", align_bytes=64)
+        nc.sync.dma_start(s_tab[scale_rows, :].bitcast(I32), x_scales[0].bitcast(I32))
+        nc.vector.memset(s_tab[0 : P - BLOCKS, :].bitcast(I32), 0)
+
+        offs_t = load_list("offs_t", offs, S)
 
         x_tab = keep.tile([P, T], U16, name="x_tab", align_bytes=64)
         nc.sync.dma_start(x_tab[:].bitcast(I32), x_words[0].bitcast(I32))
 
-        pos_t = []
-        for d, pos in enumerate((pos1, pos2)):
-            lt = lists.tile([P, V // 16], U16, name="pos_t%d" % d)
-            nc.sync.dma_start(lt[:], pos)
-            pos_t.append(lt)
+        pos_t = [load_list("pos_t0", pos1, V), load_list("pos_t1", pos2, V)]
 
         w1_rows = w1.rearrange("(p j) c -> p (j c)", j=PACK)
-        w1_raw = keep.tile([P, PACK * H], F32, name="w1_raw", tag="raw1")
+        w1_raw = keep.tile([P, PACK * H], F32, name="w1_raw", tag="raw_weights")
         for j in (0, 2):
             nc.sync.dma_start(w1_raw[:, j * H : (j + 2) * H], w1_rows[:, j * H : (j + 2) * H])
 
-        for d, pos in enumerate((pos3, pos4)):
-            lt = lists.tile([P, V // 16], U16, name="pos_t%d" % (d + 2))
-            nc.sync.dma_start(lt[:], pos)
-            pos_t.append(lt)
-        cen_t = lists.tile([P, V // 16], U16, name="cen_t")
-        nc.sync.dma_start(cen_t[:], cen)
+        pos_t.append(load_list("pos_t2", pos3, V))
+        pos_t.append(load_list("pos_t3", pos4, V))
+        cen_t = load_list("cen_t", cen, V)
 
         s_picked = keep.tile([P, S], U8, name="s_picked", align_bytes=64)
         nc.vector.tensor_copy(s_picked[:], s_tab[:].indirect(offs_t[:]))
         x_scale = keep.tile([P, S], U8, name="x_scale", align_bytes=64)
         nc.vector.memset(x_scale[:].bitcast(I32), 0)
-        for q in range(4):
-            nc.sync.dma_start(x_scale[32 * q : 32 * q + 4, :].bitcast(I32), s_picked[P - 16 + 4 * q : P - 12 + 4 * q, :].bitcast(I32))
+        for r in range(4):
+            first_row = P - BLOCKS + 4 * r
+            nc.sync.dma_start(x_scale[32 * r : 32 * r + 4, :].bitcast(I32), s_picked[first_row : first_row + 4, :].bitcast(I32))
         x_code = keep.tile([P, S], U16, name="x_code", align_bytes=64)
         nc.vector.tensor_copy(x_code[:], x_tab[:].indirect(offs_t[:]))
 
         w1_code = keep.tile([P, H], U32, name="w1_code", align_bytes=64)
         w1_scale = keep.tile([P, H], U8, name="w1_scale", align_bytes=64)
-        src = w1_raw[:].rearrange("p (j m t) -> p t m j", j=PACK, t=PACK)
-        first_bf = keep.tile([P, P, PACK], BF16, name="first_bf", tag="w1_bf", align_bytes=64)
-        nc.scalar.copy(out=first_bf[:, :, 0:2], in_=src[:, 0, :, 0:2])
-        nc.scalar.copy(out=first_bf[:, 0:64, 2:4], in_=src[:, 0, 0:64, 2:4])
-        nc.vector.tensor_copy(out=first_bf[:, 64:P, 2:4], in_=src[:, 0, 64:P, 2:4])
-        nc.vector.quantize_mx(out=w1_code[:, 0:P].bitcast(FP8X4), scales=w1_scale[:, 0:P], in_=first_bf[:].rearrange("p m j -> p (m j)"))
-        second_bf = keep.tile([P, P, PACK], BF16, name="second_bf", align_bytes=64)
-        nc.scalar.copy(out=second_bf[:], in_=src[:, 1, :, :])
-        rest_bf = keep.tile([P, 2, P, PACK], BF16, name="rest_bf", tag="w1_bf", align_bytes=64)
-        nc.vector.tensor_copy(out=rest_bf[:].rearrange("p t m j -> p m t j"), in_=src[:, 2:4, :, :].rearrange("p t m j -> p m t j"))
-        nc.vector.quantize_mx(out=w1_code[:, P : 2 * P].bitcast(FP8X4), scales=w1_scale[:, P : 2 * P], in_=second_bf[:].rearrange("p m j -> p (m j)"))
-        nc.vector.quantize_mx(out=w1_code[:, 2 * P : H].bitcast(FP8X4), scales=w1_scale[:, 2 * P : H], in_=rest_bf[:].rearrange("p t m j -> p (t m j)"))
+        w1_dealt = w1_raw[:].rearrange("p (j m t) -> p t m j", j=PACK, t=PACK)
+        w1_bf0 = keep.tile([P, P, PACK], BF16, name="w1_bf0", tag="w1_bf", align_bytes=64)
+        nc.scalar.copy(out=w1_bf0[:, :, 0:2], in_=w1_dealt[:, 0, :, 0:2])
+        nc.scalar.copy(out=w1_bf0[:, 0 : P // 2, 2:4], in_=w1_dealt[:, 0, 0 : P // 2, 2:4])
+        nc.vector.tensor_copy(out=w1_bf0[:, P // 2 : P, 2:4], in_=w1_dealt[:, 0, P // 2 : P, 2:4])
+        quantise(w1_code[:, 0:P], w1_scale[:, 0:P], w1_bf0[:].rearrange("p m j -> p (m j)"))
+        w1_bf1 = keep.tile([P, P, PACK], BF16, name="w1_bf1", align_bytes=64)
+        nc.scalar.copy(out=w1_bf1[:], in_=w1_dealt[:, 1, :, :])
+        w1_bf23 = keep.tile([P, 2, P, PACK], BF16, name="w1_bf23", tag="w1_bf", align_bytes=64)
+        nc.vector.tensor_copy(out=w1_bf23[:].rearrange("p t m j -> p m j t"), in_=w1_dealt[:, 2:4, :, :].rearrange("p t m j -> p m j t"))
+        quantise(w1_code[:, P : 2 * P], w1_scale[:, P : 2 * P], w1_bf1[:].rearrange("p m j -> p (m j)"))
+        quantise(w1_code[:, 2 * P : H], w1_scale[:, 2 * P : H], w1_bf23[:].rearrange("p t m j -> p (t m j)"))
 
         h = []
         bank = 0
         for t in range(PACK):
-            ht = keep.tile([P, S], F32, name="h%d" % t, align_bytes=64)
-            pieces = ((0, 512), (512, 768), (768, S)) if t == 0 else ((0, 512), (512, S))
+            plane = keep.tile([P, S], F32, name="h%d" % t, align_bytes=64)
+            pieces = ((0, BANK), (BANK, S - BANK // 2), (S - BANK // 2, S)) if t == 0 else ((0, BANK), (BANK, S))
             for a, b in pieces:
-                acc = psum.tile([P, b - a], F32, name="h_acc%d_%d" % (t, a), tag="bank%d" % (bank % 8))
+                acc = psum.tile([P, b - a], F32, name="h_acc%d_%d" % (t, a), tag="bank%d" % (bank % BANKS))
                 bank = bank + 1
                 nc.tensor.matmul_mx(
                     out=acc[:], lhsT=w1_code[:, t * P : (t + 1) * P].bitcast(FP8X4), lhsT_scale=w1_scale[:, t * P : (t + 1) * P],
                     rhs=x_code[:, a:b].bitcast(FP4X4), rhs_scale=x_scale[:, a:b], start=True, stop=True,
                 )
                 if t == 0 and b == S:
-                    nc.vector.tensor_scalar_max(ht[:, a:b], acc[:], 0.0)
+                    nc.vector.tensor_scalar_max(plane[:, a:b], acc[:], 0.0)
                 else:
-                    nc.scalar.activation(ht[:, a:b], acc[:], RELU)
-            h.append(ht)
+                    nc.scalar.activation(plane[:, a:b], acc[:], RELU)
+            h.append(plane)
 
-        w23_raw = keep.tile([P, 2, PACK, N], F32, name="w23_raw", tag="raw1")
-        for i, w in enumerate((w2, w3)):
-            nc.sync.dma_start(w23_raw[:, i, :, :], w.rearrange("(p j) c -> p j c", j=PACK))
+        w23_raw = keep.tile([P, 2, PACK, N], F32, name="w23_raw", tag="raw_weights")
+        for n, w in enumerate((w2, w3)):
+            nc.sync.dma_start(w23_raw[:, n, :, :], w.rearrange("(p j) c -> p j c", j=PACK))
         w23_bf = keep.tile([P, 2, N, PACK], BF16, name="w23_bf", align_bytes=64)
-        nc.scalar.copy(out=w23_bf[:], in_=w23_raw[:].rearrange("p i j c -> p i c j"))
+        nc.scalar.copy(out=w23_bf[:], in_=w23_raw[:].rearrange("p n j c -> p n c j"))
 
         early = keep.tile([P, 2, 2, 2, V], BF16, name="early", align_bytes=64)
-        shared = keep.tile([P, 5 * V], F32, name="shared", align_bytes=64)
-        g_planes = shared[:, 0 : PACK * V].rearrange("p (t v) -> p t v", t=PACK)
-        late = shared[:, FIRST : FIRST + PACK * V].bitcast(BF16).rearrange("p (e u t v) -> p e u t v", e=2, u=2, t=2)
+        g_and_late = keep.tile([P, (PACK + 1) * V], F32, name="g_and_late", align_bytes=64)
+        g_planes = g_and_late[:, 0 : PACK * V].rearrange("p (t v) -> p t v", t=PACK)
+        late = g_and_late[:, FIRST : FIRST + PACK * V].bitcast(BF16).rearrange("p (e u t v) -> p e u t v", e=2, u=2, t=2)
         for t in range(PACK):
             for d in range(4):
-                dst_nb = early[:, t, d // 2, d % 2, :] if t < 2 else late[:, d % 2, d // 2, t - 2, :]
-                nc.vector.tensor_copy(dst_nb, h[t][:].indirect(pos_t[d][:]))
+                picked = early[:, t, d // 2, d % 2, :] if t < 2 else late[:, d % 2, d // 2, t - 2, :]
+                nc.vector.tensor_copy(picked, h[t][:].indirect(pos_t[d][:]))
 
-        first_cen = cen_t[:, 0 : FIRST // 16]
-        last_cen = cen_t[:, FIRST // 16 : V // 16]
+        first_cen = cen_t[:, 0 : FIRST // STRIPE]
+        last_cen = cen_t[:, FIRST // STRIPE : V // STRIPE]
         nc.vector.tensor_copy(g_planes[:, 0, 0:FIRST], h[0][:].indirect(first_cen))
 
-        top = keep.tile([P, 2, 2, V], BF16, name="top", align_bytes=64)
+        early_tops = keep.tile([P, 2, 2, V], BF16, name="early_tops", align_bytes=64)
         gain = keep.tile([P, 2, 2, V], F32, name="gain", align_bytes=64)
-        gain_top = after.tile([P, V], F32, name="gain_top", offset=0, align_bytes=64)
-        z_planes = after.tile([P, PACK, V], BF16, name="z_planes", offset=6144, align_bytes=64)
+        final_gain = reuse.tile([P, V], F32, name="final_gain", offset=AT_FINAL_GAIN, align_bytes=64)
+        z_planes = reuse.tile([P, PACK, V], BF16, name="z_planes", offset=AT_Z_PLANES, align_bytes=64)
 
-        def rise(name, a, b, out_gain):
+        def rise(name, a, b, result):
             diff = keep.tile([P, V], F32, name=name)
             nc.gpsimd.tensor_tensor(diff[:], b, a, SUB)
-            nc.scalar.activation(out_gain, diff[:], RELU)
+            nc.scalar.activation(result, diff[:], RELU)
 
-        def rise_pair(t, u):
+        def rise_of_pair(t, u):
             rise("diff%d%d" % (t, u), early[:, t, u, 0, :], early[:, t, u, 1, :], gain[:, t, u, :])
 
-        rise_pair(0, 0)
-        rise_pair(0, 1)
-        nc.gpsimd.tensor_tensor(top[:, 0, 0, :], early[:, 0, 0, 0, :], gain[:, 0, 0, :], ADD)
-        rise_pair(1, 0)
-        nc.gpsimd.tensor_tensor(top[:, 0, 1, :], early[:, 0, 1, 0, :], gain[:, 0, 1, :], ADD)
-        rise_pair(1, 1)
-        rise("diff02", top[:, 0, 0, :], top[:, 0, 1, :], gain_top[:])
-        nc.gpsimd.tensor_tensor(top[:, 1, :, :], early[:, 1, :, 0, :], gain[:, 1, :, :], ADD)
-        nc.gpsimd.tensor_tensor(z_planes[:, 0, :], top[:, 0, 0, :], gain_top[:], ADD)
+        rise_of_pair(0, 0)
+        rise_of_pair(0, 1)
+        nc.gpsimd.tensor_tensor(early_tops[:, 0, 0, :], early[:, 0, 0, 0, :], gain[:, 0, 0, :], ADD)
+        rise_of_pair(1, 0)
+        nc.gpsimd.tensor_tensor(early_tops[:, 0, 1, :], early[:, 0, 1, 0, :], gain[:, 0, 1, :], ADD)
+        rise_of_pair(1, 1)
+        rise("diff_final", early_tops[:, 0, 0, :], early_tops[:, 0, 1, :], final_gain[:])
+        nc.gpsimd.tensor_tensor(early_tops[:, 1, :, :], early[:, 1, :, 0, :], gain[:, 1, :, :], ADD)
+        nc.gpsimd.tensor_tensor(z_planes[:, 0, :], early_tops[:, 0, 0, :], final_gain[:], ADD)
 
-        nc.vector.tensor_tensor(z_planes[:, 1, :], top[:, 1, 0, :], top[:, 1, 1, :], MAX)
-        top_late = after.tile([P, 2, 2, V], BF16, name="top_late", offset=1024, align_bytes=64)
-        nc.vector.tensor_tensor(top_late[:], late[:, 0, :, :, :], late[:, 1, :, :, :], MAX)
-        w23_code = after.tile([P, 2 * N], U32, name="w23_code", offset=0, align_bytes=64)
+        nc.vector.tensor_tensor(z_planes[:, 1, :], early_tops[:, 1, 0, :], early_tops[:, 1, 1, :], MAX)
+        late_tops = reuse.tile([P, 2, 2, V], BF16, name="late_tops", offset=AT_LATE_TOPS, align_bytes=64)
+        nc.vector.tensor_tensor(late_tops[:], late[:, 0, :, :, :], late[:, 1, :, :, :], MAX)
+        w23_code = reuse.tile([P, 2 * N], U32, name="w23_code", offset=AT_W23_CODE, align_bytes=64)
         w23_scale = keep.tile([P, 2 * N], U8, name="w23_scale", align_bytes=64)
-        nc.vector.quantize_mx(out=w23_code[:].bitcast(FP8X4), scales=w23_scale[:], in_=w23_bf[:].rearrange("p i c j -> p (i c j)"))
-        nc.vector.tensor_tensor(z_planes[:, 2:4, :], top_late[:, 0, :, :], top_late[:, 1, :, :], MAX)
+        quantise(w23_code[:], w23_scale[:], w23_bf[:].rearrange("p n c j -> p (n c j)"))
+        nc.vector.tensor_tensor(z_planes[:, 2:4, :], late_tops[:, 0, :, :], late_tops[:, 1, :, :], MAX)
+
         for t in range(1, PACK):
             nc.vector.tensor_copy(g_planes[:, t, 0:FIRST], h[t][:].indirect(first_cen))
         for t in range(PACK):
             nc.vector.tensor_copy(g_planes[:, t, FIRST:V], h[t][:].indirect(last_cen))
 
         z_bf = keep.tile([P, V, PACK], BF16, name="z_bf", align_bytes=64)
-        nc.scalar.copy(out=z_bf[:].rearrange("p (c i) t -> p c t i", i=4), in_=z_planes[:].rearrange("p t (c i) -> p c t i", i=4))
+        interleave(z_bf[:], z_planes[:])
         z_code = keep.tile([P, V], U32, name="z_code", align_bytes=64)
         z_scale = keep.tile([P, V], U8, name="z_scale", align_bytes=64)
-        nc.vector.quantize_mx(out=z_code[:].bitcast(FP8X4), scales=z_scale[:], in_=z_bf[:].rearrange("p v t -> p (v t)"))
+        quantise(z_code[:], z_scale[:], z_bf[:].rearrange("p v t -> p (v t)"))
 
-        groups = ((0, 256), (256, FIRST), (FIRST, V))
-        for i, (a, b) in enumerate(groups):
-            gt = after.tile([P, b - a, PACK], BF16, name="g_bf%d" % a, offset=6144 + 8 * a, align_bytes=64)
-            nc.scalar.copy(out=gt[:].rearrange("p (c i) t -> p c t i", i=4), in_=g_planes[:, :, a:b].rearrange("p t (c i) -> p c t i", i=4))
-            gc = keep.tile([P, b - a], U32, name="g_code%d" % a, align_bytes=64)
-            gs = keep.tile([P, b - a], U8, name="g_scale%d" % a, align_bytes=64)
-            nc.vector.quantize_mx(out=gc[:].bitcast(FP8X4), scales=gs[:], in_=gt[:].rearrange("p v t -> p (v t)"))
-            acc = psum.tile([P, b - a], F32, name="o_acc%d" % i, tag="bank%d" % (i + 1))
+        groups = ((0, V // 2), (V // 2, FIRST), (FIRST, V))
+        for n, (a, b) in enumerate(groups):
+            g_bf = reuse.tile([P, b - a, PACK], BF16, name="g_bf%d" % a, offset=AT_Z_PLANES + 2 * PACK * a, align_bytes=64)
+            interleave(g_bf[:], g_planes[:, :, a:b])
+            g_code = keep.tile([P, b - a], U32, name="g_code%d" % a, align_bytes=64)
+            g_scale = keep.tile([P, b - a], U8, name="g_scale%d" % a, align_bytes=64)
+            quantise(g_code[:], g_scale[:], g_bf[:].rearrange("p v t -> p (v t)"))
+            acc = psum.tile([P, b - a], F32, name="o_acc%d" % n, tag="bank%d" % (n + 1))
             nc.tensor.matmul_mx(
                 out=acc[:], lhsT=w23_code[:, N : 2 * N].bitcast(FP8X4), lhsT_scale=w23_scale[:, N : 2 * N],
                 rhs=z_code[:, a:b].bitcast(FP8X4), rhs_scale=z_scale[:, a:b], start=True, stop=False,
             )
             nc.tensor.matmul_mx(
                 out=acc[:], lhsT=w23_code[:, 0:N].bitcast(FP8X4), lhsT_scale=w23_scale[:, 0:N],
-                rhs=gc[:].bitcast(FP8X4), rhs_scale=gs[:], start=False, stop=True,
+                rhs=g_code[:].bitcast(FP8X4), rhs_scale=g_scale[:], start=False, stop=True,
             )
-            res = keep.tile([P, b - a], F32, name="res%d" % i)
+            res = keep.tile([P, b - a], F32, name="res%d" % n)
             if b == V:
                 nc.vector.tensor_scalar_max(res[:], acc[:], 0.0)
             else:

@@ -120,8 +120,6 @@ def tile_picked_sagecat_maxrelu_p_kernel(tc, x_words, x_scales, w1, w2, w3, offs
         w23_raw = keep.tile([P, 2, PACK, N], F32, name="w23_raw", tag="raw_weights")
         for n, w in enumerate((w2, w3)):
             nc.sync.dma_start(w23_raw[:, n, :, :], w.rearrange("(p j) c -> p j c", j=PACK))
-        w23_bf = keep.tile([P, 2, N, PACK], BF16, name="w23_bf", align_bytes=64)
-        nc.scalar.copy(out=w23_bf[:], in_=w23_raw[:].rearrange("p n j c -> p n c j"))
 
         early = keep.tile([P, 2, 2, 2, V], BF16, name="early", align_bytes=64)
         g_and_late = keep.tile([P, (PACK + 1) * V], F32, name="g_and_late", align_bytes=64)
@@ -137,27 +135,31 @@ def tile_picked_sagecat_maxrelu_p_kernel(tc, x_words, x_scales, w1, w2, w3, offs
         nc.vector.tensor_copy(g_planes[:, 0, 0:FIRST], h[0][:].indirect(first_cen))
 
         early_tops = keep.tile([P, 2, 2, V], BF16, name="early_tops", align_bytes=64)
-        gain = keep.tile([P, 2, 2, V], F32, name="gain", align_bytes=64)
+        gain1 = keep.tile([P, 2, V], F32, name="gain1", align_bytes=64)
         final_gain = reuse.tile([P, V], F32, name="final_gain", offset=AT_FINAL_GAIN, align_bytes=64)
         z_planes = reuse.tile([P, PACK, V], BF16, name="z_planes", offset=AT_Z_PLANES, align_bytes=64)
 
-        def rise(name, a, b, result):
-            diff = keep.tile([P, V], F32, name=name)
-            nc.gpsimd.tensor_tensor(diff[:], b, a, SUB)
-            nc.scalar.activation(result, diff[:], RELU)
+        def rise(diff, a, b, result):
+            nc.gpsimd.tensor_tensor(diff, b, a, SUB)
+            nc.scalar.activation(result, diff, RELU)
 
-        def rise_of_pair(t, u):
-            rise("diff%d%d" % (t, u), early[:, t, u, 0, :], early[:, t, u, 1, :], gain[:, t, u, :])
-
-        rise_of_pair(0, 0)
-        rise_of_pair(0, 1)
-        nc.gpsimd.tensor_tensor(early_tops[:, 0, 0, :], early[:, 0, 0, 0, :], gain[:, 0, 0, :], ADD)
-        rise_of_pair(1, 0)
-        nc.gpsimd.tensor_tensor(early_tops[:, 0, 1, :], early[:, 0, 1, 0, :], gain[:, 0, 1, :], ADD)
-        rise_of_pair(1, 1)
-        rise("diff_final", early_tops[:, 0, 0, :], early_tops[:, 0, 1, :], final_gain[:])
-        nc.gpsimd.tensor_tensor(early_tops[:, 1, :, :], early[:, 1, :, 0, :], gain[:, 1, :, :], ADD)
+        gain0 = []
+        for u in range(2):
+            diff = keep.tile([P, V], F32, name="diff0%d" % u)
+            risen = keep.tile([P, V], F32, name="gain0%d" % u, tag="pair%d" % u)
+            rise(diff[:], early[:, 0, u, 0, :], early[:, 0, u, 1, :], risen[:])
+            gain0.append(risen)
+        for u in range(2):
+            nc.gpsimd.tensor_tensor(early_tops[:, 0, u, :], early[:, 0, u, 0, :], gain0[u][:], ADD)
+            diff = keep.tile([P, V], F32, name="diff1%d" % u, tag="pair%d" % u)
+            rise(diff[:], early[:, 1, u, 0, :], early[:, 1, u, 1, :], gain1[:, u, :])
+        diff_final = keep.tile([P, V], F32, name="diff_final")
+        rise(diff_final[:], early_tops[:, 0, 0, :], early_tops[:, 0, 1, :], final_gain[:])
+        nc.gpsimd.tensor_tensor(early_tops[:, 1, :, :], early[:, 1, :, 0, :], gain1[:], ADD)
         nc.gpsimd.tensor_tensor(z_planes[:, 0, :], early_tops[:, 0, 0, :], final_gain[:], ADD)
+
+        w23_bf = keep.tile([P, 2, N, PACK], BF16, name="w23_bf", align_bytes=64)
+        nc.scalar.copy(out=w23_bf[:], in_=w23_raw[:].rearrange("p n j c -> p n c j"))
 
         nc.vector.tensor_tensor(z_planes[:, 1, :], early_tops[:, 1, 0, :], early_tops[:, 1, 1, :], MAX)
         late_tops = reuse.tile([P, 2, 2, V], BF16, name="late_tops", offset=AT_LATE_TOPS, align_bytes=64)

@@ -136,7 +136,8 @@ def tile_picked_sagecat_maxrelu_p_kernel(tc, x_words, x_scales, w1, w2, w3, offs
 
         early_tops = keep.tile([P, 2, 2, V], BF16, name="early_tops", align_bytes=64)
         gain1 = keep.tile([P, 2, V], F32, name="gain1", align_bytes=64)
-        final_gain = reuse.tile([P, V], F32, name="final_gain", offset=AT_FINAL_GAIN, align_bytes=64)
+        final_gain = keep.tile([P, V], F32, name="final_gain", align_bytes=64)
+        final_gain1 = reuse.tile([P, V], F32, name="final_gain1", offset=AT_FINAL_GAIN, align_bytes=64)
         z_planes = reuse.tile([P, PACK, V], BF16, name="z_planes", offset=AT_Z_PLANES, align_bytes=64)
 
         def rise(diff, a, b, result):
@@ -156,12 +157,14 @@ def tile_picked_sagecat_maxrelu_p_kernel(tc, x_words, x_scales, w1, w2, w3, offs
         diff_final = keep.tile([P, V], F32, name="diff_final")
         rise(diff_final[:], early_tops[:, 0, 0, :], early_tops[:, 0, 1, :], final_gain[:])
         nc.gpsimd.tensor_tensor(early_tops[:, 1, :, :], early[:, 1, :, 0, :], gain1[:], ADD)
+        diff_final1 = keep.tile([P, V], F32, name="diff_final1")
+        rise(diff_final1[:], early_tops[:, 1, 0, :], early_tops[:, 1, 1, :], final_gain1[:])
         nc.gpsimd.tensor_tensor(z_planes[:, 0, :], early_tops[:, 0, 0, :], final_gain[:], ADD)
+        nc.gpsimd.tensor_tensor(z_planes[:, 1, :], early_tops[:, 1, 0, :], final_gain1[:], ADD)
 
         w23_bf = keep.tile([P, 2, N, PACK], BF16, name="w23_bf", align_bytes=64)
         nc.scalar.copy(out=w23_bf[:], in_=w23_raw[:].rearrange("p n j c -> p n c j"))
 
-        nc.vector.tensor_tensor(z_planes[:, 1, :], early_tops[:, 1, 0, :], early_tops[:, 1, 1, :], MAX)
         late_tops = reuse.tile([P, 2, 2, V], BF16, name="late_tops", offset=AT_LATE_TOPS, align_bytes=64)
         nc.vector.tensor_tensor(late_tops[:], late[:, 0, :, :, :], late[:, 1, :, :, :], MAX)
         w23_code = reuse.tile([P, 2 * N], U32, name="w23_code", offset=AT_W23_CODE, align_bytes=64)

@@ -28,10 +28,14 @@ LAST = 128
 FIRST = V - LAST
 RUN = 4
 
-AT_FINAL_GAIN = 0
-AT_W23_CODE = 0
-AT_LATE_TOPS = 1024
-AT_Z_PLANES = 6144
+AT_DIFF_FINAL1 = 1024
+AT_G_GROUPED = (0, 2048, 3072)
+AT_FINAL_GAIN = 4096
+AT_W23_CODE = 4096
+AT_LATE_TOPS = 5120
+AT_LATE = 9216
+AT_G_LAST = AT_LATE
+AT_G_CODE = (AT_LATE + 2048, AT_LATE + 3072, AT_LATE + 3584)
 
 
 def tile_picked_sagecat_maxrelu_p_kernel(tc, x_words, x_scales, w1, w2, w3, offs, cen, pos1, pos2, pos3, pos4, out):
@@ -122,23 +126,23 @@ def tile_picked_sagecat_maxrelu_p_kernel(tc, x_words, x_scales, w1, w2, w3, offs
             nc.sync.dma_start(w23_raw[:, n, :, :], w.rearrange("(p j) c -> p j c", j=PACK))
 
         early = keep.tile([P, 2, 2, 2, V], BF16, name="early", align_bytes=64)
-        g_and_late = keep.tile([P, (PACK + 1) * V], F32, name="g_and_late", align_bytes=64)
-        g_planes = g_and_late[:, 0 : PACK * V].rearrange("p (t v) -> p t v", t=PACK)
-        late = g_and_late[:, FIRST : FIRST + PACK * V].bitcast(BF16).rearrange("p (e u t v) -> p e u t v", e=2, u=2, t=2)
+        late = reuse.tile([P, 2, 2, 2, V], BF16, name="late", offset=AT_LATE, align_bytes=64)
+        g_first = keep.tile([P, PACK, FIRST], F32, name="g_first", align_bytes=64)
+        first_cen = cen_t[:, 0 : FIRST // STRIPE]
+        last_cen = cen_t[:, FIRST // STRIPE : V // STRIPE]
         for t in range(PACK):
+            if t == PACK - 1:
+                for plane in range(PACK):
+                    nc.vector.tensor_copy(g_first[:, plane, :], h[plane][:].indirect(first_cen))
             for d in range(4):
                 picked = early[:, t, d // 2, d % 2, :] if t < 2 else late[:, d % 2, d // 2, t - 2, :]
                 nc.vector.tensor_copy(picked, h[t][:].indirect(pos_t[d][:]))
-
-        first_cen = cen_t[:, 0 : FIRST // STRIPE]
-        last_cen = cen_t[:, FIRST // STRIPE : V // STRIPE]
-        nc.vector.tensor_copy(g_planes[:, 0, 0:FIRST], h[0][:].indirect(first_cen))
 
         early_tops = keep.tile([P, 2, 2, V], BF16, name="early_tops", align_bytes=64)
         gain1 = keep.tile([P, 2, V], F32, name="gain1", align_bytes=64)
         final_gain = keep.tile([P, V], F32, name="final_gain", align_bytes=64)
         final_gain1 = reuse.tile([P, V], F32, name="final_gain1", offset=AT_FINAL_GAIN, align_bytes=64)
-        z_planes = reuse.tile([P, PACK, V], BF16, name="z_planes", offset=AT_Z_PLANES, align_bytes=64)
+        z_planes = keep.tile([P, PACK, V], BF16, name="z_planes", align_bytes=64)
 
         def rise(diff, a, b, result):
             nc.gpsimd.tensor_tensor(diff, b, a, SUB)
@@ -157,7 +161,7 @@ def tile_picked_sagecat_maxrelu_p_kernel(tc, x_words, x_scales, w1, w2, w3, offs
         diff_final = keep.tile([P, V], F32, name="diff_final")
         rise(diff_final[:], early_tops[:, 0, 0, :], early_tops[:, 0, 1, :], final_gain[:])
         nc.gpsimd.tensor_tensor(early_tops[:, 1, :, :], early[:, 1, :, 0, :], gain1[:], ADD)
-        diff_final1 = keep.tile([P, V], F32, name="diff_final1")
+        diff_final1 = reuse.tile([P, V], F32, name="diff_final1", offset=AT_DIFF_FINAL1, align_bytes=64)
         rise(diff_final1[:], early_tops[:, 1, 0, :], early_tops[:, 1, 1, :], final_gain1[:])
         nc.gpsimd.tensor_tensor(z_planes[:, 0, :], early_tops[:, 0, 0, :], final_gain[:], ADD)
         nc.gpsimd.tensor_tensor(z_planes[:, 1, :], early_tops[:, 1, 0, :], final_gain1[:], ADD)
@@ -165,43 +169,70 @@ def tile_picked_sagecat_maxrelu_p_kernel(tc, x_words, x_scales, w1, w2, w3, offs
         w23_bf = keep.tile([P, 2, N, PACK], BF16, name="w23_bf", align_bytes=64)
         nc.scalar.copy(out=w23_bf[:], in_=w23_raw[:].rearrange("p n j c -> p n c j"))
 
+        groups = ((0, V // 2), (V // 2, FIRST), (FIRST, V))
+        halves = ((0, V // 2), (V // 2, V))
+        g_bf = [reuse.tile([P, b - a, PACK], BF16, name="g_bf%d" % a, offset=AT_G_GROUPED[n], align_bytes=64) for n, (a, b) in enumerate(groups)]
+        for n in range(2):
+            interleave(g_bf[n][:], g_first[:, :, groups[n][0] : groups[n][1]])
+
         late_tops = reuse.tile([P, 2, 2, V], BF16, name="late_tops", offset=AT_LATE_TOPS, align_bytes=64)
-        nc.vector.tensor_tensor(late_tops[:], late[:, 0, :, :, :], late[:, 1, :, :, :], MAX)
+        for a, b in halves:
+            nc.vector.tensor_tensor(late_tops[:, :, :, a:b], late[:, 0, :, :, a:b], late[:, 1, :, :, a:b], MAX)
+        z_bf = []
+        for a, b in halves:
+            nc.vector.tensor_tensor(z_planes[:, 2:4, a:b], late_tops[:, 0, :, a:b], late_tops[:, 1, :, a:b], MAX)
+            grouped = keep.tile([P, b - a, PACK], BF16, name="z_bf%d" % a, align_bytes=64)
+            interleave(grouped[:], z_planes[:, :, a:b])
+            z_bf.append(grouped)
+
+        g_last = reuse.tile([P, PACK, LAST], F32, name="g_last", offset=AT_G_LAST, align_bytes=64)
+        for t in range(PACK):
+            nc.vector.tensor_copy(g_last[:, t, :], h[t][:].indirect(last_cen))
+        interleave(g_bf[2][:], g_last[:])
+
         w23_code = reuse.tile([P, 2 * N], U32, name="w23_code", offset=AT_W23_CODE, align_bytes=64)
         w23_scale = keep.tile([P, 2 * N], U8, name="w23_scale", align_bytes=64)
         quantise(w23_code[:], w23_scale[:], w23_bf[:].rearrange("p n c j -> p (n c j)"))
-        nc.vector.tensor_tensor(z_planes[:, 2:4, :], late_tops[:, 0, :, :], late_tops[:, 1, :, :], MAX)
 
-        for t in range(1, PACK):
-            nc.vector.tensor_copy(g_planes[:, t, 0:FIRST], h[t][:].indirect(first_cen))
-        for t in range(PACK):
-            nc.vector.tensor_copy(g_planes[:, t, FIRST:V], h[t][:].indirect(last_cen))
+        def quantise_g(n):
+            width = groups[n][1] - groups[n][0]
+            codes = reuse.tile([P, width], U32, name="g_code%d" % n, offset=AT_G_CODE[n], align_bytes=64)
+            scales = keep.tile([P, width], U8, name="g_scale%d" % n, align_bytes=64)
+            quantise(codes[:], scales[:], g_bf[n][:].rearrange("p v t -> p (v t)"))
+            return codes[:], scales[:]
 
-        z_bf = keep.tile([P, V, PACK], BF16, name="z_bf", align_bytes=64)
-        interleave(z_bf[:], z_planes[:])
-        z_code = keep.tile([P, V], U32, name="z_code", align_bytes=64)
-        z_scale = keep.tile([P, V], U8, name="z_scale", align_bytes=64)
-        quantise(z_code[:], z_scale[:], z_bf[:].rearrange("p v t -> p (v t)"))
+        def quantise_z(n):
+            codes = keep.tile([P, V // 2], U32, name="z_code%d" % n, align_bytes=64)
+            scales = keep.tile([P, V // 2], U8, name="z_scale%d" % n, align_bytes=64)
+            quantise(codes[:], scales[:], z_bf[n][:].rearrange("p v t -> p (v t)"))
+            return codes, scales
 
-        groups = ((0, V // 2), (V // 2, FIRST), (FIRST, V))
-        for n, (a, b) in enumerate(groups):
-            g_bf = reuse.tile([P, b - a, PACK], BF16, name="g_bf%d" % a, offset=AT_Z_PLANES + 2 * PACK * a, align_bytes=64)
-            interleave(g_bf[:], g_planes[:, :, a:b])
-            g_code = keep.tile([P, b - a], U32, name="g_code%d" % a, align_bytes=64)
-            g_scale = keep.tile([P, b - a], U8, name="g_scale%d" % a, align_bytes=64)
-            quantise(g_code[:], g_scale[:], g_bf[:].rearrange("p v t -> p (v t)"))
-            acc = psum.tile([P, b - a], F32, name="o_acc%d" % n, tag="bank%d" % (n + 1))
+        acc = [psum.tile([P, b - a], F32, name="o_acc%d" % n, tag="bank%d" % (n + 1)) for n, (a, b) in enumerate(groups)]
+
+        def product(n, weights, codes, scales, first):
+            cols = slice(weights * N, (weights + 1) * N)
             nc.tensor.matmul_mx(
-                out=acc[:], lhsT=w23_code[:, N : 2 * N].bitcast(FP8X4), lhsT_scale=w23_scale[:, N : 2 * N],
-                rhs=z_code[:, a:b].bitcast(FP8X4), rhs_scale=z_scale[:, a:b], start=True, stop=False,
+                out=acc[n][:], lhsT=w23_code[:, cols].bitcast(FP8X4), lhsT_scale=w23_scale[:, cols],
+                rhs=codes.bitcast(FP8X4), rhs_scale=scales, start=first, stop=not first,
             )
-            nc.tensor.matmul_mx(
-                out=acc[:], lhsT=w23_code[:, 0:N].bitcast(FP8X4), lhsT_scale=w23_scale[:, 0:N],
-                rhs=g_code[:].bitcast(FP8X4), rhs_scale=g_scale[:], start=False, stop=True,
-            )
+
+        def store(n):
+            a, b = groups[n]
             res = keep.tile([P, b - a], F32, name="res%d" % n)
             if b == V:
-                nc.vector.tensor_scalar_max(res[:], acc[:], 0.0)
+                nc.vector.tensor_scalar_max(res[:], acc[n][:], 0.0)
             else:
-                nc.scalar.activation(res[:], acc[:], RELU)
+                nc.scalar.activation(res[:], acc[n][:], RELU)
             nc.sync.dma_start(out[:, a:b], res[:])
+
+        product(0, 0, *quantise_g(0), True)
+        z_code, z_scale = quantise_z(0)
+        product(0, 1, z_code[:], z_scale[:], False)
+        store(0)
+        product(1, 0, *quantise_g(1), True)
+        z_code, z_scale = quantise_z(1)
+        product(1, 1, z_code[:, 0:LAST], z_scale[:, 0:LAST], False)
+        product(2, 1, z_code[:, LAST : 2 * LAST], z_scale[:, LAST : 2 * LAST], True)
+        store(1)
+        product(2, 0, *quantise_g(2), False)
+        store(2)

@@ -32,7 +32,6 @@ AT_DIFF_FINAL1 = 1024
 AT_G_GROUPED = (0, 2048, 3072)
 AT_FINAL_GAIN = 4096
 AT_W23_CODE = 4096
-AT_LATE_TOPS = 5120
 AT_LATE = 9216
 AT_G_LAST = AT_LATE
 AT_G_CODE = (AT_LATE + 2048, AT_LATE + 3072, AT_LATE + 3584)
@@ -127,57 +126,68 @@ def tile_picked_sagecat_maxrelu_p_kernel(tc, x_words, x_scales, w1, w2, w3, offs
 
         early = keep.tile([P, 2, 2, 2, V], BF16, name="early", align_bytes=64)
         late = reuse.tile([P, 2, 2, 2, V], BF16, name="late", offset=AT_LATE, align_bytes=64)
-        g_first = keep.tile([P, PACK, FIRST], F32, name="g_first", align_bytes=64)
         first_cen = cen_t[:, 0 : FIRST // STRIPE]
         last_cen = cen_t[:, FIRST // STRIPE : V // STRIPE]
-        for t in range(PACK):
-            if t == PACK - 1:
-                for plane in range(PACK):
-                    nc.vector.tensor_copy(g_first[:, plane, :], h[plane][:].indirect(first_cen))
+        for t in range(PACK - 1):
             for d in range(4):
                 picked = early[:, t, d // 2, d % 2, :] if t < 2 else late[:, d % 2, d // 2, t - 2, :]
                 nc.vector.tensor_copy(picked, h[t][:].indirect(pos_t[d][:]))
-
-        early_tops = keep.tile([P, 2, 2, V], BF16, name="early_tops", align_bytes=64)
-        gain1 = keep.tile([P, 2, V], F32, name="gain1", align_bytes=64)
-        final_gain = keep.tile([P, V], F32, name="final_gain", align_bytes=64)
-        final_gain1 = reuse.tile([P, V], F32, name="final_gain1", offset=AT_FINAL_GAIN, align_bytes=64)
-        z_planes = keep.tile([P, PACK, V], BF16, name="z_planes", align_bytes=64)
 
         def rise(diff, a, b, result):
             nc.gpsimd.tensor_tensor(diff, b, a, SUB)
             nc.scalar.activation(result, diff, RELU)
 
-        gain0 = []
+        halves = ((0, V // 2), (V // 2, V))
+        diff00 = keep.tile([P, V], F32, name="diff00", tag="g_first", align_bytes=64)
+        first_gain = keep.tile([P, V // 2], F32, name="first_gain", tag="first_half")
+        gain0 = [keep.tile([P, V], F32, name="gain0%d" % u, tag="pair%d" % u) for u in range(2)]
+        for a, b in halves:
+            rise(diff00[:, a:b], early[:, 0, 0, 0, a:b], early[:, 0, 0, 1, a:b], first_gain[:] if a == 0 else gain0[0][:, a:b])
+
+        g_first = keep.tile([P, PACK, FIRST], F32, name="g_first", tag="g_first", align_bytes=64)
+        for plane in range(PACK):
+            nc.vector.tensor_copy(g_first[:, plane, :], h[plane][:].indirect(first_cen))
+        for d in range(4):
+            nc.vector.tensor_copy(late[:, d % 2, d // 2, 1, :], h[PACK - 1][:].indirect(pos_t[d][:]))
+
+        tops = keep.tile([P, 3, 2, V], BF16, name="tops", align_bytes=64)
+        early_tops = tops[:, 0:3:2, :, :]
+        late_tops = tops[:, 1:3, :, :]
+        gain1 = keep.tile([P, 2, V], F32, name="gain1", align_bytes=64)
+        final_gain = keep.tile([P, V], F32, name="final_gain", align_bytes=64)
+        final_gain1 = reuse.tile([P, V], F32, name="final_gain1", offset=AT_FINAL_GAIN, align_bytes=64)
+        z_planes = keep.tile([P, PACK, V], BF16, name="z_planes", align_bytes=64)
+
+        nc.gpsimd.tensor_tensor(early_tops[:, 0, 0, 0 : V // 2], early[:, 0, 0, 0, 0 : V // 2], first_gain[:], ADD)
+        diff01 = keep.tile([P, V], F32, name="diff01", tag="first_half")
+        rise(diff01[:], early[:, 0, 1, 0, :], early[:, 0, 1, 1, :], gain0[1][:])
         for u in range(2):
-            diff = keep.tile([P, V], F32, name="diff0%d" % u)
-            risen = keep.tile([P, V], F32, name="gain0%d" % u, tag="pair%d" % u)
-            rise(diff[:], early[:, 0, u, 0, :], early[:, 0, u, 1, :], risen[:])
-            gain0.append(risen)
-        for u in range(2):
-            nc.gpsimd.tensor_tensor(early_tops[:, 0, u, :], early[:, 0, u, 0, :], gain0[u][:], ADD)
+            rest = slice(V // 2 if u == 0 else 0, V)
+            nc.gpsimd.tensor_tensor(early_tops[:, 0, u, rest], early[:, 0, u, 0, rest], gain0[u][:, rest], ADD)
             diff = keep.tile([P, V], F32, name="diff1%d" % u, tag="pair%d" % u)
             rise(diff[:], early[:, 1, u, 0, :], early[:, 1, u, 1, :], gain1[:, u, :])
         diff_final = keep.tile([P, V], F32, name="diff_final")
         rise(diff_final[:], early_tops[:, 0, 0, :], early_tops[:, 0, 1, :], final_gain[:])
         nc.gpsimd.tensor_tensor(early_tops[:, 1, :, :], early[:, 1, :, 0, :], gain1[:], ADD)
+        gain20 = keep.tile([P, V], F32, name="gain20")
+        rise(gain1[:, 0, :], late[:, 0, 0, 0, :], late[:, 1, 0, 0, :], gain20[:])
         diff_final1 = reuse.tile([P, V], F32, name="diff_final1", offset=AT_DIFF_FINAL1, align_bytes=64)
         rise(diff_final1[:], early_tops[:, 1, 0, :], early_tops[:, 1, 1, :], final_gain1[:])
         nc.gpsimd.tensor_tensor(z_planes[:, 0, :], early_tops[:, 0, 0, :], final_gain[:], ADD)
+        nc.gpsimd.tensor_tensor(late_tops[:, 0, 0, :], late[:, 0, 0, 0, :], gain20[:], ADD)
         nc.gpsimd.tensor_tensor(z_planes[:, 1, :], early_tops[:, 1, 0, :], final_gain1[:], ADD)
 
         w23_bf = keep.tile([P, 2, N, PACK], BF16, name="w23_bf", align_bytes=64)
         nc.scalar.copy(out=w23_bf[:], in_=w23_raw[:].rearrange("p n j c -> p n c j"))
 
         groups = ((0, V // 2), (V // 2, FIRST), (FIRST, V))
-        halves = ((0, V // 2), (V // 2, V))
         g_bf = [reuse.tile([P, b - a, PACK], BF16, name="g_bf%d" % a, offset=AT_G_GROUPED[n], align_bytes=64) for n, (a, b) in enumerate(groups)]
         for n in range(2):
             interleave(g_bf[n][:], g_first[:, :, groups[n][0] : groups[n][1]])
 
-        late_tops = reuse.tile([P, 2, 2, V], BF16, name="late_tops", offset=AT_LATE_TOPS, align_bytes=64)
         for a, b in halves:
-            nc.vector.tensor_tensor(late_tops[:, :, :, a:b], late[:, 0, :, :, a:b], late[:, 1, :, :, a:b], MAX)
+            rows = [tile.rearrange("p u t v -> p (u t) v")[:, 1:4, a:b] for tile in (late_tops, late[:, 0, :, :, :], late[:, 1, :, :, :])]
+            nc.vector.tensor_tensor(*rows, MAX)
         z_bf = []
         for a, b in halves:
             nc.vector.tensor_tensor(z_planes[:, 2:4, a:b], late_tops[:, 0, :, a:b], late_tops[:, 1, :, a:b], MAX)

@@ -1,6 +1,7 @@
 from contextlib import ExitStack
 
 import concourse.mybir as mybir
+from concourse.masks import make_identity
 
 K, T, S, V, H, N = 512, 4096, 1024, 512, 512, 128
 FLOPS = 2 * K * H * S + 2 * 2 * H * N * V
@@ -124,14 +125,20 @@ def tile_picked_sagecat_maxrelu_p_kernel(tc, x_words, x_scales, w1, w2, w3, offs
         for n, w in enumerate((w2, w3)):
             nc.sync.dma_start(w23_raw[:, n, :, :], w.rearrange("(p j) c -> p j c", j=PACK))
 
+        identity = keep.tile([P, P], F32, name="identity", align_bytes=64)
+        make_identity(nc, identity[:])
+
         early = keep.tile([P, 2, 2, 2, V], BF16, name="early", align_bytes=64)
-        late = reuse.tile([P, 2, 2, 2, V], BF16, name="late", offset=AT_LATE, align_bytes=64)
+        turned_pair = keep.tile([P, 2, V], F32, name="turned_pair", align_bytes=64)
+        rows = keep.tile([P, 11, V], BF16, name="rows", align_bytes=64)
+        second21 = keep.tile([P, V], BF16, name="second21", align_bytes=64)
         first_cen = cen_t[:, 0 : FIRST // STRIPE]
         last_cen = cen_t[:, FIRST // STRIPE : V // STRIPE]
-        for t in range(PACK - 1):
+        for t in range(2):
             for d in range(4):
-                picked = early[:, t, d // 2, d % 2, :] if t < 2 else late[:, d % 2, d // 2, t - 2, :]
-                nc.vector.tensor_copy(picked, h[t][:].indirect(pos_t[d][:]))
+                nc.vector.tensor_copy(early[:, t, d // 2, d % 2, :], h[t][:].indirect(pos_t[d][:]))
+        for d, picked in enumerate((turned_pair[:, 0, :], turned_pair[:, 1, :], rows[:, 0, :], second21[:])):
+            nc.vector.tensor_copy(picked, h[2][:].indirect(pos_t[d][:]))
 
         def rise(diff, a, b, result):
             nc.gpsimd.tensor_tensor(diff, b, a, SUB)
@@ -139,43 +146,61 @@ def tile_picked_sagecat_maxrelu_p_kernel(tc, x_words, x_scales, w1, w2, w3, offs
 
         halves = ((0, V // 2), (V // 2, V))
         diff00 = keep.tile([P, V], F32, name="diff00", tag="g_first", align_bytes=64)
-        first_gain = keep.tile([P, V // 2], F32, name="first_gain", tag="first_half")
+        first_gain = reuse.tile([P, V // 2], F32, name="first_gain", offset=AT_LATE, align_bytes=64)
         gain0 = [keep.tile([P, V], F32, name="gain0%d" % u, tag="pair%d" % u) for u in range(2)]
         for a, b in halves:
             rise(diff00[:, a:b], early[:, 0, 0, 0, a:b], early[:, 0, 0, 1, a:b], first_gain[:] if a == 0 else gain0[0][:, a:b])
 
+        nc.gpsimd.tensor_tensor(rows[:, 1, 0 : V // 2], early[:, 0, 0, 0, 0 : V // 2], first_gain[:], ADD)
+        diff01 = reuse.tile([P, V], F32, name="diff01", offset=AT_LATE, align_bytes=64)
+        rise(diff01[:], early[:, 0, 1, 0, :], early[:, 0, 1, 1, :], gain0[1][:])
+
         g_first = keep.tile([P, PACK, FIRST], F32, name="g_first", tag="g_first", align_bytes=64)
         for plane in range(PACK):
             nc.vector.tensor_copy(g_first[:, plane, :], h[plane][:].indirect(first_cen))
+        late = reuse.tile([P, 2, 2, V], BF16, name="late", offset=AT_LATE, align_bytes=64)
         for d in range(4):
-            nc.vector.tensor_copy(late[:, d % 2, d // 2, 1, :], h[PACK - 1][:].indirect(pos_t[d][:]))
+            nc.vector.tensor_copy(late[:, d % 2, d // 2, :], h[PACK - 1][:].indirect(pos_t[d][:]))
 
-        tops = keep.tile([P, 3, 2, V], BF16, name="tops", align_bytes=64)
-        early_tops = tops[:, 0:3:2, :, :]
-        late_tops = tops[:, 1:3, :, :]
+        tops0, tops1 = rows[:, 1:3, :], rows[:, 5:7, :]
+        late_tops = rows[:, 3:7, :].rearrange("p (u t) v -> p u t v", u=2)
+        z_planes = rows[:, 7:11, :]
         gain1 = keep.tile([P, 2, V], F32, name="gain1", align_bytes=64)
-        final_gain = keep.tile([P, V], F32, name="final_gain", align_bytes=64)
-        final_gain1 = reuse.tile([P, V], F32, name="final_gain1", offset=AT_FINAL_GAIN, align_bytes=64)
-        z_planes = keep.tile([P, PACK, V], BF16, name="z_planes", align_bytes=64)
+        last_gains = keep.tile([P, 2, V], F32, name="last_gains", align_bytes=64)
 
-        nc.gpsimd.tensor_tensor(early_tops[:, 0, 0, 0 : V // 2], early[:, 0, 0, 0, 0 : V // 2], first_gain[:], ADD)
-        diff01 = keep.tile([P, V], F32, name="diff01", tag="first_half")
-        rise(diff01[:], early[:, 0, 1, 0, :], early[:, 0, 1, 1, :], gain0[1][:])
+        def turn(name, bank_tag, *terms):
+            sums = psum.tile([P, V], F32, name=name, tag=bank_tag)
+            steps = [(term, j) for term in terms for j in range(V // P)]
+            for n, (term, j) in enumerate(steps):
+                cols = slice(j * P, (j + 1) * P)
+                nc.tensor.matmul(sums[:, cols], term[:, cols], identity[:], start=n == 0, stop=n == len(steps) - 1, is_transpose=True)
+            return sums
+
         for u in range(2):
             rest = slice(V // 2 if u == 0 else 0, V)
-            nc.gpsimd.tensor_tensor(early_tops[:, 0, u, rest], early[:, 0, u, 0, rest], gain0[u][:, rest], ADD)
+            nc.gpsimd.tensor_tensor(tops0[:, u, rest], early[:, 0, u, 0, rest], gain0[u][:, rest], ADD)
             diff = keep.tile([P, V], F32, name="diff1%d" % u, tag="pair%d" % u)
             rise(diff[:], early[:, 1, u, 0, :], early[:, 1, u, 1, :], gain1[:, u, :])
+            if u == 0:
+                minus_a = keep.tile([P, V], F32, name="minus_a", tag="pair0")
+                nc.scalar.mul(minus_a[:], turned_pair[:, 0, :], -1.0)
+        a_bank = turn("a_bank", "bank4", minus_a)
+        d_bank = turn("d_bank", "bank5", minus_a, turned_pair[:, 1, :])
+        a_turned = reuse.tile([P, V], F32, name="a_turned", offset=AT_FINAL_GAIN, align_bytes=64)
+        nc.scalar.mul(a_turned[:], a_bank[:], -1.0)
         diff_final = keep.tile([P, V], F32, name="diff_final")
-        rise(diff_final[:], early_tops[:, 0, 0, :], early_tops[:, 0, 1, :], final_gain[:])
-        nc.gpsimd.tensor_tensor(early_tops[:, 1, :, :], early[:, 1, :, 0, :], gain1[:], ADD)
-        gain20 = keep.tile([P, V], F32, name="gain20")
-        rise(gain1[:, 0, :], late[:, 0, 0, 0, :], late[:, 1, 0, 0, :], gain20[:])
+        rise(diff_final[:], tops0[:, 0, :], tops0[:, 1, :], last_gains[:, 1, :])
+        r_turned = keep.tile([P, V], F32, name="r_turned")
+        nc.scalar.activation(r_turned[:], d_bank[:], RELU)
+        top20 = turn("top20", "bank6", r_turned, a_turned)
+        nc.gpsimd.tensor_tensor(tops1, early[:, 1, :, 0, :], gain1[:], ADD)
+        rise(gain1[:, 0, :], rows[:, 0, :], second21[:], last_gains[:, 0, :])
+        nc.scalar.copy(out=late_tops[:, 0, 0, :], in_=top20[:])
+        final_gain1 = reuse.tile([P, V], F32, name="final_gain1", offset=AT_FINAL_GAIN, align_bytes=64)
         diff_final1 = reuse.tile([P, V], F32, name="diff_final1", offset=AT_DIFF_FINAL1, align_bytes=64)
-        rise(diff_final1[:], early_tops[:, 1, 0, :], early_tops[:, 1, 1, :], final_gain1[:])
-        nc.gpsimd.tensor_tensor(z_planes[:, 0, :], early_tops[:, 0, 0, :], final_gain[:], ADD)
-        nc.gpsimd.tensor_tensor(late_tops[:, 0, 0, :], late[:, 0, 0, 0, :], gain20[:], ADD)
-        nc.gpsimd.tensor_tensor(z_planes[:, 1, :], early_tops[:, 1, 0, :], final_gain1[:], ADD)
+        rise(diff_final1[:], tops1[:, 1, :], tops1[:, 0, :], final_gain1[:])
+        nc.gpsimd.tensor_tensor(rows[:, 5:8:2, :], rows[:, 0:2, :], last_gains[:], ADD)
+        nc.gpsimd.tensor_tensor(z_planes[:, 1, :], tops1[:, 1, :], final_gain1[:], ADD)
 
         w23_bf = keep.tile([P, 2, N, PACK], BF16, name="w23_bf", align_bytes=64)
         nc.scalar.copy(out=w23_bf[:], in_=w23_raw[:].rearrange("p n j c -> p n c j"))
@@ -186,8 +211,7 @@ def tile_picked_sagecat_maxrelu_p_kernel(tc, x_words, x_scales, w1, w2, w3, offs
             interleave(g_bf[n][:], g_first[:, :, groups[n][0] : groups[n][1]])
 
         for a, b in halves:
-            rows = [tile.rearrange("p u t v -> p (u t) v")[:, 1:4, a:b] for tile in (late_tops, late[:, 0, :, :, :], late[:, 1, :, :, :])]
-            nc.vector.tensor_tensor(*rows, MAX)
+            nc.vector.tensor_tensor(late_tops[:, :, 1, a:b], late[:, 0, :, a:b], late[:, 1, :, a:b], MAX)
         z_bf = []
         for a, b in halves:
             nc.vector.tensor_tensor(z_planes[:, 2:4, a:b], late_tops[:, 0, :, a:b], late_tops[:, 1, :, a:b], MAX)

@@ -1,7 +1,6 @@
 from contextlib import ExitStack
 
 import concourse.mybir as mybir
-from concourse.masks import make_identity
 
 K, T, S, V, H, N = 512, 4096, 1024, 512, 512, 128
 FLOPS = 2 * K * H * S + 2 * 2 * H * N * V
@@ -25,17 +24,18 @@ STRIPE = 16
 BLOCKS = K // 32
 BANK = 512
 BANKS = 8
-LAST = 128
-FIRST = V - LAST
+HALF = V // 2
 RUN = 4
 
-AT_DIFF_FINAL1 = 1024
-AT_G_GROUPED = (0, 2048, 3072)
-AT_FINAL_GAIN = 4096
-AT_W23_CODE = 4096
-AT_LATE = 9216
-AT_G_LAST = AT_LATE
-AT_G_CODE = (AT_LATE + 2048, AT_LATE + 3072, AT_LATE + 3584)
+KB = 1024
+AT_FIRST0 = 0
+AT_DIFF01 = 8 * KB
+AT_GAIN01 = 10 * KB
+AT_TOP01 = 28 * KB
+AT_Z_EARLY = 34 * KB
+AT_GAIN1 = 20 * KB
+AT_GAIN_FINAL1 = 24 * KB
+AT_Z = (AT_GAIN_FINAL1 + KB // 2, AT_GAIN_FINAL1 - KB // 2, AT_GAIN_FINAL1 - 2 * KB)
 
 
 def tile_picked_sagecat_maxrelu_p_kernel(tc, x_words, x_scales, w1, w2, w3, offs, cen, pos1, pos2, pos3, pos4, out):
@@ -125,148 +125,111 @@ def tile_picked_sagecat_maxrelu_p_kernel(tc, x_words, x_scales, w1, w2, w3, offs
         for n, w in enumerate((w2, w3)):
             nc.sync.dma_start(w23_raw[:, n, :, :], w.rearrange("(p j) c -> p j c", j=PACK))
 
-        identity = keep.tile([P, P], F32, name="identity", align_bytes=64)
-        make_identity(nc, identity[:])
+        def at(name, shape, dtype, offset):
+            return reuse.tile(shape, dtype, name=name, offset=offset, align_bytes=64)
 
-        early = keep.tile([P, 2, 2, 2, V], BF16, name="early", align_bytes=64)
-        turned_pair = keep.tile([P, 2, V], F32, name="turned_pair", align_bytes=64)
-        rows = keep.tile([P, 11, V], BF16, name="rows", align_bytes=64)
-        second21 = keep.tile([P, V], BF16, name="second21", align_bytes=64)
-        first_cen = cen_t[:, 0 : FIRST // STRIPE]
-        last_cen = cen_t[:, FIRST // STRIPE : V // STRIPE]
-        for t in range(2):
-            for d in range(4):
-                nc.vector.tensor_copy(early[:, t, d // 2, d % 2, :], h[t][:].indirect(pos_t[d][:]))
-        for d, picked in enumerate((turned_pair[:, 0, :], turned_pair[:, 1, :], rows[:, 0, :], second21[:])):
-            nc.vector.tensor_copy(picked, h[2][:].indirect(pos_t[d][:]))
+        def gather(picked, plane, entries):
+            nc.vector.tensor_copy(picked, h[plane][:].indirect(entries[:]))
 
         def rise(diff, a, b, result):
             nc.gpsimd.tensor_tensor(diff, b, a, SUB)
             nc.scalar.activation(result, diff, RELU)
 
-        halves = ((0, V // 2), (V // 2, V))
-        diff00 = keep.tile([P, V], F32, name="diff00", tag="g_first", align_bytes=64)
-        first_gain = reuse.tile([P, V // 2], F32, name="first_gain", offset=AT_LATE, align_bytes=64)
-        gain0 = [keep.tile([P, V], F32, name="gain0%d" % u, tag="pair%d" % u) for u in range(2)]
-        for a, b in halves:
-            rise(diff00[:, a:b], early[:, 0, 0, 0, a:b], early[:, 0, 0, 1, a:b], first_gain[:] if a == 0 else gain0[0][:, a:b])
+        z_planes = at("z_planes", [P, 2, V], BF16, AT_Z_EARLY)
+        tops = keep.tile([P, 4, V], BF16, name="tops", align_bytes=64)
 
-        nc.gpsimd.tensor_tensor(rows[:, 1, 0 : V // 2], early[:, 0, 0, 0, 0 : V // 2], first_gain[:], ADD)
-        diff01 = reuse.tile([P, V], F32, name="diff01", offset=AT_LATE, align_bytes=64)
-        rise(diff01[:], early[:, 0, 1, 0, :], early[:, 0, 1, 1, :], gain0[1][:])
-
-        g_first = keep.tile([P, PACK, FIRST], F32, name="g_first", tag="g_first", align_bytes=64)
-        for plane in range(PACK):
-            nc.vector.tensor_copy(g_first[:, plane, :], h[plane][:].indirect(first_cen))
-        late = reuse.tile([P, 2, 2, V], BF16, name="late", offset=AT_LATE, align_bytes=64)
-        for d in range(4):
-            nc.vector.tensor_copy(late[:, d % 2, d // 2, :], h[PACK - 1][:].indirect(pos_t[d][:]))
-
-        tops0, tops1 = rows[:, 1:3, :], rows[:, 5:7, :]
-        late_tops = rows[:, 3:7, :].rearrange("p (u t) v -> p u t v", u=2)
-        z_planes = rows[:, 7:11, :]
-        gain1 = keep.tile([P, 2, V], F32, name="gain1", align_bytes=64)
-        last_gains = keep.tile([P, 2, V], F32, name="last_gains", align_bytes=64)
-
-        def turn(name, bank_tag, *terms):
-            sums = psum.tile([P, V], F32, name=name, tag=bank_tag)
-            steps = [(term, j) for term in terms for j in range(V // P)]
-            for n, (term, j) in enumerate(steps):
-                cols = slice(j * P, (j + 1) * P)
-                nc.tensor.matmul(sums[:, cols], term[:, cols], identity[:], start=n == 0, stop=n == len(steps) - 1, is_transpose=True)
-            return sums
-
+        first0 = at("first0", [P, 2, V], F32, AT_FIRST0)
+        diff0 = [keep.tile([P, V], F32, name="diff00", align_bytes=64), at("diff01", [P, V], F32, AT_DIFF01)]
+        gain0 = [keep.tile([P, V], F32, name="gain00", align_bytes=64), at("gain01", [P, V], F32, AT_GAIN01)]
+        top0 = [keep.tile([P, V], BF16, name="top00", align_bytes=64), at("top01", [P, V], BF16, AT_TOP01)]
         for u in range(2):
-            rest = slice(V // 2 if u == 0 else 0, V)
-            nc.gpsimd.tensor_tensor(tops0[:, u, rest], early[:, 0, u, 0, rest], gain0[u][:, rest], ADD)
-            diff = keep.tile([P, V], F32, name="diff1%d" % u, tag="pair%d" % u)
-            rise(diff[:], early[:, 1, u, 0, :], early[:, 1, u, 1, :], gain1[:, u, :])
-            if u == 0:
-                minus_a = keep.tile([P, V], F32, name="minus_a", tag="pair0")
-                nc.scalar.mul(minus_a[:], turned_pair[:, 0, :], -1.0)
-        a_bank = turn("a_bank", "bank4", minus_a)
-        d_bank = turn("d_bank", "bank5", minus_a, turned_pair[:, 1, :])
-        a_turned = reuse.tile([P, V], F32, name="a_turned", offset=AT_FINAL_GAIN, align_bytes=64)
-        nc.scalar.mul(a_turned[:], a_bank[:], -1.0)
-        diff_final = keep.tile([P, V], F32, name="diff_final")
-        rise(diff_final[:], tops0[:, 0, :], tops0[:, 1, :], last_gains[:, 1, :])
-        r_turned = keep.tile([P, V], F32, name="r_turned")
-        nc.scalar.activation(r_turned[:], d_bank[:], RELU)
-        top20 = turn("top20", "bank6", r_turned, a_turned)
-        nc.gpsimd.tensor_tensor(tops1, early[:, 1, :, 0, :], gain1[:], ADD)
-        rise(gain1[:, 0, :], rows[:, 0, :], second21[:], last_gains[:, 0, :])
-        nc.scalar.copy(out=late_tops[:, 0, 0, :], in_=top20[:])
-        final_gain1 = reuse.tile([P, V], F32, name="final_gain1", offset=AT_FINAL_GAIN, align_bytes=64)
-        diff_final1 = reuse.tile([P, V], F32, name="diff_final1", offset=AT_DIFF_FINAL1, align_bytes=64)
-        rise(diff_final1[:], tops1[:, 1, :], tops1[:, 0, :], final_gain1[:])
-        nc.gpsimd.tensor_tensor(rows[:, 5:8:2, :], rows[:, 0:2, :], last_gains[:], ADD)
-        nc.gpsimd.tensor_tensor(z_planes[:, 1, :], tops1[:, 1, :], final_gain1[:], ADD)
+            gather(first0[:, u, :], 0, pos_t[2 * u])
+        for u in range(2):
+            nc.vector.tensor_tensor(diff0[u][:], h[0][:].indirect(pos_t[2 * u + 1][:]), first0[:, u, :], SUB)
+            nc.scalar.activation(gain0[u][:], diff0[u][:], RELU)
+            nc.gpsimd.tensor_tensor(top0[u][:], first0[:, u, :], gain0[u][:], ADD)
 
-        w23_bf = keep.tile([P, 2, N, PACK], BF16, name="w23_bf", align_bytes=64)
+        w23_bf = at("w23_bf", [P, 2, N, PACK], BF16, AT_DIFF01)
         nc.scalar.copy(out=w23_bf[:], in_=w23_raw[:].rearrange("p n j c -> p n c j"))
 
-        groups = ((0, V // 2), (V // 2, FIRST), (FIRST, V))
-        g_bf = [reuse.tile([P, b - a, PACK], BF16, name="g_bf%d" % a, offset=AT_G_GROUPED[n], align_bytes=64) for n, (a, b) in enumerate(groups)]
-        for n in range(2):
-            interleave(g_bf[n][:], g_first[:, :, groups[n][0] : groups[n][1]])
-
-        for a, b in halves:
-            nc.vector.tensor_tensor(late_tops[:, :, 1, a:b], late[:, 0, :, a:b], late[:, 1, :, a:b], MAX)
-        z_bf = []
-        for a, b in halves:
-            nc.vector.tensor_tensor(z_planes[:, 2:4, a:b], late_tops[:, 0, :, a:b], late_tops[:, 1, :, a:b], MAX)
-            grouped = keep.tile([P, b - a, PACK], BF16, name="z_bf%d" % a, align_bytes=64)
-            interleave(grouped[:], z_planes[:, :, a:b])
-            z_bf.append(grouped)
-
-        g_last = reuse.tile([P, PACK, LAST], F32, name="g_last", offset=AT_G_LAST, align_bytes=64)
+        pairs1 = keep.tile([P, 2, 2, V], BF16, name="pairs1", align_bytes=64)
+        for d in range(4):
+            gather(pairs1[:, d // 2, d % 2, :], 1, pos_t[d])
+        g = at("g", [P, PACK, V], F32, AT_FIRST0)
         for t in range(PACK):
-            nc.vector.tensor_copy(g_last[:, t, :], h[t][:].indirect(last_cen))
-        interleave(g_bf[2][:], g_last[:])
+            gather(g[:, t, :], t, cen_t)
 
-        w23_code = reuse.tile([P, 2 * N], U32, name="w23_code", offset=AT_W23_CODE, align_bytes=64)
+        gain1 = at("gain1", [P, 2, V], F32, AT_GAIN1)
+        diff10 = at("diff10", [P, V], F32, AT_GAIN01)
+        rise(diff10[:], pairs1[:, 0, 0, :], pairs1[:, 0, 1, :], gain1[:, 0, :])
+        diff_final0 = keep.tile([P, V], F32, name="diff_final0", align_bytes=64)
+        gain_final0 = keep.tile([P, V], F32, name="gain_final0", align_bytes=64)
+        rise(diff_final0[:], top0[0][:], top0[1][:], gain_final0[:])
+        diff11 = at("diff11", [P, V], F32, AT_TOP01)
+        rise(diff11[:], pairs1[:, 1, 0, :], pairs1[:, 1, 1, :], gain1[:, 1, :])
+        nc.gpsimd.tensor_tensor(z_planes[:, 0, :], top0[0][:], gain_final0[:], ADD)
+
+        late = at("late", [P, 2, 4, V], BF16, AT_GAIN01)
+        for t in (2, 3):
+            for d in range(4):
+                gather(late[:, d % 2, 2 * (t - 2) + d // 2, :], t, pos_t[d])
+
+        top1 = keep.tile([P, 2, V], BF16, name="top1", align_bytes=64)
+        nc.gpsimd.tensor_tensor(top1[:], pairs1[:, :, 0, :], gain1[:], ADD)
+        diff_final1 = at("diff_final1", [P, V], F32, AT_GAIN1)
+        gain_final1 = at("gain_final1", [P, V], F32, AT_GAIN_FINAL1)
+        rise(diff_final1[:], top1[:, 0, :], top1[:, 1, :], gain_final1[:])
+        g_bf = at("g_bf", [P, V, PACK], BF16, AT_TOP01)
+        for a in (0, HALF):
+            interleave(g_bf[:, a : a + HALF, :], g[:, :, a : a + HALF])
+        diff20 = at("diff20", [P, V], F32, AT_GAIN1 + 2 * KB)
+        gain20 = keep.tile([P, V], F32, name="gain20", align_bytes=64)
+        rise(diff20[:], late[:, 0, 0, :], late[:, 1, 0, :], gain20[:])
+        nc.gpsimd.tensor_tensor(z_planes[:, 1, :], top1[:, 0, :], gain_final1[:], ADD)
+        diff21 = at("diff21", [P, HALF], F32, AT_GAIN_FINAL1)
+        gain21 = keep.tile([P, HALF], F32, name="gain21", align_bytes=64)
+        rise(diff21[:], late[:, 0, 1, 0:HALF], late[:, 1, 1, 0:HALF], gain21[:])
+        groups = ((0, HALF), (HALF, V - P), (V - P, V))
+        z_bf = [at("z_bf%d" % a, [P, b - a, PACK], BF16, AT_Z[n]) for n, (a, b) in enumerate(groups)]
+        for grouped, (a, b) in zip(z_bf, groups):
+            interleave(grouped[:, :, 0:2], z_planes[:, 0:2, a:b])
+        nc.gpsimd.tensor_tensor(tops[:, 0, :], late[:, 0, 0, :], gain20[:], ADD)
+        nc.gpsimd.tensor_tensor(tops[:, 1, 0:HALF], late[:, 0, 1, 0:HALF], gain21[:], ADD)
+
+        nc.vector.tensor_tensor(tops[:, 2:4, 0:HALF], late[:, 0, 2:4, 0:HALF], late[:, 1, 2:4, 0:HALF], MAX)
+        nc.vector.tensor_tensor(tops[:, 1:4, HALF:V], late[:, 0, 1:4, HALF:V], late[:, 1, 1:4, HALF:V], MAX)
+        z_late = at("z_late", [P, 2, V], BF16, AT_Z_EARLY - 3 * KB // 2)
+        for a in (0, HALF):
+            nc.vector.tensor_tensor(z_late[:, :, a : a + HALF], tops[:, 0:4:2, a : a + HALF], tops[:, 1:4:2, a : a + HALF], MAX)
+        for grouped, (a, b) in zip(z_bf, groups):
+            interleave(grouped[:, :, 2:4], z_late[:, :, a:b])
+
+        w23_code = at("w23_code", [P, 2 * N], U32, AT_Z_EARLY + KB // 2)
         w23_scale = keep.tile([P, 2 * N], U8, name="w23_scale", align_bytes=64)
         quantise(w23_code[:], w23_scale[:], w23_bf[:].rearrange("p n c j -> p (n c j)"))
+        g_code = at("g_code", [P, V], U32, AT_Z_EARLY + 3 * KB // 2)
+        g_scale = keep.tile([P, V], U8, name="g_scale", align_bytes=64)
+        for a in (0, HALF):
+            quantise(g_code[:, a : a + HALF], g_scale[:, a : a + HALF], g_bf[:, a : a + HALF, :].rearrange("p v t -> p (v t)"))
 
-        def quantise_g(n):
-            width = groups[n][1] - groups[n][0]
-            codes = reuse.tile([P, width], U32, name="g_code%d" % n, offset=AT_G_CODE[n], align_bytes=64)
-            scales = keep.tile([P, width], U8, name="g_scale%d" % n, align_bytes=64)
-            quantise(codes[:], scales[:], g_bf[n][:].rearrange("p v t -> p (v t)"))
-            return codes[:], scales[:]
-
-        def quantise_z(n):
-            codes = keep.tile([P, V // 2], U32, name="z_code%d" % n, align_bytes=64)
-            scales = keep.tile([P, V // 2], U8, name="z_scale%d" % n, align_bytes=64)
-            quantise(codes[:], scales[:], z_bf[n][:].rearrange("p v t -> p (v t)"))
-            return codes, scales
-
-        acc = [psum.tile([P, b - a], F32, name="o_acc%d" % n, tag="bank%d" % (n + 1)) for n, (a, b) in enumerate(groups)]
-
-        def product(n, weights, codes, scales, first):
+        def product(acc, weights, codes, scales):
             cols = slice(weights * N, (weights + 1) * N)
             nc.tensor.matmul_mx(
-                out=acc[n][:], lhsT=w23_code[:, cols].bitcast(FP8X4), lhsT_scale=w23_scale[:, cols],
-                rhs=codes.bitcast(FP8X4), rhs_scale=scales, start=first, stop=not first,
+                out=acc[:], lhsT=w23_code[:, cols].bitcast(FP8X4), lhsT_scale=w23_scale[:, cols],
+                rhs=codes.bitcast(FP8X4), rhs_scale=scales, start=weights == 0, stop=weights == 1,
             )
 
-        def store(n):
-            a, b = groups[n]
-            res = keep.tile([P, b - a], F32, name="res%d" % n)
+        accs = [psum.tile([P, b - a], F32, name="o_acc%d" % a, tag="bank%d" % (n + 1)) for n, (a, b) in enumerate(groups)]
+        for acc, (a, b) in zip(accs, groups):
+            product(acc, 0, g_code[:, a:b], g_scale[:, a:b])
+        for acc, grouped, (a, b) in zip(accs, z_bf, groups):
+            z_code = keep.tile([P, b - a], U32, name="z_code%d" % a, align_bytes=64)
+            z_scale = keep.tile([P, b - a], U8, name="z_scale%d" % a, align_bytes=64)
+            quantise(z_code[:], z_scale[:], grouped[:].rearrange("p v t -> p (v t)"))
+            product(acc, 1, z_code[:], z_scale[:])
+            res = keep.tile([P, b - a], F32, name="res%d" % a)
             if b == V:
-                nc.vector.tensor_scalar_max(res[:], acc[n][:], 0.0)
+                nc.vector.tensor_scalar_max(res[:], acc[:], 0.0)
             else:
-                nc.scalar.activation(res[:], acc[n][:], RELU)
+                nc.scalar.activation(res[:], acc[:], RELU)
             nc.sync.dma_start(out[:, a:b], res[:])
-
-        product(0, 0, *quantise_g(0), True)
-        z_code, z_scale = quantise_z(0)
-        product(0, 1, z_code[:], z_scale[:], False)
-        store(0)
-        product(1, 0, *quantise_g(1), True)
-        z_code, z_scale = quantise_z(1)
-        product(1, 1, z_code[:, 0:LAST], z_scale[:, 0:LAST], False)
-        product(2, 1, z_code[:, LAST : 2 * LAST], z_scale[:, LAST : 2 * LAST], True)
-        store(1)
-        product(2, 0, *quantise_g(2), False)
-        store(2)

@@ -202,7 +202,10 @@ def tile_picked_sagecat_maxrelu_p_kernel(tc, x_words, x_scales, w1, w2, w3, offs
         for a in (0, HALF):
             nc.vector.tensor_tensor(z_late[:, :, a : a + HALF], tops[:, 0:4:2, a : a + HALF], tops[:, 1:4:2, a : a + HALF], MAX)
         for grouped, (a, b) in zip(z_bf, groups):
-            interleave(grouped[:, :, 2:4], z_late[:, :, a:b])
+            if b < V:
+                interleave(grouped[:, :, 2:4], z_late[:, :, a:b])
+            else:
+                nc.vector.tensor_copy(out=grouped[:, :, 2:4].rearrange("p (c i) t -> p c t i", i=RUN), in_=z_late[:, :, a:b].rearrange("p t (c i) -> p c t i", i=RUN))
 
         w23_code = at("w23_code", [P, 2 * N], U32, AT_Z_EARLY + KB // 2)
         w23_scale = keep.tile([P, 2 * N], U8, name="w23_scale", align_bytes=64)

@@ -192,7 +192,7 @@ def tile_picked_sagecat_maxrelu_p_kernel(tc, x_words, x_scales, w1, w2, w3, offs
         groups = ((0, HALF), (HALF, V - P), (V - P, V))
         z_bf = [at("z_bf%d" % a, [P, b - a, PACK], BF16, AT_Z[n]) for n, (a, b) in enumerate(groups)]
         for grouped, (a, b) in zip(z_bf, groups):
-            interleave(grouped[:, :, 0:2], z_planes[:, 0:2, a:b])
+            nc.scalar.copy(out=grouped[:, :, 0:2], in_=z_planes[:, :, a:b].rearrange("p t v -> p v t"))
         nc.gpsimd.tensor_tensor(tops[:, 0, :], late[:, 0, 0, :], gain20[:], ADD)
         nc.gpsimd.tensor_tensor(tops[:, 1, 0:HALF], late[:, 0, 1, 0:HALF], gain21[:], ADD)
 
@@ -203,9 +203,9 @@ def tile_picked_sagecat_maxrelu_p_kernel(tc, x_words, x_scales, w1, w2, w3, offs
             nc.vector.tensor_tensor(z_late[:, :, a : a + HALF], tops[:, 0:4:2, a : a + HALF], tops[:, 1:4:2, a : a + HALF], MAX)
         for grouped, (a, b) in zip(z_bf, groups):
             if b < V:
-                interleave(grouped[:, :, 2:4], z_late[:, :, a:b])
+                nc.scalar.copy(out=grouped[:, :, 2:4], in_=z_late[:, :, a:b].rearrange("p t v -> p v t"))
             else:
-                nc.vector.tensor_copy(out=grouped[:, :, 2:4].rearrange("p (c i) t -> p c t i", i=RUN), in_=z_late[:, :, a:b].rearrange("p t (c i) -> p c t i", i=RUN))
+                nc.vector.tensor_copy(out=grouped[:, :, 2:4], in_=z_late[:, :, a:b].rearrange("p t v -> p v t"))
 
         w23_code = at("w23_code", [P, 2 * N], U32, AT_Z_EARLY + KB // 2)
         w23_scale = keep.tile([P, 2 * N], U8, name="w23_scale", align_bytes=64)

@@ -24,6 +24,7 @@ STRIPE = 16
 BLOCKS = K // 32
 BANK = 512
 BANKS = 8
+SHARE = 80
 HALF = V // 2
 RUN = 4
 
@@ -31,11 +32,11 @@ KB = 1024
 AT_FIRST0 = 0
 AT_DIFF01 = 8 * KB
 AT_GAIN01 = 10 * KB
-AT_TOP01 = 28 * KB
-AT_Z_EARLY = 34 * KB
 AT_GAIN1 = 20 * KB
 AT_GAIN_FINAL1 = 24 * KB
 AT_Z = (AT_GAIN_FINAL1 + KB // 2, AT_GAIN_FINAL1 - KB // 2, AT_GAIN_FINAL1 - 2 * KB)
+AT_TOP01 = 28 * KB
+AT_Z_EARLY = 34 * KB
 
 
 def tile_picked_sagecat_maxrelu_p_kernel(tc, x_words, x_scales, w1, w2, w3, offs, cen, pos1, pos2, pos3, pos4, out):
@@ -91,22 +92,24 @@ def tile_picked_sagecat_maxrelu_p_kernel(tc, x_words, x_scales, w1, w2, w3, offs
         w1_code = keep.tile([P, H], U32, name="w1_code", align_bytes=64)
         w1_scale = keep.tile([P, H], U8, name="w1_scale", align_bytes=64)
         w1_dealt = w1_raw[:].rearrange("p (j m t) -> p t m j", j=PACK, t=PACK)
-        w1_bf0 = keep.tile([P, P, PACK], BF16, name="w1_bf0", tag="w1_bf", align_bytes=64)
+        w1_bf0 = keep.tile([P, P, PACK], BF16, name="w1_bf0", align_bytes=64)
         nc.scalar.copy(out=w1_bf0[:, :, 0:2], in_=w1_dealt[:, 0, :, 0:2])
+        w1_bf1 = keep.tile([P, P, PACK], BF16, name="w1_bf1", align_bytes=64)
+        nc.scalar.copy(out=w1_bf1[:, :, 0:2], in_=w1_dealt[:, 1, :, 0:2])
         nc.scalar.copy(out=w1_bf0[:, 0 : P // 2, 2:4], in_=w1_dealt[:, 0, 0 : P // 2, 2:4])
         nc.vector.tensor_copy(out=w1_bf0[:, P // 2 : P, 2:4], in_=w1_dealt[:, 0, P // 2 : P, 2:4])
+        w1_bf23 = keep.tile([P, 2, P, PACK], BF16, name="w1_bf23", align_bytes=64)
+        nc.vector.tensor_copy(out=w1_bf23[:, :, SHARE:P, :].rearrange("p t m j -> p m j t"), in_=w1_dealt[:, 2:4, SHARE:P, :].rearrange("p t m j -> p m j t"))
         quantise(w1_code[:, 0:P], w1_scale[:, 0:P], w1_bf0[:].rearrange("p m j -> p (m j)"))
-        w1_bf1 = keep.tile([P, P, PACK], BF16, name="w1_bf1", align_bytes=64)
-        nc.scalar.copy(out=w1_bf1[:], in_=w1_dealt[:, 1, :, :])
-        w1_bf23 = keep.tile([P, 2, P, PACK], BF16, name="w1_bf23", tag="w1_bf", align_bytes=64)
-        nc.vector.tensor_copy(out=w1_bf23[:].rearrange("p t m j -> p m j t"), in_=w1_dealt[:, 2:4, :, :].rearrange("p t m j -> p m j t"))
+        nc.scalar.copy(out=w1_bf1[:, :, 2:4], in_=w1_dealt[:, 1, :, 2:4])
+        nc.scalar.copy(out=w1_bf23[:, :, 0:SHARE, :].rearrange("p t m j -> p m j t"), in_=w1_dealt[:, 2:4, 0:SHARE, :].rearrange("p t m j -> p m j t"))
         quantise(w1_code[:, P : 2 * P], w1_scale[:, P : 2 * P], w1_bf1[:].rearrange("p m j -> p (m j)"))
         quantise(w1_code[:, 2 * P : H], w1_scale[:, 2 * P : H], w1_bf23[:].rearrange("p t m j -> p (t m j)"))
 
         h = []
         bank = 0
         for t in range(PACK):
-            plane = keep.tile([P, S], F32, name="h%d" % t, align_bytes=64)
+            plane = keep.tile([P, S], F32, name="h%d" % t, tag="h%d" % t, align_bytes=64)
             pieces = ((0, BANK), (BANK, S - BANK // 2), (S - BANK // 2, S)) if t == 0 else ((0, BANK), (BANK, S))
             for a, b in pieces:
                 acc = psum.tile([P, b - a], F32, name="h_acc%d_%d" % (t, a), tag="bank%d" % (bank % BANKS))
@@ -115,7 +118,7 @@ def tile_picked_sagecat_maxrelu_p_kernel(tc, x_words, x_scales, w1, w2, w3, offs
                     out=acc[:], lhsT=w1_code[:, t * P : (t + 1) * P].bitcast(FP8X4), lhsT_scale=w1_scale[:, t * P : (t + 1) * P],
                     rhs=x_code[:, a:b].bitcast(FP4X4), rhs_scale=x_scale[:, a:b], start=True, stop=True,
                 )
-                if t == 0 and b == S:
+                if t == 0 and a == BANK:
                     nc.vector.tensor_scalar_max(plane[:, a:b], acc[:], 0.0)
                 else:
                     nc.scalar.activation(plane[:, a:b], acc[:], RELU)
@@ -207,7 +210,7 @@ def tile_picked_sagecat_maxrelu_p_kernel(tc, x_words, x_scales, w1, w2, w3, offs
             else:
                 nc.vector.tensor_copy(out=grouped[:, :, 2:4], in_=z_late[:, :, a:b].rearrange("p t v -> p v t"))
 
-        w23_code = at("w23_code", [P, 2 * N], U32, AT_Z_EARLY + KB // 2)
+        w23_code = keep.tile([P, 2 * N], U32, name="w23_code", tag="h2", align_bytes=64)
         w23_scale = keep.tile([P, 2 * N], U8, name="w23_scale", align_bytes=64)
         quantise(w23_code[:], w23_scale[:], w23_bf[:].rearrange("p n c j -> p (n c j)"))
         g_code = at("g_code", [P, V], U32, AT_Z_EARLY + 3 * KB // 2)

@@ -109,7 +109,7 @@ def tile_picked_sagecat_maxrelu_p_kernel(tc, x_words, x_scales, w1, w2, w3, offs
         h = []
         bank = 0
         for t in range(PACK):
-            plane = keep.tile([P, S], F32, name="h%d" % t, tag="h%d" % t, align_bytes=64)
+            plane = keep.tile([P, S], F32, name="h%d" % t, align_bytes=64)
             pieces = ((0, BANK), (BANK, S - BANK // 2), (S - BANK // 2, S)) if t == 0 else ((0, BANK), (BANK, S))
             for a, b in pieces:
                 acc = psum.tile([P, b - a], F32, name="h_acc%d_%d" % (t, a), tag="bank%d" % (bank % BANKS))
@@ -210,7 +210,7 @@ def tile_picked_sagecat_maxrelu_p_kernel(tc, x_words, x_scales, w1, w2, w3, offs
             else:
                 nc.vector.tensor_copy(out=grouped[:, :, 2:4], in_=z_late[:, :, a:b].rearrange("p t v -> p v t"))
 
-        w23_code = keep.tile([P, 2 * N], U32, name="w23_code", tag="h2", align_bytes=64)
+        w23_code = at("w23_code", [P, 2 * N], U32, AT_Z_EARLY + KB // 2)
         w23_scale = keep.tile([P, 2 * N], U8, name="w23_scale", align_bytes=64)
         quantise(w23_code[:], w23_scale[:], w23_bf[:].rearrange("p n c j -> p (n c j)"))
         g_code = at("g_code", [P, V], U32, AT_Z_EARLY + 3 * KB // 2)

@@ -13,10 +13,11 @@ U16 = mybir.dt.uint16
 U8 = mybir.dt.uint8
 FP8X4 = mybir.dt.float8_e4m3fn_x4
 FP4X4 = mybir.dt.float4_e2m1fn_x4
+COPY = mybir.ActivationFunctionType.Copy
 RELU = mybir.ActivationFunctionType.Relu
 MAX = mybir.AluOpType.max
 ADD = mybir.AluOpType.add
-SUB = mybir.AluOpType.subtract
+MULT = mybir.AluOpType.mult
 
 P = 128
 PACK = 4
@@ -26,17 +27,11 @@ BANK = 512
 BANKS = 8
 SHARE = 80
 HALF = V // 2
+ON_VECTOR = 10
 RUN = 4
 
 KB = 1024
-AT_FIRST0 = 0
-AT_DIFF01 = 8 * KB
-AT_GAIN01 = 10 * KB
-AT_GAIN1 = 20 * KB
-AT_GAIN_FINAL1 = 24 * KB
-AT_Z = (AT_GAIN_FINAL1 + KB // 2, AT_GAIN_FINAL1 - KB // 2, AT_GAIN_FINAL1 - 2 * KB)
-AT_TOP01 = 28 * KB
-AT_Z_EARLY = 34 * KB
+AT_MEMBERS3 = 0
 
 
 def tile_picked_sagecat_maxrelu_p_kernel(tc, x_words, x_scales, w1, w2, w3, offs, cen, pos1, pos2, pos3, pos4, out):
@@ -131,92 +126,62 @@ def tile_picked_sagecat_maxrelu_p_kernel(tc, x_words, x_scales, w1, w2, w3, offs
         def at(name, shape, dtype, offset):
             return reuse.tile(shape, dtype, name=name, offset=offset, align_bytes=64)
 
-        def gather(picked, plane, entries):
+        def gather_vector(picked, plane, entries):
             nc.vector.tensor_copy(picked, h[plane][:].indirect(entries[:]))
 
-        def rise(diff, a, b, result):
-            nc.gpsimd.tensor_tensor(diff, b, a, SUB)
-            nc.scalar.activation(result, diff, RELU)
+        def gather_scalar(picked, plane, entries):
+            nc.scalar.activation(picked, h[plane][:].indirect(entries[:]), COPY)
 
-        z_planes = at("z_planes", [P, 2, V], BF16, AT_Z_EARLY)
-        tops = keep.tile([P, 4, V], BF16, name="tops", align_bytes=64)
+        def gpsimd_copy(target, source):
+            nc.gpsimd.tensor_scalar(target, source, 1.0, 0.0, MULT, ADD)
 
-        first0 = at("first0", [P, 2, V], F32, AT_FIRST0)
-        diff0 = [keep.tile([P, V], F32, name="diff00", align_bytes=64), at("diff01", [P, V], F32, AT_DIFF01)]
-        gain0 = [keep.tile([P, V], F32, name="gain00", align_bytes=64), at("gain01", [P, V], F32, AT_GAIN01)]
-        top0 = [keep.tile([P, V], BF16, name="top00", align_bytes=64), at("top01", [P, V], BF16, AT_TOP01)]
-        for u in range(2):
-            gather(first0[:, u, :], 0, pos_t[2 * u])
-        for u in range(2):
-            nc.vector.tensor_tensor(diff0[u][:], h[0][:].indirect(pos_t[2 * u + 1][:]), first0[:, u, :], SUB)
-            nc.scalar.activation(gain0[u][:], diff0[u][:], RELU)
-            nc.gpsimd.tensor_tensor(top0[u][:], first0[:, u, :], gain0[u][:], ADD)
+        w23_bf = keep.tile([P, 2, N, PACK], BF16, name="w23_bf", align_bytes=64)
+        gpsimd_copy(w23_bf[:], w23_raw[:].rearrange("p n j c -> p n c j"))
 
-        w23_bf = at("w23_bf", [P, 2, N, PACK], BF16, AT_DIFF01)
-        nc.scalar.copy(out=w23_bf[:], in_=w23_raw[:].rearrange("p n j c -> p n c j"))
-
-        pairs1 = keep.tile([P, 2, 2, V], BF16, name="pairs1", align_bytes=64)
-        for d in range(4):
-            gather(pairs1[:, d // 2, d % 2, :], 1, pos_t[d])
-        g = at("g", [P, PACK, V], F32, AT_FIRST0)
+        members = [keep.tile([P, 2, 2, V], BF16, name="members%d" % t, align_bytes=64) for t in range(PACK - 1)]
+        members.append(at("members3", [P, 2, 2, V], BF16, AT_MEMBERS3))
+        g = keep.tile([P, PACK, V], BF16, name="g", align_bytes=64)
         for t in range(PACK):
-            gather(g[:, t, :], t, cen_t)
-
-        gain1 = at("gain1", [P, 2, V], F32, AT_GAIN1)
-        diff10 = at("diff10", [P, V], F32, AT_GAIN01)
-        rise(diff10[:], pairs1[:, 0, 0, :], pairs1[:, 0, 1, :], gain1[:, 0, :])
-        diff_final0 = keep.tile([P, V], F32, name="diff_final0", align_bytes=64)
-        gain_final0 = keep.tile([P, V], F32, name="gain_final0", align_bytes=64)
-        rise(diff_final0[:], top0[0][:], top0[1][:], gain_final0[:])
-        diff11 = at("diff11", [P, V], F32, AT_TOP01)
-        rise(diff11[:], pairs1[:, 1, 0, :], pairs1[:, 1, 1, :], gain1[:, 1, :])
-        nc.gpsimd.tensor_tensor(z_planes[:, 0, :], top0[0][:], gain_final0[:], ADD)
-
-        late = at("late", [P, 2, 4, V], BF16, AT_GAIN01)
-        for t in (2, 3):
+            gather_scalar(g[:, t, :], t, cen_t)
+        for t in range(PACK):
             for d in range(4):
-                gather(late[:, d % 2, 2 * (t - 2) + d // 2, :], t, pos_t[d])
+                gather = gather_vector if 4 * t + d < ON_VECTOR else gather_scalar
+                gather(members[t][:, d % 2, d // 2, :], t, pos_t[d])
 
-        top1 = keep.tile([P, 2, V], BF16, name="top1", align_bytes=64)
-        nc.gpsimd.tensor_tensor(top1[:], pairs1[:, :, 0, :], gain1[:], ADD)
-        diff_final1 = at("diff_final1", [P, V], F32, AT_GAIN1)
-        gain_final1 = at("gain_final1", [P, V], F32, AT_GAIN_FINAL1)
-        rise(diff_final1[:], top1[:, 0, :], top1[:, 1, :], gain_final1[:])
-        g_bf = at("g_bf", [P, V, PACK], BF16, AT_TOP01)
-        for a in (0, HALF):
-            interleave(g_bf[:, a : a + HALF, :], g[:, :, a : a + HALF])
-        diff20 = at("diff20", [P, V], F32, AT_GAIN1 + 2 * KB)
-        gain20 = keep.tile([P, V], F32, name="gain20", align_bytes=64)
-        rise(diff20[:], late[:, 0, 0, :], late[:, 1, 0, :], gain20[:])
-        nc.gpsimd.tensor_tensor(z_planes[:, 1, :], top1[:, 0, :], gain_final1[:], ADD)
-        diff21 = at("diff21", [P, HALF], F32, AT_GAIN_FINAL1)
-        gain21 = keep.tile([P, HALF], F32, name="gain21", align_bytes=64)
-        rise(diff21[:], late[:, 0, 1, 0:HALF], late[:, 1, 1, 0:HALF], gain21[:])
-        groups = ((0, HALF), (HALF, V - P), (V - P, V))
-        z_bf = [at("z_bf%d" % a, [P, b - a, PACK], BF16, AT_Z[n]) for n, (a, b) in enumerate(groups)]
-        for grouped, (a, b) in zip(z_bf, groups):
-            nc.scalar.copy(out=grouped[:, :, 0:2], in_=z_planes[:, :, a:b].rearrange("p t v -> p v t"))
-        nc.gpsimd.tensor_tensor(tops[:, 0, :], late[:, 0, 0, :], gain20[:], ADD)
-        nc.gpsimd.tensor_tensor(tops[:, 1, 0:HALF], late[:, 0, 1, 0:HALF], gain21[:], ADD)
+        g_bf = keep.tile([P, V, PACK], BF16, name="g_bf", align_bytes=64)
+        gpsimd_copy(g_bf[:].rearrange("p (c i) t -> p c t i", i=RUN), g[:].rearrange("p t (c i) -> p c t i", i=RUN))
 
-        nc.vector.tensor_tensor(tops[:, 2:4, 0:HALF], late[:, 0, 2:4, 0:HALF], late[:, 1, 2:4, 0:HALF], MAX)
-        nc.vector.tensor_tensor(tops[:, 1:4, HALF:V], late[:, 0, 1:4, HALF:V], late[:, 1, 1:4, HALF:V], MAX)
-        z_late = at("z_late", [P, 2, V], BF16, AT_Z_EARLY - 3 * KB // 2)
-        for a in (0, HALF):
-            nc.vector.tensor_tensor(z_late[:, :, a : a + HALF], tops[:, 0:4:2, a : a + HALF], tops[:, 1:4:2, a : a + HALF], MAX)
-        for grouped, (a, b) in zip(z_bf, groups):
-            if b < V:
-                nc.scalar.copy(out=grouped[:, :, 2:4], in_=z_late[:, :, a:b].rearrange("p t v -> p v t"))
-            else:
-                nc.vector.tensor_copy(out=grouped[:, :, 2:4], in_=z_late[:, :, a:b].rearrange("p t v -> p v t"))
+        tops = [keep.tile([P, 2, V], BF16, name="tops%d" % t, align_bytes=64) for t in range(PACK)]
+        z = keep.tile([P, PACK, V], BF16, name="z", align_bytes=64)
 
-        w23_code = at("w23_code", [P, 2 * N], U32, AT_Z_EARLY + KB // 2)
+        def pairs(t, a, b):
+            nc.vector.tensor_tensor(tops[t][:, :, a:b], members[t][:, 0, :, a:b], members[t][:, 1, :, a:b], MAX)
+
+        def final(t, a, b):
+            nc.vector.tensor_tensor(z[:, t, a:b], tops[t][:, 0, a:b], tops[t][:, 1, a:b], MAX)
+
+        for t in range(3):
+            pairs(t, 0, V)
+        for t in range(3):
+            final(t, 0, V)
+        w23_code = keep.tile([P, 2 * N], U32, name="w23_code", align_bytes=64)
         w23_scale = keep.tile([P, 2 * N], U8, name="w23_scale", align_bytes=64)
         quantise(w23_code[:], w23_scale[:], w23_bf[:].rearrange("p n c j -> p (n c j)"))
-        g_code = at("g_code", [P, V], U32, AT_Z_EARLY + 3 * KB // 2)
+        for a in (0, HALF):
+            pairs(3, a, a + HALF)
+        for a in (0, HALF):
+            final(3, a, a + HALF)
+
+        groups = ((0, HALF), (HALF, V - P), (V - P, V))
+        z_bf = [keep.tile([P, b - a, PACK], BF16, name="z_bf%d" % a, align_bytes=64) for a, b in groups]
+        for grouped, (a, b) in zip(z_bf[:2], groups):
+            interleave(grouped[:], z[:, :, a:b])
+
+        g_code = at("g_code", [P, V], U32, AT_MEMBERS3)
         g_scale = keep.tile([P, V], U8, name="g_scale", align_bytes=64)
         for a in (0, HALF):
             quantise(g_code[:, a : a + HALF], g_scale[:, a : a + HALF], g_bf[:, a : a + HALF, :].rearrange("p v t -> p (v t)"))
+        nc.vector.tensor_copy(out=z_bf[2][:].rearrange("p (c i) t -> p c t i", i=RUN), in_=z[:, :, V - P : V].rearrange("p t (c i) -> p c t i", i=RUN))
 
         def product(acc, weights, codes, scales):
             cols = slice(weights * N, (weights + 1) * N)

@@ -27,11 +27,11 @@ BANK = 512
 BANKS = 8
 SHARE = 80
 HALF = V // 2
-ON_VECTOR = 10
 RUN = 4
 
 KB = 1024
-AT_MEMBERS3 = 0
+AT_MEMBERS01 = 0
+AT_G = (8 * KB, 10 * KB)
 
 
 def tile_picked_sagecat_maxrelu_p_kernel(tc, x_words, x_scales, w1, w2, w3, offs, cen, pos1, pos2, pos3, pos4, out):
@@ -49,9 +49,6 @@ def tile_picked_sagecat_maxrelu_p_kernel(tc, x_words, x_scales, w1, w2, w3, offs
 
         def quantise(codes, scales, values):
             nc.vector.quantize_mx(out=codes.bitcast(FP8X4), scales=scales, in_=values)
-
-        def interleave(grouped, planes):
-            nc.scalar.copy(out=grouped.rearrange("p (c i) t -> p c t i", i=RUN), in_=planes.rearrange("p t (c i) -> p c t i", i=RUN))
 
         scale_rows = slice(P - BLOCKS, P)
         s_tab = keep.tile([P, T], U8, name="s_tab", align_bytes=64)
@@ -127,61 +124,70 @@ def tile_picked_sagecat_maxrelu_p_kernel(tc, x_words, x_scales, w1, w2, w3, offs
             return reuse.tile(shape, dtype, name=name, offset=offset, align_bytes=64)
 
         def gather_vector(picked, plane, entries):
-            nc.vector.tensor_copy(picked, h[plane][:].indirect(entries[:]))
+            nc.vector.tensor_copy(picked, h[plane][:].indirect(entries))
 
         def gather_scalar(picked, plane, entries):
-            nc.scalar.activation(picked, h[plane][:].indirect(entries[:]), COPY)
+            nc.scalar.activation(picked, h[plane][:].indirect(entries), COPY)
 
         def gpsimd_copy(target, source):
             nc.gpsimd.tensor_scalar(target, source, 1.0, 0.0, MULT, ADD)
 
+        def runs(grouped, planes):
+            return grouped.rearrange("p (c i) t -> p c t i", i=RUN), planes.rearrange("p t (c i) -> p c t i", i=RUN)
+
+        def larger(result, a, b):
+            nc.vector.tensor_tensor(result, a, b, MAX)
+
         w23_bf = keep.tile([P, 2, N, PACK], BF16, name="w23_bf", align_bytes=64)
         gpsimd_copy(w23_bf[:], w23_raw[:].rearrange("p n j c -> p n c j"))
 
-        members = [keep.tile([P, 2, 2, V], BF16, name="members%d" % t, align_bytes=64) for t in range(PACK - 1)]
-        members.append(at("members3", [P, 2, 2, V], BF16, AT_MEMBERS3))
+        members01 = at("members01", [P, 2, 4, V], BF16, AT_MEMBERS01)
+        members23 = keep.tile([P, 2, 4, HALF], BF16, name="members23", align_bytes=64)
         g = keep.tile([P, PACK, V], BF16, name="g", align_bytes=64)
-        for t in range(PACK):
-            gather_scalar(g[:, t, :], t, cen_t)
-        for t in range(PACK):
+        first = slice(0, HALF // STRIPE)
+        second = slice(HALF // STRIPE, V // STRIPE)
+        gather_vector(g[:, 0, :], 0, cen_t[:])
+        for t in range(1, PACK):
+            gather_scalar(g[:, t, :], t, cen_t[:])
+        for t in (0, 1):
             for d in range(4):
-                gather = gather_vector if 4 * t + d < ON_VECTOR else gather_scalar
-                gather(members[t][:, d % 2, d // 2, :], t, pos_t[d])
+                gather = gather_scalar if (t, d) == (1, 3) else gather_vector
+                gather(members01[:, d % 2, 2 * t + d // 2, :], t, pos_t[d][:])
+        for t in (2, 3):
+            for d in range(4):
+                gather_scalar(members23[:, d % 2, 2 * (t - 2) + d // 2, :], t, pos_t[d][:, first])
+        late = keep.tile([P, 3, 2, HALF], BF16, name="late", align_bytes=64)
+        for d in range(1, 4):
+            for t in (2, 3):
+                gather_scalar(late[:, d - 1, t - 2, :], t, pos_t[d][:, second])
 
-        g_bf = keep.tile([P, V, PACK], BF16, name="g_bf", align_bytes=64)
-        gpsimd_copy(g_bf[:].rearrange("p (c i) t -> p c t i", i=RUN), g[:].rearrange("p t (c i) -> p c t i", i=RUN))
+        g_bf = [at("g_bf%d" % n, [P, HALF, PACK], BF16, AT_G[n]) for n in range(2)]
+        for n in range(2):
+            gpsimd_copy(*runs(g_bf[n][:], g[:, :, n * HALF : (n + 1) * HALF]))
 
-        tops = [keep.tile([P, 2, V], BF16, name="tops%d" % t, align_bytes=64) for t in range(PACK)]
         z = keep.tile([P, PACK, V], BF16, name="z", align_bytes=64)
-
-        def pairs(t, a, b):
-            nc.vector.tensor_tensor(tops[t][:, :, a:b], members[t][:, 0, :, a:b], members[t][:, 1, :, a:b], MAX)
-
-        def final(t, a, b):
-            nc.vector.tensor_tensor(z[:, t, a:b], tops[t][:, 0, a:b], tops[t][:, 1, a:b], MAX)
-
-        for t in range(3):
-            pairs(t, 0, V)
-        for t in range(3):
-            final(t, 0, V)
-        w23_code = keep.tile([P, 2 * N], U32, name="w23_code", align_bytes=64)
+        tops01 = keep.tile([P, 4, V], BF16, name="tops01", align_bytes=64)
+        larger(tops01[:], members01[:, 0], members01[:, 1])
+        w23_code = at("w23_code", [P, 2 * N], U32, AT_MEMBERS01)
         w23_scale = keep.tile([P, 2 * N], U8, name="w23_scale", align_bytes=64)
         quantise(w23_code[:], w23_scale[:], w23_bf[:].rearrange("p n c j -> p (n c j)"))
-        for a in (0, HALF):
-            pairs(3, a, a + HALF)
-        for a in (0, HALF):
-            final(3, a, a + HALF)
+        larger(z[:, 0:2, :], tops01[:, 0:4:2, :], tops01[:, 1:4:2, :])
+
+        g_code = keep.tile([P, V], U32, name="g_code", align_bytes=64)
+        g_scale = keep.tile([P, V], U8, name="g_scale", align_bytes=64)
+        quantise(g_code[:, 0:HALF], g_scale[:, 0:HALF], g_bf[0][:].rearrange("p v t -> p (v t)"))
+        tops23 = at("tops23", [P, 4, HALF], BF16, AT_G[0])
+        larger(tops23[:], members23[:, 0], members23[:, 1])
+        quantise(g_code[:, HALF:V], g_scale[:, HALF:V], g_bf[1][:].rearrange("p v t -> p (v t)"))
+        larger(z[:, 2:4, 0:HALF], tops23[:, 0:4:2, :], tops23[:, 1:4:2, :])
 
         groups = ((0, HALF), (HALF, V - P), (V - P, V))
         z_bf = [keep.tile([P, b - a, PACK], BF16, name="z_bf%d" % a, align_bytes=64) for a, b in groups]
-        for grouped, (a, b) in zip(z_bf[:2], groups):
-            interleave(grouped[:], z[:, :, a:b])
+        gpsimd_copy(*runs(z_bf[0][:], z[:, :, 0:HALF]))
 
-        g_code = at("g_code", [P, V], U32, AT_MEMBERS3)
-        g_scale = keep.tile([P, V], U8, name="g_scale", align_bytes=64)
-        for a in (0, HALF):
-            quantise(g_code[:, a : a + HALF], g_scale[:, a : a + HALF], g_bf[:, a : a + HALF, :].rearrange("p v t -> p (v t)"))
-        nc.vector.tensor_copy(out=z_bf[2][:].rearrange("p (c i) t -> p c t i", i=RUN), in_=z[:, :, V - P : V].rearrange("p t (c i) -> p c t i", i=RUN))
+        late0 = at("late0", [P, 2, HALF], BF16, AT_G[1])
+        for t in (2, 3):
+            gather_vector(late0[:, t - 2, :], t, pos_t[0][:, second])
 
         def product(acc, weights, codes, scales):
             cols = slice(weights * N, (weights + 1) * N)
@@ -193,14 +199,33 @@ def tile_picked_sagecat_maxrelu_p_kernel(tc, x_words, x_scales, w1, w2, w3, offs
         accs = [psum.tile([P, b - a], F32, name="o_acc%d" % a, tag="bank%d" % (n + 1)) for n, (a, b) in enumerate(groups)]
         for acc, (a, b) in zip(accs, groups):
             product(acc, 0, g_code[:, a:b], g_scale[:, a:b])
-        for acc, grouped, (a, b) in zip(accs, z_bf, groups):
+
+        def close(n):
+            a, b = groups[n]
             z_code = keep.tile([P, b - a], U32, name="z_code%d" % a, align_bytes=64)
             z_scale = keep.tile([P, b - a], U8, name="z_scale%d" % a, align_bytes=64)
-            quantise(z_code[:], z_scale[:], grouped[:].rearrange("p v t -> p (v t)"))
-            product(acc, 1, z_code[:], z_scale[:])
+            quantise(z_code[:], z_scale[:], z_bf[n][:].rearrange("p v t -> p (v t)"))
+            product(accs[n], 1, z_code[:], z_scale[:])
+
+        def leave(n):
+            a, b = groups[n]
             res = keep.tile([P, b - a], F32, name="res%d" % a)
             if b == V:
-                nc.vector.tensor_scalar_max(res[:], acc[:], 0.0)
+                nc.vector.tensor_scalar_max(res[:], accs[n][:], 0.0)
             else:
-                nc.scalar.activation(res[:], acc[:], RELU)
+                nc.scalar.activation(res[:], accs[n][:], RELU)
             nc.sync.dma_start(out[:, a:b], res[:])
+
+        of_two = keep.tile([P, 2, HALF], BF16, name="of_two", align_bytes=64)
+        larger(of_two[:], late0[:], late[:, 0])
+        close(0)
+        of_three = keep.tile([P, 2, HALF], BF16, name="of_three", align_bytes=64)
+        larger(of_three[:], of_two[:], late[:, 1])
+        for a, b in groups[1:]:
+            larger(z[:, 2:4, a:b], of_three[:, :, a - HALF : b - HALF], late[:, 2, :, a - HALF : b - HALF])
+        nc.scalar.copy(*runs(z_bf[1][:], z[:, :, HALF : V - P]))
+        nc.vector.tensor_copy(*runs(z_bf[2][:], z[:, :, V - P : V]))
+        close(1)
+        close(2)
+        for n in range(3):
+            leave(n)

@@ -32,6 +32,7 @@ RUN = 4
 KB = 1024
 AT_MEMBERS01 = 0
 AT_G = (8 * KB, 10 * KB)
+AT_Z = 12 * KB
 
 
 def tile_picked_sagecat_maxrelu_p_kernel(tc, x_words, x_scales, w1, w2, w3, offs, cen, pos1, pos2, pos3, pos4, out):
@@ -151,8 +152,10 @@ def tile_picked_sagecat_maxrelu_p_kernel(tc, x_words, x_scales, w1, w2, w3, offs
             gather_scalar(g[:, t, :], t, cen_t[:])
         for t in (0, 1):
             for d in range(4):
-                gather = gather_scalar if (t, d) == (1, 3) else gather_vector
-                gather(members01[:, d % 2, 2 * t + d // 2, :], t, pos_t[d][:])
+                if (t, d) != (1, 3):
+                    gather_vector(members01[:, d % 2, 2 * t + d // 2, :], t, pos_t[d][:])
+        gather_vector(members01[:, 1, 3, 0:HALF], 1, pos_t[3][:, first])
+        gather_scalar(members01[:, 1, 3, HALF:V], 1, pos_t[3][:, second])
         for t in (2, 3):
             for d in range(4):
                 gather_scalar(members23[:, d % 2, 2 * (t - 2) + d // 2, :], t, pos_t[d][:, first])
@@ -163,7 +166,7 @@ def tile_picked_sagecat_maxrelu_p_kernel(tc, x_words, x_scales, w1, w2, w3, offs
 
         g_bf = [at("g_bf%d" % n, [P, HALF, PACK], BF16, AT_G[n]) for n in range(2)]
         for n in range(2):
-            gpsimd_copy(*runs(g_bf[n][:], g[:, :, n * HALF : (n + 1) * HALF]))
+            gpsimd_copy(g_bf[n][:], g[:, :, n * HALF : (n + 1) * HALF].rearrange("p t v -> p v t"))
 
         z = keep.tile([P, PACK, V], BF16, name="z", align_bytes=64)
         tops01 = keep.tile([P, 4, V], BF16, name="tops01", align_bytes=64)
@@ -182,8 +185,8 @@ def tile_picked_sagecat_maxrelu_p_kernel(tc, x_words, x_scales, w1, w2, w3, offs
         larger(z[:, 2:4, 0:HALF], tops23[:, 0:4:2, :], tops23[:, 1:4:2, :])
 
         groups = ((0, HALF), (HALF, V - P), (V - P, V))
-        z_bf = [keep.tile([P, b - a, PACK], BF16, name="z_bf%d" % a, align_bytes=64) for a, b in groups]
-        gpsimd_copy(*runs(z_bf[0][:], z[:, :, 0:HALF]))
+        z_bf = [at("z_bf%d" % a, [P, b - a, PACK], BF16, AT_Z + 8 * a) for a, b in groups]
+        gpsimd_copy(z_bf[0][:], z[:, :, 0:HALF].rearrange("p t v -> p v t"))
 
         late0 = at("late0", [P, 2, HALF], BF16, AT_G[1])
         for t in (2, 3):
@@ -219,7 +222,7 @@ def tile_picked_sagecat_maxrelu_p_kernel(tc, x_words, x_scales, w1, w2, w3, offs
         of_two = keep.tile([P, 2, HALF], BF16, name="of_two", align_bytes=64)
         larger(of_two[:], late0[:], late[:, 0])
         close(0)
-        of_three = keep.tile([P, 2, HALF], BF16, name="of_three", align_bytes=64)
+        of_three = at("of_three", [P, 2, HALF], BF16, AT_Z)
         larger(of_three[:], of_two[:], late[:, 1])
         for a, b in groups[1:]:
             larger(z[:, 2:4, a:b], of_three[:, :, a - HALF : b - HALF], late[:, 2, :, a - HALF : b - HALF])

@@ -17,6 +17,8 @@ COPY = mybir.ActivationFunctionType.Copy
 RELU = mybir.ActivationFunctionType.Relu
 MAX = mybir.AluOpType.max
 ADD = mybir.AluOpType.add
+SUB = mybir.AluOpType.subtract
+MIN = mybir.AluOpType.min
 MULT = mybir.AluOpType.mult
 
 P = 128
@@ -27,12 +29,12 @@ BANK = 512
 BANKS = 8
 SHARE = 80
 HALF = V // 2
+LARGEST = 3.4028234663852886e38
 RUN = 4
 
 KB = 1024
-AT_MEMBERS01 = 0
-AT_G = (8 * KB, 10 * KB)
-AT_Z = 12 * KB
+AT_SCALES = 0
+AT_W1_BF23 = 4 * KB
 
 
 def tile_picked_sagecat_maxrelu_p_kernel(tc, x_words, x_scales, w1, w2, w3, offs, cen, pos1, pos2, pos3, pos4, out):
@@ -52,7 +54,7 @@ def tile_picked_sagecat_maxrelu_p_kernel(tc, x_words, x_scales, w1, w2, w3, offs
             nc.vector.quantize_mx(out=codes.bitcast(FP8X4), scales=scales, in_=values)
 
         scale_rows = slice(P - BLOCKS, P)
-        s_tab = keep.tile([P, T], U8, name="s_tab", align_bytes=64)
+        s_tab = reuse.tile([P, T], U8, name="s_tab", offset=AT_SCALES, align_bytes=64)
         nc.sync.dma_start(s_tab[scale_rows, :].bitcast(I32), x_scales[0].bitcast(I32))
         nc.vector.memset(s_tab[0 : P - BLOCKS, :].bitcast(I32), 0)
 
@@ -64,7 +66,7 @@ def tile_picked_sagecat_maxrelu_p_kernel(tc, x_words, x_scales, w1, w2, w3, offs
         pos_t = [load_list("pos_t0", pos1, V), load_list("pos_t1", pos2, V)]
 
         w1_rows = w1.rearrange("(p j) c -> p (j c)", j=PACK)
-        w1_raw = keep.tile([P, PACK * H], F32, name="w1_raw", tag="raw_weights")
+        w1_raw = keep.tile([P, PACK * H], F32, name="w1_raw")
         for j in (0, 2):
             nc.sync.dma_start(w1_raw[:, j * H : (j + 2) * H], w1_rows[:, j * H : (j + 2) * H])
 
@@ -91,7 +93,7 @@ def tile_picked_sagecat_maxrelu_p_kernel(tc, x_words, x_scales, w1, w2, w3, offs
         nc.scalar.copy(out=w1_bf1[:, :, 0:2], in_=w1_dealt[:, 1, :, 0:2])
         nc.scalar.copy(out=w1_bf0[:, 0 : P // 2, 2:4], in_=w1_dealt[:, 0, 0 : P // 2, 2:4])
         nc.vector.tensor_copy(out=w1_bf0[:, P // 2 : P, 2:4], in_=w1_dealt[:, 0, P // 2 : P, 2:4])
-        w1_bf23 = keep.tile([P, 2, P, PACK], BF16, name="w1_bf23", align_bytes=64)
+        w1_bf23 = reuse.tile([P, 2, P, PACK], BF16, name="w1_bf23", offset=AT_W1_BF23, align_bytes=64)
         nc.vector.tensor_copy(out=w1_bf23[:, :, SHARE:P, :].rearrange("p t m j -> p m j t"), in_=w1_dealt[:, 2:4, SHARE:P, :].rearrange("p t m j -> p m j t"))
         quantise(w1_code[:, 0:P], w1_scale[:, 0:P], w1_bf0[:].rearrange("p m j -> p (m j)"))
         nc.scalar.copy(out=w1_bf1[:, :, 2:4], in_=w1_dealt[:, 1, :, 2:4])
@@ -117,7 +119,7 @@ def tile_picked_sagecat_maxrelu_p_kernel(tc, x_words, x_scales, w1, w2, w3, offs
                     nc.scalar.activation(plane[:, a:b], acc[:], RELU)
             h.append(plane)
 
-        w23_raw = keep.tile([P, 2, PACK, N], F32, name="w23_raw", tag="raw_weights")
+        w23_raw = reuse.tile([P, 2, PACK, N], F32, name="w23_raw", offset=AT_SCALES, align_bytes=64)
         for n, w in enumerate((w2, w3)):
             nc.sync.dma_start(w23_raw[:, n, :, :], w.rearrange("(p j) c -> p j c", j=PACK))
 
@@ -139,58 +141,63 @@ def tile_picked_sagecat_maxrelu_p_kernel(tc, x_words, x_scales, w1, w2, w3, offs
         def larger(result, a, b):
             nc.vector.tensor_tensor(result, a, b, MAX)
 
-        w23_bf = keep.tile([P, 2, N, PACK], BF16, name="w23_bf", align_bytes=64)
+        w23_bf = at("w23_bf", [P, 2, N, PACK], BF16, AT_W1_BF23)
         gpsimd_copy(w23_bf[:], w23_raw[:].rearrange("p n j c -> p n c j"))
 
-        members01 = at("members01", [P, 2, 4, V], BF16, AT_MEMBERS01)
+        first0 = keep.tile([P, 2, V], F32, name="first0", align_bytes=64)
+        diff0 = keep.tile([P, 2, V], F32, name="diff0", align_bytes=64)
+        gain0 = keep.tile([P, 2, V], F32, name="gain0", align_bytes=64)
+        members1 = keep.tile([P, 2, 2, V], BF16, name="members1", align_bytes=64)
         members23 = keep.tile([P, 2, 4, HALF], BF16, name="members23", align_bytes=64)
+        late = keep.tile([P, 4, 2, HALF], BF16, name="late", align_bytes=64)
+        tops01 = keep.tile([P, 2, 2, V], BF16, name="tops01", align_bytes=64)
         g = keep.tile([P, PACK, V], BF16, name="g", align_bytes=64)
         first = slice(0, HALF // STRIPE)
         second = slice(HALF // STRIPE, V // STRIPE)
-        gather_vector(g[:, 0, :], 0, cen_t[:])
+        for u in range(2):
+            gather_vector(first0[:, u, :], 0, pos_t[2 * u][:])
+            if u == 1:
+                gather_vector(g[:, 0, :], 0, cen_t[:])
+            nc.vector.tensor_tensor(diff0[:, u, :], h[0][:].indirect(pos_t[2 * u + 1][:]), first0[:, u, :], SUB)
+            nc.gpsimd.tensor_scalar(gain0[:, u, :], diff0[:, u, :], LARGEST, 0.0, MIN, MAX)
+            nc.gpsimd.tensor_tensor(tops01[:, u, 0, :], first0[:, u, :], gain0[:, u, :], ADD)
         for t in range(1, PACK):
             gather_scalar(g[:, t, :], t, cen_t[:])
-        for t in (0, 1):
-            for d in range(4):
-                if (t, d) != (1, 3):
-                    gather_vector(members01[:, d % 2, 2 * t + d // 2, :], t, pos_t[d][:])
-        gather_vector(members01[:, 1, 3, 0:HALF], 1, pos_t[3][:, first])
-        gather_scalar(members01[:, 1, 3, HALF:V], 1, pos_t[3][:, second])
+        for d in range(4):
+            gather_vector(members1[:, d % 2, d // 2, :], 1, pos_t[d][:])
         for t in (2, 3):
             for d in range(4):
-                gather_scalar(members23[:, d % 2, 2 * (t - 2) + d // 2, :], t, pos_t[d][:, first])
-        late = keep.tile([P, 3, 2, HALF], BF16, name="late", align_bytes=64)
-        for d in range(1, 4):
+                gather = gather_vector if (t, d) == (2, 0) else gather_scalar
+                gather(members23[:, d % 2, 2 * (t - 2) + d // 2, :], t, pos_t[d][:, first])
+        for d in range(4):
             for t in (2, 3):
-                gather_scalar(late[:, d - 1, t - 2, :], t, pos_t[d][:, second])
+                gather_scalar(late[:, d, t - 2, :], t, pos_t[d][:, second])
 
-        g_bf = [at("g_bf%d" % n, [P, HALF, PACK], BF16, AT_G[n]) for n in range(2)]
+        g_bf = [keep.tile([P, HALF, PACK], BF16, name="g_bf%d" % n, align_bytes=64) for n in range(2)]
         for n in range(2):
             gpsimd_copy(g_bf[n][:], g[:, :, n * HALF : (n + 1) * HALF].rearrange("p t v -> p v t"))
 
         z = keep.tile([P, PACK, V], BF16, name="z", align_bytes=64)
-        tops01 = keep.tile([P, 4, V], BF16, name="tops01", align_bytes=64)
-        larger(tops01[:], members01[:, 0], members01[:, 1])
-        w23_code = at("w23_code", [P, 2 * N], U32, AT_MEMBERS01)
+        larger(tops01[:, :, 1, :], members1[:, 0], members1[:, 1])
+        w23_code = keep.tile([P, 2 * N], U32, name="w23_code", align_bytes=64)
         w23_scale = keep.tile([P, 2 * N], U8, name="w23_scale", align_bytes=64)
         quantise(w23_code[:], w23_scale[:], w23_bf[:].rearrange("p n c j -> p (n c j)"))
-        larger(z[:, 0:2, :], tops01[:, 0:4:2, :], tops01[:, 1:4:2, :])
+        larger(z[:, 0:2, :], tops01[:, 0], tops01[:, 1])
 
         g_code = keep.tile([P, V], U32, name="g_code", align_bytes=64)
         g_scale = keep.tile([P, V], U8, name="g_scale", align_bytes=64)
-        quantise(g_code[:, 0:HALF], g_scale[:, 0:HALF], g_bf[0][:].rearrange("p v t -> p (v t)"))
-        tops23 = at("tops23", [P, 4, HALF], BF16, AT_G[0])
+
+        def quantise_g(n):
+            half = slice(n * HALF, (n + 1) * HALF)
+            quantise(g_code[:, half], g_scale[:, half], g_bf[n][:].rearrange("p v t -> p (v t)"))
+
+        tops23 = keep.tile([P, 4, HALF], BF16, name="tops23", align_bytes=64)
         larger(tops23[:], members23[:, 0], members23[:, 1])
-        quantise(g_code[:, HALF:V], g_scale[:, HALF:V], g_bf[1][:].rearrange("p v t -> p (v t)"))
+        quantise_g(0)
         larger(z[:, 2:4, 0:HALF], tops23[:, 0:4:2, :], tops23[:, 1:4:2, :])
 
         groups = ((0, HALF), (HALF, V - P), (V - P, V))
-        z_bf = [at("z_bf%d" % a, [P, b - a, PACK], BF16, AT_Z + 8 * a) for a, b in groups]
-        gpsimd_copy(z_bf[0][:], z[:, :, 0:HALF].rearrange("p t v -> p v t"))
-
-        late0 = at("late0", [P, 2, HALF], BF16, AT_G[1])
-        for t in (2, 3):
-            gather_vector(late0[:, t - 2, :], t, pos_t[0][:, second])
+        z_bf = [keep.tile([P, b - a, PACK], BF16, name="z_bf%d" % a, align_bytes=64) for a, b in groups]
 
         def product(acc, weights, codes, scales):
             cols = slice(weights * N, (weights + 1) * N)
@@ -200,8 +207,10 @@ def tile_picked_sagecat_maxrelu_p_kernel(tc, x_words, x_scales, w1, w2, w3, offs
             )
 
         accs = [psum.tile([P, b - a], F32, name="o_acc%d" % a, tag="bank%d" % (n + 1)) for n, (a, b) in enumerate(groups)]
-        for acc, (a, b) in zip(accs, groups):
-            product(acc, 0, g_code[:, a:b], g_scale[:, a:b])
+
+        def open_group(n):
+            a, b = groups[n]
+            product(accs[n], 0, g_code[:, a:b], g_scale[:, a:b])
 
         def close(n):
             a, b = groups[n]
@@ -219,13 +228,18 @@ def tile_picked_sagecat_maxrelu_p_kernel(tc, x_words, x_scales, w1, w2, w3, offs
                 nc.scalar.activation(res[:], accs[n][:], RELU)
             nc.sync.dma_start(out[:, a:b], res[:])
 
+        open_group(0)
         of_two = keep.tile([P, 2, HALF], BF16, name="of_two", align_bytes=64)
-        larger(of_two[:], late0[:], late[:, 0])
+        larger(of_two[:], late[:, 0], late[:, 1])
+        nc.vector.tensor_copy(*runs(z_bf[0][:], z[:, :, 0:HALF]))
+        of_three = keep.tile([P, 2, HALF], BF16, name="of_three", align_bytes=64)
+        larger(of_three[:], of_two[:], late[:, 2])
         close(0)
-        of_three = at("of_three", [P, 2, HALF], BF16, AT_Z)
-        larger(of_three[:], of_two[:], late[:, 1])
         for a, b in groups[1:]:
-            larger(z[:, 2:4, a:b], of_three[:, :, a - HALF : b - HALF], late[:, 2, :, a - HALF : b - HALF])
+            larger(z[:, 2:4, a:b], of_three[:, :, a - HALF : b - HALF], late[:, 3, :, a - HALF : b - HALF])
+        quantise_g(1)
+        open_group(1)
+        open_group(2)
         nc.scalar.copy(*runs(z_bf[1][:], z[:, :, HALF : V - P]))
         nc.vector.tensor_copy(*runs(z_bf[2][:], z[:, :, V - P : V]))
         close(1)

@@ -17,8 +17,6 @@ COPY = mybir.ActivationFunctionType.Copy
 RELU = mybir.ActivationFunctionType.Relu
 MAX = mybir.AluOpType.max
 ADD = mybir.AluOpType.add
-SUB = mybir.AluOpType.subtract
-MIN = mybir.AluOpType.min
 MULT = mybir.AluOpType.mult
 
 P = 128
@@ -29,12 +27,10 @@ BANK = 512
 BANKS = 8
 SHARE = 80
 HALF = V // 2
-LARGEST = 3.4028234663852886e38
 RUN = 4
 
 KB = 1024
-AT_SCALES = 0
-AT_W1_BF23 = 4 * KB
+AT_MEMBERS01 = 0
 
 
 def tile_picked_sagecat_maxrelu_p_kernel(tc, x_words, x_scales, w1, w2, w3, offs, cen, pos1, pos2, pos3, pos4, out):
@@ -54,7 +50,7 @@ def tile_picked_sagecat_maxrelu_p_kernel(tc, x_words, x_scales, w1, w2, w3, offs
             nc.vector.quantize_mx(out=codes.bitcast(FP8X4), scales=scales, in_=values)
 
         scale_rows = slice(P - BLOCKS, P)
-        s_tab = reuse.tile([P, T], U8, name="s_tab", offset=AT_SCALES, align_bytes=64)
+        s_tab = keep.tile([P, T], U8, name="s_tab", align_bytes=64)
         nc.sync.dma_start(s_tab[scale_rows, :].bitcast(I32), x_scales[0].bitcast(I32))
         nc.vector.memset(s_tab[0 : P - BLOCKS, :].bitcast(I32), 0)
 
@@ -66,7 +62,7 @@ def tile_picked_sagecat_maxrelu_p_kernel(tc, x_words, x_scales, w1, w2, w3, offs
         pos_t = [load_list("pos_t0", pos1, V), load_list("pos_t1", pos2, V)]
 
         w1_rows = w1.rearrange("(p j) c -> p (j c)", j=PACK)
-        w1_raw = keep.tile([P, PACK * H], F32, name="w1_raw")
+        w1_raw = keep.tile([P, PACK * H], F32, name="w1_raw", tag="raw_weights")
         for j in (0, 2):
             nc.sync.dma_start(w1_raw[:, j * H : (j + 2) * H], w1_rows[:, j * H : (j + 2) * H])
 
@@ -93,7 +89,7 @@ def tile_picked_sagecat_maxrelu_p_kernel(tc, x_words, x_scales, w1, w2, w3, offs
         nc.scalar.copy(out=w1_bf1[:, :, 0:2], in_=w1_dealt[:, 1, :, 0:2])
         nc.scalar.copy(out=w1_bf0[:, 0 : P // 2, 2:4], in_=w1_dealt[:, 0, 0 : P // 2, 2:4])
         nc.vector.tensor_copy(out=w1_bf0[:, P // 2 : P, 2:4], in_=w1_dealt[:, 0, P // 2 : P, 2:4])
-        w1_bf23 = reuse.tile([P, 2, P, PACK], BF16, name="w1_bf23", offset=AT_W1_BF23, align_bytes=64)
+        w1_bf23 = keep.tile([P, 2, P, PACK], BF16, name="w1_bf23", align_bytes=64)
         nc.vector.tensor_copy(out=w1_bf23[:, :, SHARE:P, :].rearrange("p t m j -> p m j t"), in_=w1_dealt[:, 2:4, SHARE:P, :].rearrange("p t m j -> p m j t"))
         quantise(w1_code[:, 0:P], w1_scale[:, 0:P], w1_bf0[:].rearrange("p m j -> p (m j)"))
         nc.scalar.copy(out=w1_bf1[:, :, 2:4], in_=w1_dealt[:, 1, :, 2:4])
@@ -119,7 +115,7 @@ def tile_picked_sagecat_maxrelu_p_kernel(tc, x_words, x_scales, w1, w2, w3, offs
                     nc.scalar.activation(plane[:, a:b], acc[:], RELU)
             h.append(plane)
 
-        w23_raw = reuse.tile([P, 2, PACK, N], F32, name="w23_raw", offset=AT_SCALES, align_bytes=64)
+        w23_raw = keep.tile([P, 2, PACK, N], F32, name="w23_raw", tag="raw_weights")
         for n, w in enumerate((w2, w3)):
             nc.sync.dma_start(w23_raw[:, n, :, :], w.rearrange("(p j) c -> p j c", j=PACK))
 
@@ -141,34 +137,28 @@ def tile_picked_sagecat_maxrelu_p_kernel(tc, x_words, x_scales, w1, w2, w3, offs
         def larger(result, a, b):
             nc.vector.tensor_tensor(result, a, b, MAX)
 
-        w23_bf = at("w23_bf", [P, 2, N, PACK], BF16, AT_W1_BF23)
+        w23_bf = keep.tile([P, 2, N, PACK], BF16, name="w23_bf", align_bytes=64)
         gpsimd_copy(w23_bf[:], w23_raw[:].rearrange("p n j c -> p n c j"))
 
-        first0 = keep.tile([P, 2, V], F32, name="first0", align_bytes=64)
-        diff0 = keep.tile([P, 2, V], F32, name="diff0", align_bytes=64)
-        gain0 = keep.tile([P, 2, V], F32, name="gain0", align_bytes=64)
-        members1 = keep.tile([P, 2, 2, V], BF16, name="members1", align_bytes=64)
+        members01 = at("members01", [P, 2, 2, 2, V], BF16, AT_MEMBERS01)
         members23 = keep.tile([P, 2, 4, HALF], BF16, name="members23", align_bytes=64)
         late = keep.tile([P, 4, 2, HALF], BF16, name="late", align_bytes=64)
         tops01 = keep.tile([P, 2, 2, V], BF16, name="tops01", align_bytes=64)
         g = keep.tile([P, PACK, V], BF16, name="g", align_bytes=64)
         first = slice(0, HALF // STRIPE)
         second = slice(HALF // STRIPE, V // STRIPE)
-        for u in range(2):
-            gather_vector(first0[:, u, :], 0, pos_t[2 * u][:])
-            if u == 1:
-                gather_vector(g[:, 0, :], 0, cen_t[:])
-            nc.vector.tensor_tensor(diff0[:, u, :], h[0][:].indirect(pos_t[2 * u + 1][:]), first0[:, u, :], SUB)
-            nc.gpsimd.tensor_scalar(gain0[:, u, :], diff0[:, u, :], LARGEST, 0.0, MIN, MAX)
-            nc.gpsimd.tensor_tensor(tops01[:, u, 0, :], first0[:, u, :], gain0[:, u, :], ADD)
+        gather_vector(g[:, 0, :], 0, cen_t[:])
         for t in range(1, PACK):
             gather_scalar(g[:, t, :], t, cen_t[:])
-        for d in range(4):
-            gather_vector(members1[:, d % 2, d // 2, :], 1, pos_t[d][:])
-        for t in (2, 3):
+        for t in (0, 1):
             for d in range(4):
-                gather = gather_vector if (t, d) == (2, 0) else gather_scalar
-                gather(members23[:, d % 2, 2 * (t - 2) + d // 2, :], t, pos_t[d][:, first])
+                gather_vector(members01[:, d % 2, d // 2, t, :], t, pos_t[d][:])
+        gather_vector(members23[:, 0, 0, :], 2, pos_t[0][:, first])
+        gather_vector(members23[:, 0, 2, 0:P], 3, pos_t[0][:, 0 : P // STRIPE])
+        gather_scalar(members23[:, 0, 2, P:HALF], 3, pos_t[0][:, P // STRIPE : HALF // STRIPE])
+        for t in (2, 3):
+            for d in range(1, 4):
+                gather_scalar(members23[:, d % 2, 2 * (t - 2) + d // 2, :], t, pos_t[d][:, first])
         for d in range(4):
             for t in (2, 3):
                 gather_scalar(late[:, d, t - 2, :], t, pos_t[d][:, second])
@@ -178,7 +168,7 @@ def tile_picked_sagecat_maxrelu_p_kernel(tc, x_words, x_scales, w1, w2, w3, offs
             gpsimd_copy(g_bf[n][:], g[:, :, n * HALF : (n + 1) * HALF].rearrange("p t v -> p v t"))
 
         z = keep.tile([P, PACK, V], BF16, name="z", align_bytes=64)
-        larger(tops01[:, :, 1, :], members1[:, 0], members1[:, 1])
+        larger(tops01[:], members01[:, 0], members01[:, 1])
         w23_code = keep.tile([P, 2 * N], U32, name="w23_code", align_bytes=64)
         w23_scale = keep.tile([P, 2 * N], U8, name="w23_scale", align_bytes=64)
         quantise(w23_code[:], w23_scale[:], w23_bf[:].rearrange("p n c j -> p (n c j)"))

@@ -27,6 +27,7 @@ BANK = 512
 BANKS = 8
 SHARE = 80
 HALF = V // 2
+SPLIT = 64
 RUN = 4
 
 KB = 1024
@@ -154,8 +155,8 @@ def tile_picked_sagecat_maxrelu_p_kernel(tc, x_words, x_scales, w1, w2, w3, offs
             for d in range(4):
                 gather_vector(members01[:, d % 2, d // 2, t, :], t, pos_t[d][:])
         gather_vector(members23[:, 0, 0, :], 2, pos_t[0][:, first])
-        gather_vector(members23[:, 0, 2, 0:P], 3, pos_t[0][:, 0 : P // STRIPE])
-        gather_scalar(members23[:, 0, 2, P:HALF], 3, pos_t[0][:, P // STRIPE : HALF // STRIPE])
+        gather_vector(members23[:, 0, 2, 0:SPLIT], 3, pos_t[0][:, 0 : SPLIT // STRIPE])
+        gather_scalar(members23[:, 0, 2, SPLIT:HALF], 3, pos_t[0][:, SPLIT // STRIPE : HALF // STRIPE])
         for t in (2, 3):
             for d in range(1, 4):
                 gather_scalar(members23[:, d % 2, 2 * (t - 2) + d // 2, :], t, pos_t[d][:, first])

@@ -27,7 +27,7 @@ BANK = 512
 BANKS = 8
 SHARE = 80
 HALF = V // 2
-SPLIT = 64
+SPLIT = 320
 RUN = 4
 
 KB = 1024
@@ -142,8 +142,9 @@ def tile_picked_sagecat_maxrelu_p_kernel(tc, x_words, x_scales, w1, w2, w3, offs
         gpsimd_copy(w23_bf[:], w23_raw[:].rearrange("p n j c -> p n c j"))
 
         members01 = at("members01", [P, 2, 2, 2, V], BF16, AT_MEMBERS01)
-        members23 = keep.tile([P, 2, 4, HALF], BF16, name="members23", align_bytes=64)
-        late = keep.tile([P, 4, 2, HALF], BF16, name="late", align_bytes=64)
+        pair0 = keep.tile([P, 2, 2, V], BF16, name="pair0", tag="pair0", align_bytes=64)
+        pair1 = keep.tile([P, 2, 2, HALF], BF16, name="pair1", align_bytes=64)
+        late = keep.tile([P, 2, 2, HALF], BF16, name="late", align_bytes=64)
         tops01 = keep.tile([P, 2, 2, V], BF16, name="tops01", align_bytes=64)
         g = keep.tile([P, PACK, V], BF16, name="g", align_bytes=64)
         first = slice(0, HALF // STRIPE)
@@ -153,16 +154,19 @@ def tile_picked_sagecat_maxrelu_p_kernel(tc, x_words, x_scales, w1, w2, w3, offs
             gather_scalar(g[:, t, :], t, cen_t[:])
         for t in (0, 1):
             for d in range(4):
-                gather_vector(members01[:, d % 2, d // 2, t, :], t, pos_t[d][:])
-        gather_vector(members23[:, 0, 0, :], 2, pos_t[0][:, first])
-        gather_vector(members23[:, 0, 2, 0:SPLIT], 3, pos_t[0][:, 0 : SPLIT // STRIPE])
-        gather_scalar(members23[:, 0, 2, SPLIT:HALF], 3, pos_t[0][:, SPLIT // STRIPE : HALF // STRIPE])
+                end = SPLIT if (t, d) == (1, 3) else V
+                gather_vector(members01[:, d % 2, d // 2, t, 0:end], t, pos_t[d][:, 0 : end // STRIPE])
+        gather_vector(pair0[:, 0, 0, :], 2, pos_t[0][:])
+        gather_scalar(pair0[:, 0, 1, :], 3, pos_t[0][:])
+        for d, t in ((2, 2), (2, 3), (3, 2)):
+            gather_scalar(pair1[:, d - 2, t - 2, :], t, pos_t[d][:, first])
+        gather_scalar(members01[:, 1, 1, 1, SPLIT:V], 1, pos_t[3][:, SPLIT // STRIPE : V // STRIPE])
+        gather_scalar(pair1[:, 1, 1, :], 3, pos_t[3][:, first])
         for t in (2, 3):
-            for d in range(1, 4):
-                gather_scalar(members23[:, d % 2, 2 * (t - 2) + d // 2, :], t, pos_t[d][:, first])
-        for d in range(4):
+            gather_scalar(pair0[:, 1, t - 2, :], t, pos_t[1][:])
+        for d in (2, 3):
             for t in (2, 3):
-                gather_scalar(late[:, d, t - 2, :], t, pos_t[d][:, second])
+                gather_scalar(late[:, d - 2, t - 2, :], t, pos_t[d][:, second])
 
         g_bf = [keep.tile([P, HALF, PACK], BF16, name="g_bf%d" % n, align_bytes=64) for n in range(2)]
         for n in range(2):
@@ -170,25 +174,23 @@ def tile_picked_sagecat_maxrelu_p_kernel(tc, x_words, x_scales, w1, w2, w3, offs
 
         z = keep.tile([P, PACK, V], BF16, name="z", align_bytes=64)
         larger(tops01[:], members01[:, 0], members01[:, 1])
-        w23_code = keep.tile([P, 2 * N], U32, name="w23_code", align_bytes=64)
+        top1 = keep.tile([P, 2, HALF], BF16, name="top1", align_bytes=64)
+        larger(top1[:], pair1[:, 0], pair1[:, 1])
+        larger(z[:, 0:2, :], tops01[:, 0], tops01[:, 1])
+        w23_code = at("w23_code", [P, 2 * N], U32, AT_MEMBERS01)
         w23_scale = keep.tile([P, 2 * N], U8, name="w23_scale", align_bytes=64)
         quantise(w23_code[:], w23_scale[:], w23_bf[:].rearrange("p n c j -> p (n c j)"))
-        larger(z[:, 0:2, :], tops01[:, 0], tops01[:, 1])
 
-        g_code = keep.tile([P, V], U32, name="g_code", align_bytes=64)
         g_scale = keep.tile([P, V], U8, name="g_scale", align_bytes=64)
 
-        def quantise_g(n):
-            half = slice(n * HALF, (n + 1) * HALF)
-            quantise(g_code[:, half], g_scale[:, half], g_bf[n][:].rearrange("p v t -> p (v t)"))
-
-        tops23 = keep.tile([P, 4, HALF], BF16, name="tops23", align_bytes=64)
-        larger(tops23[:], members23[:, 0], members23[:, 1])
-        quantise_g(0)
-        larger(z[:, 2:4, 0:HALF], tops23[:, 0:4:2, :], tops23[:, 1:4:2, :])
+        top0 = keep.tile([P, 2, HALF], BF16, name="top0", align_bytes=64)
+        larger(top0[:], pair0[:, 0, :, 0:HALF], pair0[:, 1, :, 0:HALF])
+        of_two = keep.tile([P, 2, HALF], BF16, name="of_two", align_bytes=64)
+        larger(of_two[:], pair0[:, 0, :, HALF:V], pair0[:, 1, :, HALF:V])
+        larger(z[:, 2:4, 0:HALF], top0[:], top1[:])
 
         groups = ((0, HALF), (HALF, V - P), (V - P, V))
-        z_bf = [keep.tile([P, b - a, PACK], BF16, name="z_bf%d" % a, align_bytes=64) for a, b in groups]
+        z_bf = [keep.tile([P, b - a, PACK], BF16, name="z_bf%d" % a, tag="z_bf%d" % a, align_bytes=64) for a, b in groups]
 
         def product(acc, weights, codes, scales):
             cols = slice(weights * N, (weights + 1) * N)
@@ -199,9 +201,12 @@ def tile_picked_sagecat_maxrelu_p_kernel(tc, x_words, x_scales, w1, w2, w3, offs
 
         accs = [psum.tile([P, b - a], F32, name="o_acc%d" % a, tag="bank%d" % (n + 1)) for n, (a, b) in enumerate(groups)]
 
-        def open_group(n):
+        def open_group(n, tag):
             a, b = groups[n]
-            product(accs[n], 0, g_code[:, a:b], g_scale[:, a:b])
+            g_code = keep.tile([P, b - a], U32, name="g_code%d" % a, tag=tag, align_bytes=64)
+            values = g_bf[a // HALF][:, a % HALF : a % HALF + b - a, :]
+            quantise(g_code[:], g_scale[:, a:b], values.rearrange("p v t -> p (v t)"))
+            product(accs[n], 0, g_code[:], g_scale[:, a:b])
 
         def close(n):
             a, b = groups[n]
@@ -219,18 +224,15 @@ def tile_picked_sagecat_maxrelu_p_kernel(tc, x_words, x_scales, w1, w2, w3, offs
                 nc.scalar.activation(res[:], accs[n][:], RELU)
             nc.sync.dma_start(out[:, a:b], res[:])
 
-        open_group(0)
-        of_two = keep.tile([P, 2, HALF], BF16, name="of_two", align_bytes=64)
-        larger(of_two[:], late[:, 0], late[:, 1])
+        open_group(1, "g_code1")
+        open_group(0, "pair0")
         nc.vector.tensor_copy(*runs(z_bf[0][:], z[:, :, 0:HALF]))
         of_three = keep.tile([P, 2, HALF], BF16, name="of_three", align_bytes=64)
-        larger(of_three[:], of_two[:], late[:, 2])
+        larger(of_three[:], of_two[:], late[:, 0])
         close(0)
         for a, b in groups[1:]:
-            larger(z[:, 2:4, a:b], of_three[:, :, a - HALF : b - HALF], late[:, 3, :, a - HALF : b - HALF])
-        quantise_g(1)
-        open_group(1)
-        open_group(2)
+            larger(z[:, 2:4, a:b], of_three[:, :, a - HALF : b - HALF], late[:, 1, :, a - HALF : b - HALF])
+        open_group(2, "z_bf0")
         nc.scalar.copy(*runs(z_bf[1][:], z[:, :, HALF : V - P]))
         nc.vector.tensor_copy(*runs(z_bf[2][:], z[:, :, V - P : V]))
         close(1)

from contextlib import ExitStack

import concourse.mybir as mybir

K, T, S, V, H, N = 512, 4096, 1024, 512, 512, 128
FLOPS = 2 * K * H * S + 2 * 2 * H * N * V

F32 = mybir.dt.float32
BF16 = mybir.dt.bfloat16
I32 = mybir.dt.int32
U32 = mybir.dt.uint32
U16 = mybir.dt.uint16
U8 = mybir.dt.uint8
FP8X4 = mybir.dt.float8_e4m3fn_x4
FP4X4 = mybir.dt.float4_e2m1fn_x4
COPY = mybir.ActivationFunctionType.Copy
RELU = mybir.ActivationFunctionType.Relu
MAX = mybir.AluOpType.max
ADD = mybir.AluOpType.add
MULT = mybir.AluOpType.mult

P = 128
PACK = 4
STRIPE = 16
BLOCKS = K // 32
BANK = 512
BANKS = 8
SHARE = 80
HALF = V // 2
SPLIT = 320
RUN = 4

KB = 1024
AT_MEMBERS01 = 0


def tile_picked_sagecat_maxrelu_p_kernel(tc, x_words, x_scales, w1, w2, w3, offs, cen, pos1, pos2, pos3, pos4, out):
    nc = tc.nc
    with ExitStack() as ctx:
        lists = ctx.enter_context(tc.tile_pool(name="lists", bufs=1))
        keep = ctx.enter_context(tc.tile_pool(name="keep", bufs=1))
        reuse = ctx.enter_context(tc.tile_pool(name="reuse", bufs=1))
        psum = ctx.enter_context(tc.psum_pool(name="psum", bufs=1))

        def load_list(name, source, entries):
            tile = lists.tile([P, entries // STRIPE], U16, name=name)
            nc.sync.dma_start(tile[:], source)
            return tile

        def quantise(codes, scales, values):
            nc.vector.quantize_mx(out=codes.bitcast(FP8X4), scales=scales, in_=values)

        scale_rows = slice(P - BLOCKS, P)
        s_tab = keep.tile([P, T], U8, name="s_tab", align_bytes=64)
        nc.sync.dma_start(s_tab[scale_rows, :].bitcast(I32), x_scales[0].bitcast(I32))
        nc.vector.memset(s_tab[0 : P - BLOCKS, :].bitcast(I32), 0)

        offs_t = load_list("offs_t", offs, S)

        x_tab = keep.tile([P, T], U16, name="x_tab", align_bytes=64)
        nc.sync.dma_start(x_tab[:].bitcast(I32), x_words[0].bitcast(I32))

        pos_t = [load_list("pos_t0", pos1, V), load_list("pos_t1", pos2, V)]

        w1_rows = w1.rearrange("(p j) c -> p (j c)", j=PACK)
        w1_raw = keep.tile([P, PACK * H], F32, name="w1_raw", tag="raw_weights")
        for j in (0, 2):
            nc.sync.dma_start(w1_raw[:, j * H : (j + 2) * H], w1_rows[:, j * H : (j + 2) * H])

        pos_t.append(load_list("pos_t2", pos3, V))
        pos_t.append(load_list("pos_t3", pos4, V))
        cen_t = load_list("cen_t", cen, V)

        s_picked = keep.tile([P, S], U8, name="s_picked", align_bytes=64)
        nc.vector.tensor_copy(s_picked[:], s_tab[:].indirect(offs_t[:]))
        x_scale = keep.tile([P, S], U8, name="x_scale", align_bytes=64)
        nc.vector.memset(x_scale[:].bitcast(I32), 0)
        for r in range(4):
            first_row = P - BLOCKS + 4 * r
            nc.sync.dma_start(x_scale[32 * r : 32 * r + 4, :].bitcast(I32), s_picked[first_row : first_row + 4, :].bitcast(I32))
        x_code = keep.tile([P, S], U16, name="x_code", align_bytes=64)
        nc.vector.tensor_copy(x_code[:], x_tab[:].indirect(offs_t[:]))

        w1_code = keep.tile([P, H], U32, name="w1_code", align_bytes=64)
        w1_scale = keep.tile([P, H], U8, name="w1_scale", align_bytes=64)
        w1_dealt = w1_raw[:].rearrange("p (j m t) -> p t m j", j=PACK, t=PACK)
        w1_bf0 = keep.tile([P, P, PACK], BF16, name="w1_bf0", align_bytes=64)
        nc.scalar.copy(out=w1_bf0[:, :, 0:2], in_=w1_dealt[:, 0, :, 0:2])
        w1_bf1 = keep.tile([P, P, PACK], BF16, name="w1_bf1", align_bytes=64)
        nc.scalar.copy(out=w1_bf1[:, :, 0:2], in_=w1_dealt[:, 1, :, 0:2])
        nc.scalar.copy(out=w1_bf0[:, 0 : P // 2, 2:4], in_=w1_dealt[:, 0, 0 : P // 2, 2:4])
        nc.vector.tensor_copy(out=w1_bf0[:, P // 2 : P, 2:4], in_=w1_dealt[:, 0, P // 2 : P, 2:4])
        w1_bf23 = keep.tile([P, 2, P, PACK], BF16, name="w1_bf23", align_bytes=64)
        nc.vector.tensor_copy(out=w1_bf23[:, :, SHARE:P, :].rearrange("p t m j -> p m j t"), in_=w1_dealt[:, 2:4, SHARE:P, :].rearrange("p t m j -> p m j t"))
        quantise(w1_code[:, 0:P], w1_scale[:, 0:P], w1_bf0[:].rearrange("p m j -> p (m j)"))
        nc.scalar.copy(out=w1_bf1[:, :, 2:4], in_=w1_dealt[:, 1, :, 2:4])
        nc.scalar.copy(out=w1_bf23[:, :, 0:SHARE, :].rearrange("p t m j -> p m j t"), in_=w1_dealt[:, 2:4, 0:SHARE, :].rearrange("p t m j -> p m j t"))
        quantise(w1_code[:, P : 2 * P], w1_scale[:, P : 2 * P], w1_bf1[:].rearrange("p m j -> p (m j)"))
        quantise(w1_code[:, 2 * P : H], w1_scale[:, 2 * P : H], w1_bf23[:].rearrange("p t m j -> p (t m j)"))

        h = []
        bank = 0
        for t in range(PACK):
            plane = keep.tile([P, S], F32, name="h%d" % t, align_bytes=64)
            pieces = ((0, BANK), (BANK, S - BANK // 2), (S - BANK // 2, S)) if t == 0 else ((0, BANK), (BANK, S))
            for a, b in pieces:
                acc = psum.tile([P, b - a], F32, name="h_acc%d_%d" % (t, a), tag="bank%d" % (bank % BANKS))
                bank = bank + 1
                nc.tensor.matmul_mx(
                    out=acc[:], lhsT=w1_code[:, t * P : (t + 1) * P].bitcast(FP8X4), lhsT_scale=w1_scale[:, t * P : (t + 1) * P],
                    rhs=x_code[:, a:b].bitcast(FP4X4), rhs_scale=x_scale[:, a:b], start=True, stop=True,
                )
                if t == 0 and a == BANK:
                    nc.vector.tensor_scalar_max(plane[:, a:b], acc[:], 0.0)
                else:
                    nc.scalar.activation(plane[:, a:b], acc[:], RELU)
            h.append(plane)

        w23_raw = keep.tile([P, 2, PACK, N], F32, name="w23_raw", tag="raw_weights")
        for n, w in enumerate((w2, w3)):
            nc.sync.dma_start(w23_raw[:, n, :, :], w.rearrange("(p j) c -> p j c", j=PACK))

        def at(name, shape, dtype, offset):
            return reuse.tile(shape, dtype, name=name, offset=offset, align_bytes=64)

        def gather_vector(picked, plane, entries):
            nc.vector.tensor_copy(picked, h[plane][:].indirect(entries))

        def gather_scalar(picked, plane, entries):
            nc.scalar.activation(picked, h[plane][:].indirect(entries), COPY)

        def gpsimd_copy(target, source):
            nc.gpsimd.tensor_scalar(target, source, 1.0, 0.0, MULT, ADD)

        def runs(grouped, planes):
            return grouped.rearrange("p (c i) t -> p c t i", i=RUN), planes.rearrange("p t (c i) -> p c t i", i=RUN)

        def larger(result, a, b):
            nc.vector.tensor_tensor(result, a, b, MAX)

        w23_bf = keep.tile([P, 2, N, PACK], BF16, name="w23_bf", align_bytes=64)
        gpsimd_copy(w23_bf[:], w23_raw[:].rearrange("p n j c -> p n c j"))

        members01 = at("members01", [P, 2, 2, 2, V], BF16, AT_MEMBERS01)
        pair0 = keep.tile([P, 2, 2, V], BF16, name="pair0", tag="pair0", align_bytes=64)
        pair1 = keep.tile([P, 2, 2, HALF], BF16, name="pair1", align_bytes=64)
        late = keep.tile([P, 2, 2, HALF], BF16, name="late", align_bytes=64)
        tops01 = keep.tile([P, 2, 2, V], BF16, name="tops01", align_bytes=64)
        g = keep.tile([P, PACK, V], BF16, name="g", align_bytes=64)
        first = slice(0, HALF // STRIPE)
        second = slice(HALF // STRIPE, V // STRIPE)
        gather_vector(g[:, 0, :], 0, cen_t[:])
        for t in range(1, PACK):
            gather_scalar(g[:, t, :], t, cen_t[:])
        for t in (0, 1):
            for d in range(4):
                end = SPLIT if (t, d) == (1, 3) else V
                gather_vector(members01[:, d % 2, d // 2, t, 0:end], t, pos_t[d][:, 0 : end // STRIPE])
        gather_vector(pair0[:, 0, 0, :], 2, pos_t[0][:])
        gather_scalar(pair0[:, 0, 1, :], 3, pos_t[0][:])
        for d, t in ((2, 2), (2, 3), (3, 2)):
            gather_scalar(pair1[:, d - 2, t - 2, :], t, pos_t[d][:, first])
        gather_scalar(members01[:, 1, 1, 1, SPLIT:V], 1, pos_t[3][:, SPLIT // STRIPE : V // STRIPE])
        gather_scalar(pair1[:, 1, 1, :], 3, pos_t[3][:, first])
        for t in (2, 3):
            gather_scalar(pair0[:, 1, t - 2, :], t, pos_t[1][:])
        for d in (2, 3):
            for t in (2, 3):
                gather_scalar(late[:, d - 2, t - 2, :], t, pos_t[d][:, second])

        g_bf = [keep.tile([P, HALF, PACK], BF16, name="g_bf%d" % n, align_bytes=64) for n in range(2)]
        for n in range(2):
            gpsimd_copy(g_bf[n][:], g[:, :, n * HALF : (n + 1) * HALF].rearrange("p t v -> p v t"))

        z = keep.tile([P, PACK, V], BF16, name="z", align_bytes=64)
        larger(tops01[:], members01[:, 0], members01[:, 1])
        top1 = keep.tile([P, 2, HALF], BF16, name="top1", align_bytes=64)
        larger(top1[:], pair1[:, 0], pair1[:, 1])
        larger(z[:, 0:2, :], tops01[:, 0], tops01[:, 1])
        w23_code = at("w23_code", [P, 2 * N], U32, AT_MEMBERS01)
        w23_scale = keep.tile([P, 2 * N], U8, name="w23_scale", align_bytes=64)
        quantise(w23_code[:], w23_scale[:], w23_bf[:].rearrange("p n c j -> p (n c j)"))

        g_scale = keep.tile([P, V], U8, name="g_scale", align_bytes=64)

        top0 = keep.tile([P, 2, HALF], BF16, name="top0", align_bytes=64)
        larger(top0[:], pair0[:, 0, :, 0:HALF], pair0[:, 1, :, 0:HALF])
        of_two = keep.tile([P, 2, HALF], BF16, name="of_two", align_bytes=64)
        larger(of_two[:], pair0[:, 0, :, HALF:V], pair0[:, 1, :, HALF:V])
        larger(z[:, 2:4, 0:HALF], top0[:], top1[:])

        groups = ((0, HALF), (HALF, V - P), (V - P, V))
        z_bf = [keep.tile([P, b - a, PACK], BF16, name="z_bf%d" % a, tag="z_bf%d" % a, align_bytes=64) for a, b in groups]

        def product(acc, weights, codes, scales):
            cols = slice(weights * N, (weights + 1) * N)
            nc.tensor.matmul_mx(
                out=acc[:], lhsT=w23_code[:, cols].bitcast(FP8X4), lhsT_scale=w23_scale[:, cols],
                rhs=codes.bitcast(FP8X4), rhs_scale=scales, start=weights == 0, stop=weights == 1,
            )

        accs = [psum.tile([P, b - a], F32, name="o_acc%d" % a, tag="bank%d" % (n + 1)) for n, (a, b) in enumerate(groups)]

        def open_group(n, tag):
            a, b = groups[n]
            g_code = keep.tile([P, b - a], U32, name="g_code%d" % a, tag=tag, align_bytes=64)
            values = g_bf[a // HALF][:, a % HALF : a % HALF + b - a, :]
            quantise(g_code[:], g_scale[:, a:b], values.rearrange("p v t -> p (v t)"))
            product(accs[n], 0, g_code[:], g_scale[:, a:b])

        def close(n):
            a, b = groups[n]
            z_code = keep.tile([P, b - a], U32, name="z_code%d" % a, align_bytes=64)
            z_scale = keep.tile([P, b - a], U8, name="z_scale%d" % a, align_bytes=64)
            quantise(z_code[:], z_scale[:], z_bf[n][:].rearrange("p v t -> p (v t)"))
            product(accs[n], 1, z_code[:], z_scale[:])

        def leave(n):
            a, b = groups[n]
            res = keep.tile([P, b - a], F32, name="res%d" % a)
            if b == V:
                nc.vector.tensor_scalar_max(res[:], accs[n][:], 0.0)
            else:
                nc.scalar.activation(res[:], accs[n][:], RELU)
            nc.sync.dma_start(out[:, a:b], res[:])

        open_group(1, "g_code1")
        open_group(0, "pair0")
        nc.vector.tensor_copy(*runs(z_bf[0][:], z[:, :, 0:HALF]))
        of_three = keep.tile([P, 2, HALF], BF16, name="of_three", align_bytes=64)
        larger(of_three[:], of_two[:], late[:, 0])
        close(0)
        for a, b in groups[1:]:
            larger(z[:, 2:4, a:b], of_three[:, :, a - HALF : b - HALF], late[:, 1, :, a - HALF : b - HALF])
        open_group(2, "z_bf0")
        nc.scalar.copy(*runs(z_bf[1][:], z[:, :, HALF : V - P]))
        nc.vector.tensor_copy(*runs(z_bf[2][:], z[:, :, V - P : V]))
        close(1)
        close(2)
        for n in range(3):
            leave(n)
